import numpy as np, ml_dtypes
CORES = [1,5,17,21,33,37,49,53]
N = 8
BF = ml_dtypes.bfloat16
def gentries(a):
    return np.ascontiguousarray(a.reshape(8, 16, -1).transpose(0, 2, 1)).reshape(8, -1)
def gtable(e):
    e = np.asarray(e); return np.ascontiguousarray(e.reshape(8, -1, 16).transpose(0, 2, 1)).reshape(128, -1).astype(np.int32)
V, P, XC, B, RO = 128, 256, 8192, 64, 3
E = 16 * V
def place_record(n, a, p, t):
    return ((n * (2 * a + 1) >> 4) + n + 37 * p + 77 * t) & (XC - 1)
def seat(rng, ln, key=None, mix=True, pair=False):
    oc = np.full((N, 8, E), P, np.int64); qs = np.full((N, 8, 16 * P), E, np.int64)
    for r in range(N):
        for g in range(8):
            at = np.flatnonzero((np.arange(16) < ln[r, g][:, None]).reshape(-1))
            if pair and g & 1: at = at[np.argsort(2 * np.minimum(at, at ^ (16 * B)) + (at > (at ^ (16 * B))))]
            s = rng.permutation(16 * P) if key is None else np.argsort(key[r, g].reshape(-1))
            s = s[:len(at)]
            if mix: s = rng.permutation(s)
            oc[r, g, at] = s >> 4; qs[r, g, s] = at
    return oc, qs
def put(oc, qs, r, g, s, n):
    b = int(np.flatnonzero(qs[r, g] == n)[0]); m = int(qs[r, g, s])
    qs[r, g, s] = n; qs[r, g, b] = m; oc[r, g, m] = b >> 4; oc[r, g, n] = s >> 4
def aim(w, y, u):
    i = np.arange(1, 16)[:, None]
    w[0] = (u - np.sum(16 * i * w[1:] + np.minimum(w[1:], y[1:, None]), axis=0)) & (V - 1)
def pack(x, want, oc, qs, th):
    return {"x": np.ascontiguousarray(x.reshape(N, 128, XC)).astype(np.float32).astype(BF), "want": np.stack([want.reshape(128, P)] * N).astype(np.float32).astype(BF),
            "oc": np.stack([gtable(a) for a in oc]), "qs": np.stack([gtable(a) for a in qs]), "th": np.repeat(th, 16, axis=1).reshape(N, 128, 1).astype(np.int32)}
def goods(rng):
    return rng.integers(0, 256, (N, 8, 16, XC)), rng.integers(0, 256, (8, 16, P))
def setup_inputs(rng):
    x, want = goods(rng); oc, qs = seat(rng, rng.integers(8, 17, (N, 8, V)))
    return pack(x, want, oc, qs, rng.integers(450, 901, (N, 8)))
def setup_inputs_alike(rng):
    x, want = goods(rng); ln = rng.choice(np.array([16, 16, 8, 3, 12]), (N, 8, V))
    ln[:, 2] = 16; ln[:, 4] = rng.integers(12, 16, (N, V)); ln[:, 6] = rng.integers(12, 16, (N, V)); ln[:, 6, 1] = 16; ln[N - 1, 6, V - 1] = 15
    key = rng.random((N, 8, P, 1)) + 0.0001 * rng.random((N, 8, P, 16))
    oc, qs = seat(rng, ln, key, False, True)
    want[3] = want[3][:, :1]; x[N - 1, 5] = x[N - 1, 5] >> 1
    key = rng.random((N, 8, P, 16)); one = np.arange(16) == rng.integers(0, 16, (N, P, 1))
    key[:, 4] = np.where(one, -1, np.where(np.roll(one, 1, axis=2), 9, key[:, 4]))
    key[:, 6, 1:N + 1] = 9; key[:, 6, P - 1] = 9; key[N - 1, 6, P - 1, :15] = -1
    for r in range(N): key[r, 6, r + 1, r] = -1
    oc2, qs2 = seat(rng, ln, key)
    oc[:, 2:7:2] = oc2[:, 2:7:2]; qs[:, 2:7:2] = qs2[:, 2:7:2]
    n = np.arange(E); m = n ^ (16 * B)
    for r in range(N):
        a = np.where((n & 15) == 0, n >> 4, np.roll(oc[r, 2], 1)); c = place_record(m, a[m], oc[r, 2], 0)
        y = x[r, 2] >> 1; y[:, c] = y[:, c] | 128; x[r, 2] = y
        put(oc, qs, r, 6, 16 * (r + 1) + r, 128)
    for k in range(15): put(oc, qs, N - 1, 6, 16 * (P - 1) + k, E - 16 + k)
    y = rng.integers(0, 256, 16); y[0] = 255; x[:, 4] = y[:, None]; want[4] = want[4][:, :1]; aim(want[4], y, 0)
    u = 2 + rng.integers(0, V - 3, P); u[1:N + 1] = 1; u[P - 1] = V - 1
    x[:, 6] = 255; aim(want[6], np.full(16, 255), u)
    th = rng.integers(600, 1500, (N, 8)); th[:, 2] = 4080
    return pack(x, want, oc, qs, th)
def setup_inputs_ties(rng):
    x, want = goods(rng); x = 85 * (x >> 6); want = 85 * (want >> 6)
    oc, qs = seat(rng, rng.integers(8, 17, (N, 8, V)))
    for a in (x, oc, qs): a[:, ::2] = a[:1, ::2]
    x[0, 2] = np.minimum(x[0, 2], 170); x[0, 6] = np.minimum(x[0, 6], 170)
    return pack(x, want, oc, qs, 85 * rng.integers(4, 11, (N, 8)) - rng.integers(0, 2, (N, 8)))
def setup_inputs_corners(rng):
    x, want = goods(rng); ln = rng.choice(np.array([0, 1, 15, 16]), (N, 8, V))
    kind = rng.random((N, 8, 1, XC)); x = np.where(kind < 0.4, 255, np.where(kind < 0.5, 0, x))
    cls = rng.integers(0, 4, (8, 1, P)); kind = rng.random((8, 1, P)); many = np.full((8, 16, P), 255); many[:, 1:2] = 255 - cls
    want = np.where(kind < 0.6, many, np.where(kind < 0.7, 0, want))
    want[7, :, ::16] = 255; want[7, 7, ::16] = 254
    for g in range(8):
        x[:g % N, g, 0] = np.minimum(x[:g % N, g, 0], 254)
        for c in range(4): ln[:, g, (16 * 120 * 255 + 4080 - 17 * c) & (V - 1)] = (15, 0, 16, 1)[(g + c) & 3]
    ln[:, 7, V - 1] = 15; ln[:, 0, V - 1] = 16; ln[:, 7, 0] = 16
    c = rng.integers(0, 5, (N, 8, P, 1)); c[:, :, 4::9] = 3
    one = np.arange(16) == rng.integers(0, 16, (N, 8, P, 1))
    key = rng.random((N, 8, P, 1)) + 0.0001 * rng.random((N, 8, P, 16))
    key = key + np.where(c == 0, 0, np.where(c == 1, np.where(one, 3, 0), np.where(c == 2, np.where(one, -3, 3), np.where(c == 3, 6, 1))))
    key[N - 1, 7, 0] = np.where(np.arange(16) < 15, -1, 9)
    oc, qs = seat(rng, ln, key)
    th = rng.choice(np.array([0, 1, 1000, 2000, 4080]), (N, 8)); th[:, ::2] = 4080; th[:, 5] = 4079; th[:, 7] = 4080
    return pack(x, want, oc, qs, th)
def setup_inputs_ends(rng):
    v = np.arange(V); low = np.minimum(v, v ^ B)
    ln = np.where((rng.random((N, 8, V)) < 0.35)[..., low], 16, 0)
    for q in (0, V - 1): ln[..., q] = 16; ln[..., q ^ B] = 16
    who = rng.random((N, 8, P, 1)); who[:, :, 0] = -1; who[:, :, P - 1] = -1
    oc, qs = seat(rng, ln, who + 0.0001 * rng.random((N, 8, P, 16)))
    kind = rng.random((8, 1, P)); want = np.where(kind < 0.25, 255, np.where(kind < 0.4, 0, 255 * rng.integers(0, 2, (8, 16, P))))
    want[:, :, 0] = 255; want[:, :, P - 1] = 255; want[:, :, P // 2] = 0; want[:, :, P - 2] = 0
    kind = rng.random((N, 8, 1, XC)); x = np.where(kind < 0.3, 255, np.where(kind < 0.45, 0, 255 * rng.integers(0, 2, (N, 8, 16, XC))))
    x[..., 0] = 255; x[..., XC - 1] = 255
    for r in range(N):
        for g in range(8):
            put(oc, qs, r, g, 16 * P - 1, E - 1); put(oc, qs, r, g, 0, 0)
            x[r, g, :, int(place_record(E - 1, int(oc[r, g, E - 2]), P - 1, 0))] = 255
    th = np.where(rng.random((N, 8)) < 0.3, 0, 4080); th[:, 0] = 4080; th[:, 1] = 0; th[:, 7] = 4080
    return pack(x, want, oc, qs, th)
def setup_inputs_spread(rng):
    x = np.minimum((np.exp2(8 * rng.random((N, 8, 1, XC))) * rng.random((N, 8, 16, XC))).astype(np.int64), 255)
    want = np.minimum((np.exp2(2 + 6 * rng.random((8, 1, P))) * rng.random((8, 16, P))).astype(np.int64), 255)
    ln = np.minimum((17 * rng.random((N, 8, V)) ** rng.choice(np.array([0.3, 0.6, 1.0, 2.0]), (N, 8, 1))).astype(np.int64), 16)
    oc, qs = seat(rng, ln)
    return pack(x, want, oc, qs, np.minimum(np.exp2(12 * rng.random((N, 8))).astype(np.int64), 4080))
def check_inputs(d):
    bad = []
    for k, hi in (("x", 255), ("want", 255), ("oc", P), ("qs", E), ("th", 4080)):
        a = np.asarray(d[k]).astype(np.float64)
        if not np.all((a >= 0) & (a <= hi)): bad.append("range of " + k)
        elif not np.all(a == np.floor(a)): bad.append("whole numbers of " + k)
    w = np.asarray(d["want"]).astype(np.float32)
    if not np.all(w == w[:1]): bad.append("want alike on all ranks")
    t = np.asarray(d["th"]).reshape(N, 8, 16)
    if not np.all(t == t[:, :, :1]): bad.append("th alike in the rows of a group")
    if "range of oc" in bad or "range of qs" in bad: return bad
    o = np.stack([gentries(a) for a in d["oc"]]).astype(np.int64); q = np.stack([gentries(a) for a in d["qs"]]).astype(np.int64)
    b = (o < P).reshape(N, 8, V, 16)
    if np.any(b[..., 1:] & ~b[..., :-1]): bad.append("queues of oc without gaps")
    ok = True; person = np.arange(16 * P) >> 4
    for r in range(N):
        for g in range(8):
            n = np.bincount(q[r, g], minlength=E + 1)[:E]; back = np.full(E + 1, P, np.int64); back[q[r, g]] = person
            ok = ok and np.array_equal(n, (o[r, g] < P).astype(n.dtype)) and np.array_equal(back[:E], o[r, g])
    if not ok: bad.append("every occupied place of oc in just one slot of qs, of its person")
    return bad
def reference(x, want, oc, qs, th):
    xs = x.astype(np.float32).astype(np.int32).reshape(N, 8, 16, XC); ws = want.astype(np.float32).astype(np.int32).reshape(N, 8, 16, P)
    wp = np.concatenate([ws, np.zeros((N, 8, 16, 1), np.int32)], axis=3); wsum = np.add.reduce(16 * np.arange(16)[:, None] * ws.astype(np.int64), axis=2)
    o = np.stack([gentries(a) for a in oc]).astype(np.int64)
    q = np.stack([gentries(a) for a in qs]).astype(np.int64)
    lim = th.astype(np.int64).reshape(N, 8, 16)[:, :, :1]
    n = np.arange(E); mate = n ^ (16 * B); v = n >> 4; head = (n & 15) == 0; none = np.full((N, 8, 1), E, np.int64)
    for t in range(RO):
        occ = o < P; ahead = np.where(head, v, np.roll(o, 1, axis=2))
        w = np.take_along_axis(wp, o[:, :, None, :], 3)
        own = np.add.reduce(np.minimum(np.take_along_axis(xs, place_record(n, ahead, o, t)[:, :, None, :], 3), w), axis=2).astype(np.int64)
        other = np.add.reduce(np.minimum(np.take_along_axis(xs, place_record(mate, ahead[..., mate], o, t)[:, :, None, :], 3), w), axis=2).astype(np.int64)
        swap = occ & occ[..., mate] & (other + other[..., mate] > own + own[..., mate])
        o2 = np.where(swap, o[..., mate], o); c = np.where(swap, other[..., mate], own)
        qd = np.take_along_axis(np.concatenate([np.where(swap, mate, n), none], axis=2), q, 2)
        best = np.max(np.take_along_axis(np.concatenate([c, np.full((N, 8, 1), -1, np.int64)], axis=2), qd, 2).reshape(N, 8, P, 16), axis=3)
        top = np.max(best, axis=0); holder = np.argmax(best, axis=0)
        tp = np.concatenate([np.broadcast_to(top, (N, 8, P)), np.zeros((N, 8, 1), np.int64)], axis=2)
        go = (c < np.take_along_axis(tp, o2, 2) - lim) | (head & ((v & 7) == t))
        stay = (occ & ~go).astype(np.int64).reshape(N, 8, V, 16)
        to = np.where(stay == 1, 16 * np.arange(V)[:, None] + np.add.accumulate(stay, axis=3) - stay, E).reshape(N, 8, E)
        o = np.full((N, 8, E + 1), P, np.int64); np.put_along_axis(o, to, o2, 2); o = np.ascontiguousarray(o[..., :E])
        q = np.take_along_axis(np.concatenate([to, none], axis=2), qd, 2)
        ln = np.add.reduce(stay, axis=3); empty = q.reshape(N, 8, P, 16) == E; u = (wsum + top) & (V - 1)
        for r in range(N):
            for g in range(8):
                p = np.flatnonzero(np.any(empty[r, g], axis=1) & (top[g] >= 0) & (holder[g] == r)); p = p[ln[r, g, u[r, g, p]] < 16]
                k, i = np.unique(u[r, g, p], return_index=True); p = p[i]; at = 16 * k + ln[r, g, k]
                o[r, g, at] = p; q[r, g, 16 * p + np.argmax(empty[r, g, p], axis=1)] = at
    return {"yoc": np.stack([gtable(a) for a in o]).astype(np.float32), "yq": np.stack([gtable(a) for a in q]).astype(np.float32)}

@@ -1,0 +1,706 @@
+import math
+from concourse.bass import DstId, RemoteDMATransfer
+from concourse.mybir import AluOpType as OP, ActivationFunctionType as AF
+
+F32, BF, H, I32, U16 = "float32", "bfloat16", "float16", "int32", "uint16"
+
+
+def _sb(dtype, **names):
+    return {n: ("sbuf", [128, w], dtype) for n, w in names.items()}
+
+
+SCRATCH = {}
+SCRATCH.update(_sb(BF, xs=8192, wn=272, gmb=128, lkb=2048, apb=128, bkb=2048, tri=128, i8=128, in8=128, qlm=128, lenm=128,
+                   trit=128, cneg=128, c16=128, k2=128, c77=256, trf=128, ihb=128, sm=64, ctb=256, on=128, rho=256,
+                   dm=256, ivb=128, hm=384, wg=2048, mn=4096, zd=4096, zf=4096, ze=2048, hfs=256,
+                   oh=2048, ub=256))
+SCRATCH.update(_sb(I32, oci=128, qsi=256, thi=1, cint=8, qi=256, qa=256, hz=256, hm13=256, zu=32))
+SCRATCH.update(_sb(U16, ol=128, ql=256, hu=256, ol2=128, clist=16, ul=16))
+SCRATCH.update(_sb(H, ih=128, sh=128, stmp=128, hcb=256, i37=128, pre=128, emp=128, sc=128, trie=128, cst=384, csl=384,
+                   k2l=128, o=128, cp=128, c2=128, o2=128, kb=256, st=128, e16=128, fr=2048, o3t=128, tof=128, em=256,
+                   qt=256))
+SCRATCH.update(_sb(F32, col=32, cI=128, cg=128, ck=128, c8=128, ipm=256, rs=256, rb=256, rb4=32, ch=32, cht=32, cno=32, R=16, n8=128,
+                   sx=320, pc=48, of32=128, y1=128, sd=128, dw=2064, fw=2064, tsb=256, tm=256, land0=128, land1=128,
+                   land2=128, x2=256, ce=512, p16=160, kt=128, kp=16, wm=272, lna=160, apf=8, qp=128, corr=128, iseq=128,
+                   appl=128, qlw=128, l16=128, lv=128, tt=128, wmk=256, npl=256, fe=256, yo=128, yqs=256))
+PSUM = ("r0", "r1", "r2", "r3", "pa", "plo", "phi", "pq")
+SCRATCH.update({n: ("psum", [128, 512], F32) for n in PSUM})
+SEMAPHORES = ["cV", "cS", "cP", "cG", "d_oc", "d_qs", "d_wn", "d_th", "d_x", "d_yo", "d_yq", "arr0", "arr1", "arr2", "loc"]
+PART = {"pint": ("cint", 0, 1), "kint": ("cint", 1, 1), "gint": ("cint", 2, 1), "lint": ("cint", 3, 1), "hint": ("cint", 4, 1),
+        "dlo": ("sx", 0, 64), "dd": ("sx", 64, 64), "s": ("sx", 128, 64), "ml": ("sx", 192, 64), "dhi": ("sx", 256, 64),
+        "gc": ("sm", 0, 16), "ngc": ("sm", 16, 16), "wi": ("sm", 32, 16), "wts": ("sm", 48, 16), "gth": ("pc", 0, 16),
+        "thc": ("pc", 16, 16), "wsc": ("pc", 32, 16), "zi": ("zu", 0, 16), "ui": ("zu", 16, 16)}
+
+
+CYCLE, WAKE, TRIP, SLACK = 1.0, 120.0, 4700.0, 5.0
+PLAN = {}
+
+
+def plan(ops, trips):
+    n = len(ops)
+    pred = [dict() for _ in range(n)]
+    hist, bank = {}, {}
+    for i, op in enumerate(ops):
+        e = op[0]
+        regs = [(False, rg[0], rg[1], rg[2]) for rg in op[2]] + [(True, rg[0], rg[1], rg[2]) for rg in op[3]]
+        for wr, b, lo, hi in regs:
+            if b in PSUM:
+                for k, v in bank.get(b, {}).items():
+                    pred[i][v] = max(pred[i].get(v, 0), int(k != e))
+            else:
+                for a in hist.get(b, []):
+                    if a[1] < hi and lo < a[2] and (wr or a[0]):
+                        pred[i][a[3]] = 1
+        for wr, b, lo, hi in regs:
+            if b in PSUM:
+                bank.setdefault(b, {})[e] = i
+            else:
+                h = hist.setdefault(b, [])
+                if wr:
+                    h[:] = [a for a in h if not (lo <= a[1] and a[2] <= hi)]
+                h.append((wr, lo, hi, i))
+    for a, b in trips:
+        pred[b][a] = 2
+    succ = [[] for _ in range(n)]
+    for i in range(n):
+        for p, k in pred[i].items():
+            succ[p].append((i, k))
+    way = [0.0] * n
+    for i in range(n - 1, -1, -1):
+        way[i] = ops[i][6] + max([way[j] + (0, WAKE, TRIP)[k] for j, k in succ[i]] or [0.0])
+
+    def forward(urgent, back):
+        after = succ if not back else [list(p.items()) for p in pred]
+        before = [list(p.items()) for p in pred] if not back else succ
+        left = [len(p) for p in before]
+        ready = {e: [i for i in range(n) if ops[i][0] == e and not left[i]] for e in "VSPGY"}
+        free, newest, end, order = dict.fromkeys("VSPGY", 0.0), dict.fromkeys("VSPGY", -1), [0.0] * n, []
+
+        def begin(i):
+            e = ops[i][0]
+            t = free[e]
+            for p, k in before[i]:
+                if k == 2:
+                    t = max(t, end[p] + TRIP)
+                elif k == 1 and (end[p] > free[e] or newest[e] == p):
+                    t = max(t, end[p] + WAKE)
+            return t
+
+        while len(order) < n:
+            best = None
+            for e in "VSPGY":
+                if ready[e]:
+                    st = [(begin(i), i) for i in ready[e]]
+                    t0 = min(st)[0]
+                    t, i = max(((t, i) for t, i in st if t <= t0 + SLACK), key=lambda q: (urgent[q[1]], q[1] if back else -q[1]))
+                    if best is None or t < best[0]:
+                        best = (t, i, e)
+            t, i, e = best
+            ready[e].remove(i)
+            end[i] = t + ops[i][6]
+            free[e] = t + 70 if e == "Y" and not back else end[i]
+            newest[e] = i
+            order.append(i)
+            for j, k in after[i]:
+                left[j] -= 1
+                if not left[j]:
+                    ready[ops[j][0]].append(j)
+        return max(end), order, end
+
+    best, urgent = None, way
+    for i in range(4):
+        total, order, end = forward(urgent, False)
+        if best is None or total < best[0]:
+            best = (total, order)
+        urgent = forward(end, True)[2]
+    return best[1]
+
+
+def rank_program(g, core, T, topo):
+    rank = T.rank_of(core)
+    if rank is None:
+        return
+    eng = {"V": g.vector, "S": g.scalar, "P": g.tensor, "G": g, "Y": g.sync}
+    count = {"V": 0, "S": 0, "P": 0, "G": 0}
+    known = {e: {} for e in eng}
+    snap = {}
+    ops = []
+    trips = []
+    hist = {}
+    bank = {}
+
+    def wait(e, ev):
+        if known[e].get(ev[0], 0) >= ev[1]:
+            return
+        eng[e].wait_ge(T.sem[ev[0]], ev[1])
+        for k, v in list(snap[ev].items()) + [ev]:
+            if known[e].get(k, 0) < v:
+                known[e][k] = v
+
+    def run(e, fn, reads, writes, sem=None, inc=1, cost=100.0, pre=None):
+        ops.append((e, fn, reads, writes, sem, inc, cost, pre))
+
+    def emit(e, fn, reads, writes, sem, inc, cost, pre):
+        evs = []
+        for wr, regs in ((False, reads), (True, writes)):
+            for rg in regs:
+                b, lo, hi = rg[0], rg[1], rg[2]
+                if b in PSUM:
+                    evs += [v for k, v in bank.get(b, {}).items() if k != e]
+                else:
+                    evs += [a[3] for a in hist.get(b, []) if a[1] < hi and lo < a[2] and (wr or a[0])]
+        need = {}
+        for k, v in evs:
+            need[k] = max(need.get(k, 0), v)
+        for ev in sorted(need.items(), key=lambda q: -q[1]):
+            wait(e, ev)
+        if pre:
+            pre()
+        if not inc:
+            fn()
+            return
+        if sem is None:
+            sem = "c" + e
+            count[e] += 1
+            ev = (sem, count[e])
+        else:
+            ev = (sem, inc)
+        fn().then_inc(T.sem[sem], inc)
+        snap[ev] = dict(known[e])
+        for wr, regs in ((False, reads), (True, writes)):
+            for rg in regs:
+                b, lo, hi = rg[0], rg[1], rg[2]
+                if b in PSUM:
+                    bank.setdefault(b, {})[e] = ev
+                else:
+                    h = hist.setdefault(b, [])
+                    if wr:
+                        h[:] = [a for a in h if not (lo <= a[1] and a[2] <= hi)]
+                    else:
+                        h[:] = [a for a in h if not (not a[0] and a[3][0] == ev[0] and a[1] == lo and a[2] == hi)]
+                    h.append((wr, lo, hi, ev))
+
+    def c(b, lo=None, hi=None, step=1):
+        n, at, w = PART.get(b) or (b, 0, SCRATCH[b][1][1])
+        if lo is None:
+            lo, hi = 0, w
+        return (n, at + lo, at + hi, step)
+
+    def ap(x):
+        if x[0] == "ind":
+            return ap(x[1]).indirect(ap(x[2]))
+        return T[x[0]][:, x[1]:x[2]:x[3]] if x[3] != 1 else T[x[0]][:, x[1]:x[2]]
+
+    def ind(w, o):
+        return ("ind", w, o)
+
+    def rd(*xs):
+        out = []
+        for x in xs:
+            if isinstance(x, tuple):
+                out += [x[1], x[2]] if x[0] == "ind" else [x]
+        return out
+
+    def val(x):
+        return ap(x) if isinstance(x, tuple) else x
+
+    def wide(x):
+        return 16 * (x[2][2] - x[2][1]) if x[0] == "ind" else -(-(x[2] - x[1]) // x[3])
+
+    def took(out, *ins):
+        if any(x[0] == "ind" for x in ins):
+            return 50 + 1.56 * CYCLE * wide(out)
+        small = all(SCRATCH[x[0]][2] in (BF, H, U16) for x in (out,) + ins)
+        both = len(ins) == 2 and not any(x[0] in PSUM for x in ins)
+        return CYCLE * max(64, wide(out) * (2 if both else 0.5 if small and len(ins) == 1 else 1))
+
+    def ts(out, a, s1, s2, o0, o1=None):
+        if o1 is None:
+            run("V", lambda: g.vector.tensor_scalar(ap(out), ap(a), val(s1), None, o0), rd(a, s1), [out], cost=took(out, a))
+        else:
+            run("V", lambda: g.vector.tensor_scalar(ap(out), ap(a), val(s1), val(s2), o0, o1), rd(a, s1, s2), [out], cost=took(out, a))
+
+    def tt(out, a, b, op):
+        run("V", lambda: g.vector.tensor_tensor(ap(out), ap(a), ap(b), op), rd(a, b), [out], cost=took(out, a, b))
+
+    def cp(out, a):
+        run("V", lambda: g.vector.tensor_copy(ap(out), ap(a)), rd(a), [out], cost=took(out, a))
+
+    def scan(out, d0, d1, o0, o1):
+        run("V", lambda: g.vector.tensor_tensor_scan(ap(out), ap(d0), ap(d1), 0.0, o0, o1), rd(d0, d1), [out], cost=CYCLE * max(64, wide(out)))
+
+    def fill(out, v):
+        run("V", lambda: g.vector.memset(ap(out), v), [], [out], cost=took(out))
+
+    def act(out, a, func, bias=0.0, scale=1.0):
+        cost = 65 + 1.56 * CYCLE * wide(out) if a[0] == "ind" else CYCLE * max(64, wide(out))
+        run("S", lambda: g.scalar.activation(ap(out), ap(a), func, bias=val(bias), scale=val(scale)), rd(a, bias, scale), [out],
+            cost=cost + (1300 if func == AF.Exp else 0))
+
+    def mm(out, l, r, start, stop):
+        run("P", lambda: g.tensor.matmul(ap(out), ap(l), ap(r), start, stop), rd(l, r), [out],
+            cost=CYCLE * max(min(64, wide(l)), wide(r)) * (4 if SCRATCH[l[0]][2] == F32 else 1))
+
+    def iota(out, pattern, base, cm):
+        cost = 130 + 2 * CYCLE * wide(out)
+        if SCRATCH[out[0]][2] != I32:
+            run("G", lambda: g.iota(ap(out), pattern, base, cm, allow_small_or_imprecise_dtypes=True), [], [out], cost=cost)
+        else:
+            run("G", lambda: g.iota(ap(out), pattern, base, cm), [], [out], cost=cost)
+
+    def load(e, sem, b, hi, src):
+        run(e, lambda: eng[e].dma_start(T[b][:, 0:hi], src), [], [c(b, 0, hi)], sem=sem, inc=16, cost=9000.0 if b == "xs" else 2000.0)
+
+    def k_(b, k):
+        return c(b, 128 * k, 128 * k + 128)
+
+    PC, KC, GC, K8, BC, TH, THR, P64, W64, WX, PP, L3, LN, KX = [c("col", i, i + 1) for i in range(14)]
+    add, sub, mul, mx, mi, eq, ge, gt, lt = (OP.add, OP.subtract, OP.mult, OP.max, OP.min, OP.is_equal, OP.is_ge, OP.is_gt, OP.is_lt)
+
+    load("Y", "d_oc", "oci", 128, T.oc[:, :])
+    load("Y", "d_wn", "wn", 256, T.want[:, :])
+    load("Y", "d_x", "xs", 8192, T.x[:, :])
+    load("Y", "d_qs", "qsi", 256, T.qs[:, :])
+    load("Y", "d_th", "thi", 1, T.th[:, :])
+
+    iota(c("pint"), [[0, 1]], 0, 1)
+    iota(c("cI"), [[1, 128]], 0, 0)
+    iota(PC, [[0, 1]], 0, 1)
+    iota(c("cg"), [[1, 8], [0, 16]], 0, 0)
+    iota(c("ck"), [[0, 8], [1, 16]], 0, 0)
+    iota(c("c8"), [[0, 16], [1, 8]], 0, 0)
+    iota(c("ch"), [[0, 8], [64, 4]], 0, 0)
+    iota(c("ipm"), [[1, 256]], -256, 0)
+
+    fill(c("wn", 256, 272), 0.0)
+    fill(c("lkb"), 0.0)
+    fill(LN, math.exp(43.23))
+    fill(c("dw", 2048, 2064), 0.0)
+    fill(c("wm", 256, 272), 0.0)
+    ts(c("kint"), c("pint"), 15, None, OP.bitwise_and)
+    ts(c("gint"), c("pint"), 4, None, OP.arith_shift_right)
+    ts(c("lint"), c("pint"), 63, None, OP.bitwise_and)
+    ts(c("hint"), c("pint"), 6, None, OP.arith_shift_right)
+    cp(KC, c("kint"))
+    cp(GC, c("gint"))
+    cp(P64, c("lint"))
+    cp(W64, c("hint"))
+    ts(c("gmb"), c("cg"), GC, None, eq)
+    ts(c("ih"), c("cI"), PC, None, eq)
+    ts(c("R"), c("cI", 0, 16), KC, None, eq)
+    ts(K8, KC, 0.125, None, mul)
+    ts(c("stmp"), c("cI"), 1.0, PC, sub, eq)
+    ts(c("hcb", 0, 128), c("cI"), c("R", 0, 1), 8.5, mul, add)
+    ts(c("hcb", 128, 256), c("cI"), 0.0, -0.46875, mul, add)
+    tt(c("sh"), c("stmp"), c("gmb"), mul)
+    ts(c("i37"), c("ih"), 37.0, None, mul)
+    ts(c("n8"), c("cI"), 2.0, K8, mul, add)
+    cp(c("o"), c("oci"))
+    cp(c("ol"), c("oci"))
+    act(WX, P64, AF.Exp, 43.0, -1.0)
+    act(L3, LN, AF.Ln)
+    for k in range(16):
+        act(c("lkb", 128 * k + k, 128 * k + 128, 16), c("gmb", k, 128, 16), AF.Copy)
+    ts(c("pre"), c("cI"), 0.0, -2047.0, mul, add)
+
+    def h_consts(t):
+        mm(c("pa", 0, 256), c("ih"), c("hcb"), True, False)
+        if t:
+            mm(c("pa", 128, 256), c("ih"), c("c77", 128 * (t - 1), 128 * t), False, False)
+
+    def h_data():
+        mm(c("pa", 0, 128), c("sh"), c("o"), False, False)
+        mm(c("pa", 128, 256), c("i37"), c("o"), False, True)
+
+    def empties():
+        ts(c("emp"), c("o"), 256.0, -8192.0, ge, mul)
+
+    h_consts(0)
+    h_data()
+
+    def offsets():
+        tt(c("y1"), c("pa", 0, 128), c("n8"), mul)
+        for i in (0, 1):
+            q, a = 64 * i, 128 * i
+            tt(c("hz", a, a + 64), c("y1", q, q + 64), c("pa", 128 + q, 192 + q), add)
+            tt(c("hz", a + 64, a + 128), c("y1", 64 - q, 128 - q), c("pa", 128 + q, 192 + q), add)
+            ts(c("hm13", a, a + 128), c("hz", a, a + 128), 8191, None, OP.bitwise_and)
+            cp(c("hu", a, a + 128), c("hm13", a, a + 128))
+
+    def setup_b():
+        ts(c("qa"), c("qsi"), 15, None, OP.bitwise_and)
+        ts(c("hm13"), c("qsi"), 4, None, OP.arith_shift_right)
+        ts(c("qi"), c("qsi"), 2048.0, 1920.0, ge, mul)
+        ts(c("qa"), c("qa"), 128.0, None, mul)
+        tt(c("hm13"), c("hm13"), c("qi"), add)
+        tt(c("qi"), c("qa"), c("hm13"), add)
+        cp(c("ql"), c("qi"))
+        ts(BC, KC, -256.0, 2048.0, mul, add)
+        ts(KX, KC, 16.0, None, mul)
+        cp(TH, c("thi"))
+        cp(c("gc", 0, 8), c("gmb", 0, 128, 16))
+        ts(c("ngc", 0, 8), c("gc", 0, 8), -1.0, None, mul)
+        ts(c("ctb", 0, 128), c("cI"), 32.0, 32.0, ge, mul)
+        ts(c("ctb", 128, 256), c("cI"), 64.0, 32.0, ge, mul)
+        fill(c("on"), 1.0)
+        fill(c("rho"), (7 - rank) / 2048.0)
+        for b in (0, 1):
+            ts(c("rs", 128 * b, 128 * b + 128), c("ck"), 0.0, None, gt)
+            ts(c("rb", 128 * b, 128 * b + 128), c("ck"), 0.0, 1e5, eq, mul)
+        ts(c("rb4"), c("ch"), 0.0, 1e5, eq, mul)
+        ts(c("clist"), c("cI", 0, 16), 0.0, None, add)
+        ts(c("sc"), c("cI"), 32.0, -4096.0, ge, mul)
+        ts(c("sc", 64, 128), c("sc", 0, 64), 1.0, None, mul)
+        for t in range(3):
+            ts(c("hm", 128 * t, 128 * t + 128), c("c8"), float(t), c("R", 0, 1), eq, mul)
+
+    def setup_s():
+        for k in range(16):
+            act(k_("bkb", k), c("gmb"), AF.Copy, 0.0, c("R", k, k + 1))
+        act(THR, TH, AF.Identity, -2048.5, -1.0)
+        act(c("gth", 0, 8), c("gc", 0, 8), AF.Copy, 0.0, TH)
+        act(c("of32"), c("cI"), AF.Identity, 0.0625, 0.0)
+        act(c("wi", 0, 8), c("gc", 0, 8), AF.Copy, 0.0, KX)
+        mm(c("pq", 0, 8), c("of32"), c("gth", 0, 8), True, True)
+        mm(c("pq", 8, 16), c("of32"), c("gth", 0, 8), True, True)
+        mm(c("pq", 16, 24), c("wn", 0, 128), c("wi", 0, 8), True, True)
+        mm(c("pq", 24, 32), c("wn", 128, 256), c("wi", 0, 8), True, True)
+        act(c("thc"), c("pq", 0, 16), AF.Identity, 0.75 - (7 - rank) / 16.0)
+        act(c("wsc"), c("pq", 16, 32), AF.Identity, -1.21875)
+        act(c("cht"), c("ch"), AF.Identity, L3)
+        act(c("cno"), c("ch"), AF.Identity, 256.0 - 43.23 - 63 * math.log(2.0), -1.0)
+        act(c("ivb"), c("cI"), AF.Copy)
+        act(c("cneg"), c("cI"), AF.Identity, -10240.0, 0.0)
+        act(c("c16"), c("ck"), AF.Identity, 32768.0, -4096.0)
+        act(c("k2"), c("cI"), AF.Identity, 2048.0, 0.0)
+        act(c("c77", 0, 128), c("cI"), AF.Identity, 77.0, 0.0)
+        act(c("c77", 128, 256), c("cI"), AF.Identity, 154.0, 0.0)
+        act(c("fw", 2048, 2064), c("dw", 2048, 2064), AF.Relu, BC)
+        act(c("qlm"), c("gmb"), AF.Copy, 0.0, 128.0)
+        act(c("lenm"), c("gmb"), AF.Copy, 0.0, -256.0)
+        act(c("in8"), c("ihb"), AF.Copy, 0.0, -8192.0)
+        act(c("i8"), c("ihb"), AF.Copy, 0.0, 8192.0)
+        act(c("trit"), c("tri"), AF.Copy, 0.0, 128.0)
+
+    def setup_c():
+        ts(c("stmp"), c("tri"), 256.0, None, mul)
+        tt(c("trie"), c("stmp"), c("i8"), add)
+        ts(c("cst", 0, 128), c("cI"), 2048.0, None, sub)
+        ts(c("cst", 128, 256), c("cI"), 2048.0, None, sub)
+        ts(c("cst", 256, 384), c("ck"), 256.0, 256.0, mul, add)
+        ts(c("dm", 0, 128), c("ck"), KC, None, eq)
+        ts(c("dm", 128, 256), c("ck"), KC, None, eq)
+        ts(c("wts", 0, 2), c("cI", 0, 2), W64, WX, eq, mul)
+
+    def setup_d():
+        ts(c("stmp"), c("tri"), 2.0, None, mul)
+        tt(c("stmp"), c("stmp"), c("ih"), sub)
+        ts(c("trf"), c("stmp"), 4096.0, None, mul)
+
+    def setup_f():
+        ts(c("csl", 0, 128), c("cI"), 16.0, -2048.0, mul, add)
+        ts(c("csl", 128, 256), c("cI"), 16.0, -2048.0, mul, add)
+        ts(c("csl", 256, 384), c("ck"), 256.0, 256.0, mul, add)
+        ts(c("lv"), c("cI"), 16.0, -2032.0, mul, add)
+        ts(PP, PC, 64.0, 4096.0, ge, mul)
+        ts(c("k2l"), c("cI"), 0.0, PP, mul, add)
+        ts(c("k2l"), c("k2l"), 2048.0, None, sub)
+
+    def spread(src, k0, k1):
+        for k in range(k0, k1):
+            mm(c("r%d" % (k // 4), 128 * (k % 4), 128 * (k % 4) + 128), k_("bkb", k), c(src), True, True)
+
+    def thermo(e, dst, i):
+        if e == "V":
+            ts(c(dst, 512 * i, 512 * i + 512), c("r%d" % i), BC, 0.0, add, mx)
+        else:
+            act(c(dst, 512 * i, 512 * i + 512), c("r%d" % i), AF.Relu, BC)
+
+    def pick(e, z, a, b, win, off):
+        if e == "V":
+            ts(c(z, a, b), ind(win, off), -1.0, -256.0, mul, mx)
+        else:
+            act(c(z, a, b), ind(win, off), AF.Relu, 256.0, -1.0)
+
+    def slots_gather(e, i):
+        pick(e, "zf", 1024 * i, 1024 * i + 1024, c("fw"), c("ql", 64 * i, 64 * i + 64))
+
+    HB = ("pa", "pq")
+
+    def slots_sum(h, fin):
+        mm(c(HB[h], 0, 128), c("ih"), c("k2l" if fin else "k2"), True, False)
+        for j in range(16):
+            mm(c(HB[h], j, 128, 16), c("zf", 2048 * h + j, 2048 * h + 2048, 16), c("ngc", 0, 8), False, j == 15)
+
+    def slots_turn(h, between=None):
+        q = c("qt", 128 * h, 128 * h + 128)
+        cp(q, c(HB[h], 0, 128))
+        mm(c(HB[h], 128, 256), q, c("ih"), True, True)
+        e = c("em", 128 * h, 128 * h + 128)
+        ts(e, c(HB[h], 128, 256), 0.0, None, eq)
+        if between:
+            between()
+        mm(c(HB[h], 256, 384), c("trf"), e, True, True)
+
+    def slots_put(h, fin):
+        a, b = 128 * h, 128 * h + 128
+        tt(c("fe", a, b), c(HB[h], 256, 384), c("npl", a, b), mx)
+        if fin:
+            tt(c("wmk", a, b), c(HB[h], 128, 256), c("fe", a, b), mi)
+            ts(c("yqs", a, b), c("wmk", a, b), 2048.0, None, add)
+        else:
+            tt(c("qi", a, b), c(HB[h], 128, 256), c("fe", a, b), mi)
+            ts(c("ql", a, b), c("qi", a, b), 2048.0, None, add)
+
+    def list_queues():
+        mm(c("pq", 128, 256), c("apb"), c("ih"), True, True)
+        tt(c("ub"), ind(c("ui"), c("clist")), c("dm"), mul)
+        for b in (0, 1):
+            mm(c("pq", 64 + 8 * b, 72 + 8 * b), c("ub", 128 * b, 128 * b + 128), c("gc", 0, 8), True, True)
+
+    def applied():
+        cp(c("qp"), c("pq", 128, 256))
+        cp(c("ul"), c("pq", 64, 80))
+
+    def appended():
+        tt(c("wmk"), ind(c("qp"), c("ul")), c("ipm"), eq)
+        tt(c("npl"), ind(c("qlw"), c("ul")), c("wmk"), mul)
+
+    off = [d for d in T.cores if d != core and topo.chip(d) != topo.chip(core)]
+    near = [d for d in T.cores if d != core and topo.chip(d) == topo.chip(core)]
+    off_e = sorted(set(e for d in off for e in topo.engines(core, d)))
+    near_e = [e for d in near for e in topo.engines(core, d) if e not in off_e]
+
+    def did(d):
+        a = topo.addr(d)
+        return DstId(rid=a[0], pnc=a[1])
+
+    def sums(b, a, z0, stop=True):
+        for k in range(16):
+            mm(c(b, a, a + 64), k_("lkb", k), c("mn", z0 + k, z0 + 1024, 16), False, stop and k == 15)
+
+    for t in range(3):
+        last = t == 2
+        land = "land%d" % t
+        for i in (0, 1):
+            act(c("wg", 1024 * i, 1024 * i + 1024), ind(c("wn"), c("ol", 64 * i, 64 * i + 64)), AF.Copy)
+        if t == 0:
+            offsets()
+            empties()
+            cp(c("ihb"), c("ih"))
+            ts(c("stmp"), c("cI"), PC, None, gt)
+            tt(c("tri"), c("stmp"), c("gmb"), mul)
+            setup_b()
+            setup_s()
+        else:
+            for i in range(4):
+                thermo("S", "fw", i)
+            for i in range(4):
+                slots_gather("S", i)
+        mm(c("plo", 0, 128), c("ih"), c("pre"), True, False)
+        mm(c("plo", 64, 128), c("ih"), c("emp", 0, 64), False, False)
+        mm(c("phi", 0, 64), c("ih"), c("pre", 0, 64), True, False)
+
+        def records(i, other):
+            a = 2048 * i + 1024 * other
+            tt(c("mn", a, a + 1024), ind(c("xs"), c("hu", 128 * i + 64 * other, 128 * i + 64 * other + 64)),
+               c("wg", 1024 * i, 1024 * i + 1024), mi)
+            return a
+
+        sums("plo", 0, records(0, 0), False)
+        if t:
+            list_queues()
+        sums("plo", 64, records(0, 1))
+        mm(c("r3", 0, 64), c("ih"), c("emp", 64, 128), True, False)
+        mm(c("r3", 0, 64), c("ih"), c("pre", 0, 64), False, False)
+        sums("phi", 0, records(1, 0))
+        if t == 1:
+            setup_f()
+        cp(c("ml"), c("plo", 0, 64))
+        tt(c("dlo"), c("plo", 64, 128), c("ml"), sub)
+        sums("r3", 0, records(1, 1))
+        if t:
+            applied()
+            appended()
+            slots_sum(0, False)
+        cp(c("sd", 64, 128), c("phi", 0, 64))
+        tt(c("dhi"), c("r3", 0, 64), c("sd", 64, 128), sub)
+        tt(c("dd"), c("dhi"), c("dlo"), add)
+        ts(c("s"), c("dd"), 0.0, None, gt)
+        tt(c("dlo"), c("s"), c("dlo"), mul)
+        tt(c("dhi"), c("s"), c("dhi"), mul)
+        tt(c("cp", 0, 64), c("ml"), c("dlo"), add)
+        tt(c("cp", 64, 128), c("phi", 0, 64), c("dhi"), add)
+        spread("cp", 0, 4)
+        if t:
+            slots_turn(0, lambda: spread("cp", 4, 8))
+        else:
+            spread("cp", 4, 8)
+        spread("cp", 8, 16)
+        thermo("V", "dw", 0)
+        if t:
+            slots_put(0, False)
+        thermo("V", "dw", 2)
+        thermo("S", "dw", 1)
+        thermo("S", "dw", 3)
+        if t:
+            slots_sum(1, False)
+        mm(c("plo", 0, 256), c("on"), c("rho"), True, False)
+        for b in (0, 1):
+            mm(c("plo", 128 * b, 128 * b + 128), c("ctb", 128 * b, 128 * b + 128), c("on"), False, False)
+        for b in (0, 1):
+            m = (32, 64)[b]
+            z = 2048 * b
+            pick("V", "zd", z, z + 16 * m, c("dw"), c("ql", 128 * b, 128 * b + m))
+            pick("S", "zd", z + 16 * m, z + 2048, c("dw"), c("ql", 128 * b + m, 128 * b + 128))
+            if b == 0 and t:
+                slots_turn(1)
+                slots_put(1, False)
+            for j in range(16):
+                mm(c("plo", 128 * b + j, 128 * b + 128, 16), c("zd", z + j, z + 2048, 16), c("ngc", 0, 8), False, b == 1 and j == 15)
+        own = c(land, 16 * rank, 16 * rank + 16)
+        scan(c("tm"), c("rs"), c("plo", 0, 256), mul, mx)
+        cp(own, c("tm", 15, 256, 16))
+        src = T[land][:, 16 * rank:16 * rank + 16]
+        sem = T.sem["arr%d" % t]
+        moves = [RemoteDMATransfer(dst_ids=[did(d) for d in off], dma_engine_mask=sum(1 << e for e in off_e), remote_sem=sem,
+                                   srcs=[src], dsts=[src for d in off])]
+        if near:
+            moves.append(RemoteDMATransfer(dst_ids=[did(d) for d in near], dma_engine_mask=sum(1 << e for e in near_e),
+                                           remote_sem=sem, srcs=[src], dsts=[src for d in near]))
+        run("G", lambda moves=moves: g.remote_dma_fused(moves, local_sem=T.sem.loc), [own], [], inc=0, cost=300.0)
+        sent = len(ops) - 1
+        arrive = len(off_e) * len(off) + len(near_e) * len(near)
+        if t == 0:
+            setup_c()
+        act(c("tsb"), c("plo", 0, 256), AF.Copy)
+        tt(c("x2", 0, 64), c("o", 64, 128), c("o", 0, 64), sub)
+        tt(c("x2", 64, 128), c("cp", 64, 128), c("cp", 0, 64), sub)
+        ts(c("qa"), c("qi"), 3975, None, OP.bitwise_and)
+        tt(c("x2", 128, 192), c("x2", 0, 64), c("s"), mul)
+        tt(c("x2", 192, 256), c("x2", 64, 128), c("s"), mul)
+        ts(c("hfs"), c("qa"), float(t + (2048 if t else 0)), None, eq)
+        tt(c("o2", 0, 64), c("o", 0, 64), c("x2", 128, 192), add)
+        tt(c("o2", 64, 128), c("o", 64, 128), c("x2", 128, 192), sub)
+        tt(c("c2", 0, 64), c("cp", 0, 64), c("x2", 192, 256), add)
+        tt(c("c2", 64, 128), c("cp", 64, 128), c("x2", 192, 256), sub)
+        cp(c("ol2"), c("o2"))
+        for b in (0, 1):
+            mm(c("phi", 128 * b, 128 * b + 128), c("hfs", 128 * b, 128 * b + 128), c("in8"), True, True)
+        mm(c("plo", 0, 128), c("ih"), c("c2"), True, False)
+        mm(c("plo", 0, 128), c("ih"), c("emp"), False, False)
+        mm(c("plo", 0, 128), c("in8"), c("hm", 128 * t, 128 * t + 128), False, False)
+        mm(c("plo", 0, 128), c("ih"), c("sc"), False, False)
+        ts(c("p16", 32, 48), own, 1.0, -100.0, lt, mul)
+        tt(c("ce", 0, 256), c("phi", 0, 256), c("tsb"), add)
+        tt(c("p16", 64, 80), own, c("p16", 32, 48), add)
+        scan(c("ce", 256, 512), c("rb"), c("ce", 0, 256), add, mi)
+        ts(c("p16", 16, 32), c("ce", 271, 512, 16), 1.0, -20000.0, lt, mul)
+        tt(c("p16", 48, 64), c("ce", 271, 512, 16), c("thc"), add)
+        tt(c("p16", 80, 96), c("p16", 48, 64), c("p16", 16, 32), add)
+        tt(c("p16", 112, 128), c("p16", 64, 80), c("p16", 80, 96), gt)
+        tt(c("p16", 128, 144), c("p16", 112, 128), c("p16", 64, 80), mul)
+        mm(c("phi", 0, 384), c("ih"), c("csl" if last else "cst"), True, False)
+        mm(c("r0", 0, 128), c("ih"), c("cneg"), True, False)
+        mm(c("r0", 0, 128), c("ih"), c("o2"), False, False)
+        if t == 0:
+            setup_d()
+        tt(c("kt", 0, 64), c(land, 0, 64), c(land, 64, 128), mx)
+        ops[-1] = ops[-1][:7] + (lambda sem=sem, n=arrive: g.vector.wait_ge(sem, n),)
+        trips.append((sent, len(ops) - 1))
+        tt(c("kt", 64, 96), c("kt", 0, 32), c("kt", 32, 64), mx)
+        tt(c("kp"), c("kt", 64, 80), c("kt", 80, 96), mx)
+        ts(c("kb"), ind(c("kp"), c("clist")), -2048.21875, None, add)
+        for b in (0, 1):
+            mm(c("pa", 128 * b, 128 * b + 128), c("kb", 128 * b, 128 * b + 128), c("ih"), True, True)
+        tt(c("zi"), c("kp"), c("wsc"), add)
+        tt(c("p16", 96, 112), c("kp"), c("p16", 128, 144), eq)
+        ts(c("ui"), c("zi"), 127, None, OP.bitwise_and)
+        ts(c("wm", 0, 256), c("pa", 0, 256), BC, 0.0, add, mx)
+        for i in (0, 1):
+            pick("V", "ze", 1024 * i, 1024 * i + 512, c("wm"), c("ol2", 64 * i, 64 * i + 32))
+            pick("S", "ze", 1024 * i + 512, 1024 * i + 1024, c("wm"), c("ol2", 64 * i + 32, 64 * i + 64))
+            for k in range(16):
+                mm(c("plo", 64 * i, 64 * i + 64), k_("lkb", k), c("ze", 1024 * i + k, 1024 * i + 1024, 16), False, i == 1 and k == 15)
+        cp(c("p16", 144, 160), c("ui"))
+        for i in range(16):
+            ts(k_("oh", i), c("ivb"), c("p16", 144 + i, 145 + i), c("p16", 96 + i, 97 + i), eq, mul)
+        ts(c("st"), c("plo", 0, 128), THR, None, ge)
+        mm(c("r0", 0, 128), c("trie"), c("st"), False, True)
+        mm(c("phi", 0, 128), c("tri" if last else "trit"), c("st"), False, False)
+        mm(c("phi", 128, 256), c("gmb" if last else "qlm"), c("st"), False, False)
+        mm(c("phi", 256, 384), c("st"), c("lenm"), False, True)
+        mm(c("plo", 0, 128), c("ih"), c("c16"), True, False)
+        for i in range(16):
+            b, h = i // 8, i % 8
+            mm(c("pq", 4 * h + 2 * b, 4 * h + 2 * b + 2), k_("oh", i), c("wts", 0, 2), True, True)
+        act(c("lna", 0, 32), c("pq", 0, 32), AF.Ln, 2.0 ** -63)
+        cp(c("e16"), c("r0", 0, 128))
+
+        def follow():
+            tt(c("tt"), c("phi", 0, 128), c("st"), mul)
+            tt(c("x2", 0, 64), c("tt", 64, 128), c("tt", 0, 64), sub)
+            tt(c("x2", 64, 128), c("x2", 0, 64), c("s"), mul)
+            tt(c("tof", 0, 64), c("tt", 0, 64), c("x2", 64, 128), add)
+            tt(c("tof", 64, 128), c("tt", 64, 128), c("x2", 64, 128), sub)
+
+        if last:
+            follow()
+            spread("tof", 0, 16)
+        for r in range(16):
+            ts(k_("fr", r), c("e16"), 256.0 * r - 2048.0, 256.0 * r - 1792.0, mx, mi)
+            mm(c("plo", r, 128, 16), k_("fr", r), c("gc", 0, 8), False, r == 15)
+        if not last:
+            follow()
+        ts(c("lna", 32, 64), c("pq", 0, 32), 1e-14, None, lt)
+        tt(c("lna", 64, 96), c("lna", 32, 64), c("cno"), mul)
+        ts(c("corr"), c("phi", 256, 384), 256.0, None, mi)
+        tt(c("lna", 32, 64), c("lna", 64, 96), c("cht"), add)
+        tt(c("lna", 96, 128), c("lna", 32, 64), c("lna", 0, 32), sub)
+        ts(c("iseq"), c("phi", 256, 384), 256.0, None, eq)
+        scan(c("lna", 128, 160), c("rb4"), c("lna", 96, 128), add, mi)
+        if last:
+            tt(c("l16"), c("phi", 128, 256), c("lv"), lt)
+        else:
+            act(c("qlw"), c("phi", 128, 256), AF.Copy)
+        if last:
+            tt(c("qlw"), c("phi", 128, 256), c("l16"), mul)
+        ts(c("apf"), c("lna", 131, 160, 4), 12582912.0, 12583168.0, add, sub)
+        tt(c("appl"), ind(c("apf"), c("clist", 0, 8)), c("iseq"), mul)
+        tt(c("corr"), c("corr"), c("appl"), add)
+        act(c("apb"), ind(c("apf"), c("clist", 0, 8)), AF.Copy)
+        tt(c("o3t"), c("plo", 0, 128), c("corr"), add)
+        mm(c("plo", 128, 256), c("o3t"), c("ih"), True, True)
+        if not last:
+            h_consts(t + 1)
+            cp(c("o"), c("plo", 128, 256))
+            cp(c("ol"), c("plo", 128, 256))
+            h_data()
+            spread("tof", 0, 16)
+            offsets()
+            empties()
+        else:
+            cp(c("yo"), c("plo", 128, 256))
+            run("Y", lambda: g.sync.dma_start(T.yoc[:, :], T.yo[:, :]), [c("yo")], [], sem="d_yo", inc=16)
+            list_queues()
+            for i in range(4):
+                thermo("VS"[i & 1], "fw", i)
+            applied()
+            appended()
+            for h in (0, 1):
+                slots_gather("V", 2 * h)
+                slots_gather("S", 2 * h + 1)
+                slots_sum(h, True)
+            for h in (0, 1):
+                slots_turn(h)
+                slots_put(h, True)
+            run("Y", lambda: g.sync.dma_start(T.yq[:, :], T.yqs[:, :]), [c("yqs")], [], sem="d_yq", inc=16)
+    if "order" not in PLAN:
+        PLAN["order"] = plan(ops, trips)
+    for i in PLAN["order"]:
+        emit(*ops[i])
+    g.sync.wait_ge(T.sem.d_yo, 16)
+    g.sync.wait_ge(T.sem.d_yq, 16)
+    for e in ("V", "S", "P", "G"):
+        g.wait_ge(T.sem["c" + e], count[e])
+    g.wait_ge(T.sem.loc, 3 * (len(off_e) + (len(near_e) if near else 0)))

@@ -10,33 +10,37 @@ def _sb(dtype, **names):
 
 
 SCRATCH = {}
-SCRATCH.update(_sb(BF, xs=8192, wn=272, gmb=128, lkb=2048, apb=128, bkb=2048, tri=128, i8=128, in8=128, qlm=128, lenm=128,
-                   trit=128, cneg=128, c16=128, k2=128, c77=256, trf=128, ihb=128, sm=64, ctb=256, on=128, rho=256,
-                   dm=256, ivb=128, hm=384, wg=2048, mn=4096, zd=4096, zf=4096, ze=2048, hfs=256,
-                   oh=2048, ub=256))
+SCRATCH.update(_sb(BF, xs=8192, wn=272, lkb=2048, mat=3328, pm=512, pu=512, sm=160, c77=256, rho=128, dm=256, hm=384, wt=384,
+                   cT=768, ty=256, p8=256, wg=2048, mn=4096, zd=4096, zf=4096, ze=2048, oh=2048, dw=2064, fw=2064, hfs=256,
+                   hfd=256, ub=256, qs16=256, qt=256, uw=256, sg=256, sgt=256, hi=128, o=128, emp=128, st=128, tof=128, ob=128,
+                   tb=128, apx=128, apm=128, l1=128, l2=128))
 SCRATCH.update(_sb(I32, oci=128, qsi=256, thi=1, cint=8, qi=256, qa=256, hz=256, hm13=256, zu=32))
 SCRATCH.update(_sb(U16, ol=128, ql=256, hu=256, ol2=128, clist=16, ul=16))
-SCRATCH.update(_sb(H, ih=128, sh=128, stmp=128, hcb=256, i37=128, pre=128, emp=128, sc=128, trie=128, cst=384, csl=384,
-                   k2l=128, o=128, cp=128, c2=128, o2=128, kb=256, st=128, e16=128, fr=2048, o3t=128, tof=128, em=256,
-                   qt=256))
-SCRATCH.update(_sb(F32, col=32, cI=128, cg=128, ck=128, c8=128, ipm=256, rs=256, rb=256, rb4=32, ch=32, cht=32, cno=32, R=16, n8=128,
-                   sx=320, pc=48, of32=128, y1=128, sd=128, dw=2064, fw=2064, tsb=256, tm=256, land0=128, land1=128,
-                   land2=128, x2=256, ce=512, p16=160, kt=128, kp=16, wm=272, lna=160, apf=8, qp=128, corr=128, iseq=128,
-                   appl=128, qlw=128, l16=128, lv=128, tt=128, wmk=256, npl=256, fe=256, yo=128, yqs=256))
+SCRATCH.update(_sb(H, stmp=128, stmp2=128, cB=129, frac=128, pre=128, thb=128, thx=256, q16=256, qo=256, cp=128, o2c=256, k16=16,
+                   kb=256, e16=128, fr=2048))
+SCRATCH.update(_sb(F32, col=32, cI=128, cg=128, ck=128, n0=128, rs=128, rb4=32, ch=32, cht=32, R=16, R2=8, n8=128, sx=384, wsc=16,
+                   y1=128, ym=128, tm=256, land0=128, land1=128, land2=128, x2=256, p16=64, kt=128, kp=16, wm=272, lna=160,
+                   apf=8, e2=128, tab=128, cs=256, npl=256, np2=256, yo=128, yqs=256))
 PSUM = ("r0", "r1", "r2", "r3", "pa", "plo", "phi", "pq")
 SCRATCH.update({n: ("psum", [128, 512], F32) for n in PSUM})
 SEMAPHORES = ["cV", "cS", "cP", "cG", "d_oc", "d_qs", "d_wn", "d_th", "d_x", "d_yo", "d_yq", "arr0", "arr1", "arr2", "loc"]
 PART = {"pint": ("cint", 0, 1), "kint": ("cint", 1, 1), "gint": ("cint", 2, 1), "lint": ("cint", 3, 1), "hint": ("cint", 4, 1),
-        "dlo": ("sx", 0, 64), "dd": ("sx", 64, 64), "s": ("sx", 128, 64), "ml": ("sx", 192, 64), "dhi": ("sx", 256, 64),
-        "gc": ("sm", 0, 16), "ngc": ("sm", 16, 16), "wi": ("sm", 32, 16), "wts": ("sm", 48, 16), "gth": ("pc", 0, 16),
-        "thc": ("pc", 16, 16), "wsc": ("pc", 32, 16), "zi": ("zu", 0, 16), "ui": ("zu", 16, 16)}
+        "oint": ("cint", 5, 1), "dlo": ("sx", 0, 64), "dd": ("sx", 64, 64), "s": ("sx", 128, 64), "ml": ("sx", 192, 64),
+        "dhi": ("sx", 256, 64), "mh": ("sx", 320, 64), "gc": ("sm", 0, 8), "wi": ("sm", 32, 8), "g3": ("sm", 48, 48),
+        "wf": ("sm", 96, 32), "o2": ("o2c", 0, 128), "c2": ("o2c", 128, 128), "zi": ("zu", 0, 16), "ui": ("zu", 16, 16),
+        "free": ("p16", 0, 16), "ak": ("p16", 16, 16), "uf": ("p16", 32, 16), "asks": ("p16", 48, 16)}
+PART.update({n: ("mat", 128 * i, 128) for i, n in enumerate(
+    ("gmb", "ihb", "tri", "i8", "in8", "i4k", "n4k", "i37b", "i256", "i16", "gneg", "m1", "m2", "trf", "sc", "on", "ivb", "k2",
+     "cA", "cC", "sb", "r16", "nih", "t1", "t2", "hd"))})
+FIRST = 20
+CV, DV, TV, EV, FV, US = (64, 64), 64, (8, 10), 208, (40, 56), 5
 
 
-CYCLE, WAKE, TRIP, SLACK = 1.0, 120.0, 4700.0, 5.0
+CYCLE, WAKE, TRIP, PASSES = 1.04, 70.0, 3000.0, 1500
 PLAN = {}
 
 
-def plan(ops, trips):
+def plan(ops, links):
     n = len(ops)
     pred = [dict() for _ in range(n)]
     hist, bank = {}, {}
@@ -59,60 +63,112 @@ def plan(ops, trips):
                 if wr:
                     h[:] = [a for a in h if not (lo <= a[1] and a[2] <= hi)]
                 h.append((wr, lo, hi, i))
-    for a, b in trips:
-        pred[b][a] = 2
-    succ = [[] for _ in range(n)]
+    dmas = [i for i in range(n) if ops[i][0] == "Y"]
+    for a, b in zip(dmas, dmas[1:]):
+        pred[b].setdefault(a, 0)
+    for a, b, k in links:
+        pred[b][a] = max(k, pred[b].get(a, 0))
+    queue = [op[0] for op in ops]
+    cost = [op[6] for op in ops]
+    held = [70.0 if op[0] == "Y" else op[6] for op in ops]
+    gap = (0.0, WAKE, TRIP)
+    before = [[(p, (held if k == 0 else cost)[p] + gap[k]) for p, k in pred[i].items()] for i in range(n)]
+    after = [[] for _ in range(n)]
     for i in range(n):
-        for p, k in pred[i].items():
-            succ[p].append((i, k))
+        for p, d in before[i]:
+            after[p].append((i, d))
+
+    def lay(key, back):
+        near = after if back else before
+        key, at = list(key), [0.0] * n
+        for i in (range(n - 1, -1, -1) if back else range(n)):
+            for p, d in near[i]:
+                if key[p] >= key[i]:
+                    key[i] = key[p] + 1e-3
+        busy = {e: ([], []) for e in "VSPGY"}
+        for i in sorted(range(n), key=lambda q: key[q]):
+            h = held[i]
+            t = cost[i] - h if back else 0.0
+            for p, d in near[i]:
+                x = at[p] + d - h if back else at[p] + d
+                if x > t:
+                    t = x
+            starts, ends = busy[queue[i]]
+            lo, hi = 0, len(ends)
+            while lo < hi:
+                mid = (lo + hi) // 2
+                if ends[mid] <= t:
+                    lo = mid + 1
+                else:
+                    hi = mid
+            while lo < len(ends) and starts[lo] < t + h - 1e-6:
+                t = ends[lo]
+                lo += 1
+            starts.insert(lo, t)
+            ends.insert(lo, t + h)
+            at[i] = t + h if back else t
+        return at
+
+    def tried(key):
+        at = lay(key, False)
+        order = sorted(range(n), key=lambda q: (at[q], q))
+        free, newest, end, why = dict.fromkeys("VSPGY", 0.0), dict.fromkeys("VSPGY", -1), [0.0] * n, [-1] * n
+        for i in order:
+            e = queue[i]
+            t, why[i] = free[e], newest[e]
+            for p, k in pred[i].items():
+                if k and (k == 2 or end[p] > free[e] or newest[e] == p) and end[p] + gap[k] > t:
+                    t, why[i] = end[p] + gap[k], p
+            end[i], free[e], newest[e] = t + cost[i], t + held[i], i
+        i = max(range(n), key=lambda q: end[q])
+        total, pairs = end[i], []
+        while why[i] >= 0:
+            if why[i] not in pred[i] or pred[i][why[i]] == 1 and queue[why[i]] == queue[i]:
+                pairs.append((why[i], i))
+            i = why[i]
+        return total, order, at, pairs
+
+    seed = [1]
+
+    def draw(k):
+        seed[0] = (seed[0] * 1103515245 + 12345) % 2147483648
+        return seed[0] * k // 2147483648
+
+    def sooner(key, i, k):
+        todo = {i}
+        key[i] = k
+        while todo:
+            j = max(todo)
+            todo.remove(j)
+            for p in pred[j]:
+                if key[p] >= key[j]:
+                    key[p] = key[j] - 1e-3
+                    todo.add(p)
+
     way = [0.0] * n
     for i in range(n - 1, -1, -1):
-        way[i] = ops[i][6] + max([way[j] + (0, WAKE, TRIP)[k] for j, k in succ[i]] or [0.0])
-
-    def forward(urgent, back):
-        after = succ if not back else [list(p.items()) for p in pred]
-        before = [list(p.items()) for p in pred] if not back else succ
-        left = [len(p) for p in before]
-        ready = {e: [i for i in range(n) if ops[i][0] == e and not left[i]] for e in "VSPGY"}
-        free, newest, end, order = dict.fromkeys("VSPGY", 0.0), dict.fromkeys("VSPGY", -1), [0.0] * n, []
-
-        def begin(i):
-            e = ops[i][0]
-            t = free[e]
-            for p, k in before[i]:
-                if k == 2:
-                    t = max(t, end[p] + TRIP)
-                elif k == 1 and (end[p] > free[e] or newest[e] == p):
-                    t = max(t, end[p] + WAKE)
-            return t
-
-        while len(order) < n:
-            best = None
-            for e in "VSPGY":
-                if ready[e]:
-                    st = [(begin(i), i) for i in ready[e]]
-                    t0 = min(st)[0]
-                    t, i = max(((t, i) for t, i in st if t <= t0 + SLACK), key=lambda q: (urgent[q[1]], q[1] if back else -q[1]))
-                    if best is None or t < best[0]:
-                        best = (t, i, e)
-            t, i, e = best
-            ready[e].remove(i)
-            end[i] = t + ops[i][6]
-            free[e] = t + 70 if e == "Y" and not back else end[i]
-            newest[e] = i
-            order.append(i)
-            for j, k in after[i]:
-                left[j] -= 1
-                if not left[j]:
-                    ready[ops[j][0]].append(j)
-        return max(end), order, end
-
-    best, urgent = None, way
-    for i in range(4):
-        total, order, end = forward(urgent, False)
-        if best is None or total < best[0]:
-            best = (total, order)
-        urgent = forward(end, True)[2]
+        way[i] = max([way[j] + d for j, d in after[i]] + [cost[i]])
+    best = now = tried([-w for w in way])
+    for k in range(PASSES):
+        key = list(now[2])
+        if k % 16 == 0:
+            key = [-a for a in lay([-(key[i] + cost[i]) for i in range(n)], True)]
+        for _ in range(1 + draw(2)):
+            u, v = now[3][draw(len(now[3]))]
+            if u in pred[v]:
+                later = [j for j in range(n) if queue[j] == queue[v] and key[v] < key[j] < key[v] + 1500.0]
+                if later:
+                    sooner(key, later[draw(len(later))], key[v] - 0.5)
+            elif draw(2):
+                sooner(key, v, key[u] - 1.0 - draw(2) * draw(1500))
+            else:
+                key[u] = key[v] + 1.0 + draw(2) * draw(1500)
+        new = tried(key)
+        if new[0] <= now[0] + 30.0:
+            now = new
+            if new[0] < best[0]:
+                best = new
+    PLAN["length"] = best[0]
     return best[1]
 
 
@@ -125,7 +181,8 @@ def rank_program(g, core, T, topo):
     known = {e: {} for e in eng}
     snap = {}
     ops = []
-    trips = []
+    links = []
+    mark = {}
     hist = {}
     bank = {}
 
@@ -139,6 +196,16 @@ def rank_program(g, core, T, topo):
 
     def run(e, fn, reads, writes, sem=None, inc=1, cost=100.0, pre=None):
         ops.append((e, fn, reads, writes, sem, inc, cost, pre))
+
+    def name(n):
+        mark[n] = len(ops) - 1
+
+    def behind(*names):
+        links.extend((mark[n], len(ops) - 1, 0) for n in names)
+
+    def follows(n):
+        behind(n)
+        name(n)
 
     def emit(e, fn, reads, writes, sem, inc, cost, pre):
         evs = []
@@ -186,6 +253,9 @@ def rank_program(g, core, T, topo):
             lo, hi = 0, w
         return (n, at + lo, at + hi, step)
 
+    def k_(b, k):
+        return c(b, 128 * k, 128 * k + 128)
+
     def ap(x):
         if x[0] == "ind":
             return ap(x[1]).indirect(ap(x[2]))
@@ -232,10 +302,19 @@ def rank_program(g, core, T, topo):
     def fill(out, v):
         run("V", lambda: g.vector.memset(ap(out), v), [], [out], cost=took(out))
 
-    def act(out, a, func, bias=0.0, scale=1.0):
+    def turn(out, a):
+        run("V", lambda: g.vector.transpose(ap(out), ap(a)), [a], [out], cost=took(out, a))
+
+    def act(out, a, func=AF.Copy, bias=0.0, scale=1.0):
         cost = 65 + 1.56 * CYCLE * wide(out) if a[0] == "ind" else CYCLE * max(64, wide(out))
         run("S", lambda: g.scalar.activation(ap(out), ap(a), func, bias=val(bias), scale=val(scale)), rd(a, bias, scale), [out],
-            cost=cost + (1300 if func == AF.Exp else 0))
+            cost=cost + (1300 if func == AF.Exp else 1500 if func == AF.Ln and wide(out) == 1 else 0))
+
+    def times(out, a, f):
+        act(out, a, AF.Copy, 0.0, f)
+
+    def even(out, v):
+        act(out, c("cI"), AF.Identity, v, 0.0)
 
     def mm(out, l, r, start, stop):
         run("P", lambda: g.tensor.matmul(ap(out), ap(l), ap(r), start, stop), rd(l, r), [out],
@@ -248,173 +327,194 @@ def rank_program(g, core, T, topo):
         else:
             run("G", lambda: g.iota(ap(out), pattern, base, cm), [], [out], cost=cost)
 
+    def select(out, a, pattern, op, other, base, cm):
+        run("G", lambda: g.affine_select(ap(out), ap(a), pattern, op, other, base, cm), [a], [out], cost=170 + 2 * CYCLE * wide(out))
+
+    def diag(out, a, d, op=OP.is_equal, other=0.0):
+        select(out, a, [[1, 128]], op, other, -d, -1)
+
     def load(e, sem, b, hi, src):
-        run(e, lambda: eng[e].dma_start(T[b][:, 0:hi], src), [], [c(b, 0, hi)], sem=sem, inc=16, cost=9000.0 if b == "xs" else 2000.0)
+        run(e, lambda: eng[e].dma_start(T[b][:, 0:hi], src), [], [c(b, 0, hi)], sem=sem, inc=16, cost=7000.0 if b == "xs" else 1200.0)
 
-    def k_(b, k):
-        return c(b, 128 * k, 128 * k + 128)
-
-    PC, KC, GC, K8, BC, TH, THR, P64, W64, WX, PP, L3, LN, KX = [c("col", i, i + 1) for i in range(14)]
+    PC, KC, GC, BC, TH, THR, P64, W64, WX, W0, W1, L3, LN, KX, K2, EVN, ODD, BK, BT, P0, P1 = [c("col", i, i + 1) for i in range(21)]
     add, sub, mul, mx, mi, eq, ge, gt, lt = (OP.add, OP.subtract, OP.mult, OP.max, OP.min, OP.is_equal, OP.is_ge, OP.is_gt, OP.is_lt)
+    AND, SHR = OP.bitwise_and, OP.arith_shift_right
+    BIG, RHO = float(1 << 22), (7 - rank) / 16.0
 
     load("Y", "d_oc", "oci", 128, T.oc[:, :])
     load("Y", "d_wn", "wn", 256, T.want[:, :])
-    load("Y", "d_x", "xs", 8192, T.x[:, :])
     load("Y", "d_qs", "qsi", 256, T.qs[:, :])
     load("Y", "d_th", "thi", 1, T.th[:, :])
+    load("Y", "d_x", "xs", 8192, T.x[:, :])
 
     iota(c("pint"), [[0, 1]], 0, 1)
     iota(c("cI"), [[1, 128]], 0, 0)
     iota(PC, [[0, 1]], 0, 1)
     iota(c("cg"), [[1, 8], [0, 16]], 0, 0)
     iota(c("ck"), [[0, 8], [1, 16]], 0, 0)
-    iota(c("c8"), [[0, 16], [1, 8]], 0, 0)
     iota(c("ch"), [[0, 8], [64, 4]], 0, 0)
-    iota(c("ipm"), [[1, 256]], -256, 0)
+    iota(c("n0"), [[256, 8], [1, 16]], 0, 0)
+    iota(c("p8"), [[8192, 256]], 0, 0)
+    iota(c("cC"), [[0, 8], [-3840, 16]], 28928, 0)
+    iota(k_("ty", 0), [[16, 8], [128, 16]], 0, 0)
+    iota(k_("ty", 1), [[16, 128]], 0, 0)
+    iota(k_("cT", 0), [[0, 128]], 0, 0)
+    iota(k_("cT", 1), [[-128, 2], [0, 64]], 64, 0)
+    iota(k_("cT", 3), [[64, 2], [0, 4], [1, 16]], 0, 0)
+    iota(k_("cT", 4), [[-64, 2], [0, 4], [1, 16]], 64, 0)
+    iota(c("lkb", 512, 2048), [[0, 1536]], 0, 0)
 
+    fill(c("lkb", 0, 512), 0.0)
     fill(c("wn", 256, 272), 0.0)
-    fill(c("lkb"), 0.0)
     fill(LN, math.exp(43.23))
-    fill(c("dw", 2048, 2064), 0.0)
+    fill(c("dw", 2048, 2064), -1024.0)
+    fill(c("fw", 2048, 2064), 128.0)
     fill(c("wm", 256, 272), 0.0)
-    ts(c("kint"), c("pint"), 15, None, OP.bitwise_and)
-    ts(c("gint"), c("pint"), 4, None, OP.arith_shift_right)
-    ts(c("lint"), c("pint"), 63, None, OP.bitwise_and)
-    ts(c("hint"), c("pint"), 6, None, OP.arith_shift_right)
+    fill(c("frac"), -0.46875)
+    fill(c("pre"), -2047.0)
+    ts(c("kint"), c("pint"), 15, None, AND)
+    ts(c("gint"), c("pint"), 4, None, SHR)
+    ts(c("lint"), c("pint"), 63, None, AND)
+    ts(c("hint"), c("pint"), 6, None, SHR)
+    ts(c("oint"), c("pint"), 4, 1, SHR, AND)
     cp(KC, c("kint"))
     cp(GC, c("gint"))
     cp(P64, c("lint"))
     cp(W64, c("hint"))
+    cp(ODD, c("oint"))
+    ts(EVN, ODD, -1.0, 1.0, mul, add)
     ts(c("gmb"), c("cg"), GC, None, eq)
-    ts(c("ih"), c("cI"), PC, None, eq)
+    ts(c("ihb"), c("cI"), PC, None, eq)
     ts(c("R"), c("cI", 0, 16), KC, None, eq)
-    ts(K8, KC, 0.125, None, mul)
-    ts(c("stmp"), c("cI"), 1.0, PC, sub, eq)
-    ts(c("hcb", 0, 128), c("cI"), c("R", 0, 1), 8.5, mul, add)
-    ts(c("hcb", 128, 256), c("cI"), 0.0, -0.46875, mul, add)
-    tt(c("sh"), c("stmp"), c("gmb"), mul)
-    ts(c("i37"), c("ih"), 37.0, None, mul)
-    ts(c("n8"), c("cI"), 2.0, K8, mul, add)
-    cp(c("o"), c("oci"))
-    cp(c("ol"), c("oci"))
+    ts(K2, KC, 2.0, None, mul)
     act(WX, P64, AF.Exp, 43.0, -1.0)
     act(L3, LN, AF.Ln)
+    times(k_("pm", 0), c("ihb"), EVN)
+    times(k_("pm", 3), c("ihb"), ODD)
+    even(c("t1"), EVN)
+    even(c("t2"), ODD)
+    diag(k_("pm", 1), c("t1"), 16)
+    diag(k_("pm", 2), c("t2"), -16)
+    times(c("i37b"), c("ihb"), 37.0)
+    times(c("in8"), c("ihb"), -8192.0)
+    ts(c("n8"), c("n0"), 0.125, K2, mul, add)
+    ts(c("stmp"), c("cg"), 16.0, KC, mul, add)
+    ts(c("stmp2"), c("ck"), 0.0, None, eq)
+    tt(c("stmp"), c("stmp"), c("stmp2"), mul)
+    ts(c("cB", 0, 128), c("stmp"), 8.5, None, add)
+    fill(c("cB", 128, 129), 0.0)
     for k in range(16):
-        act(c("lkb", 128 * k + k, 128 * k + 128, 16), c("gmb", k, 128, 16), AF.Copy)
-    ts(c("pre"), c("cI"), 0.0, -2047.0, mul, add)
+        act(c("lkb", 128 * k + k, 128 * k + 128, 16), c("gmb", k, 128, 16))
 
-    def h_consts(t):
-        mm(c("pa", 0, 256), c("ih"), c("hcb"), True, False)
-        if t:
-            mm(c("pa", 128, 256), c("ih"), c("c77", 128 * (t - 1), 128 * t), False, False)
+    def relay(src, b):
+        turn(c("tb"), c(src))
+        name("tb")
+        for u in range(4):
+            for c2 in (0, 1):
+                for g2 in (0, 1):
+                    mm(c(b, 32 * u + 16 * c2, 32 * u + 16 * c2 + 16), k_("pm", 2 * c2 + g2), c("tb", 32 * u + 16 * g2, 32 * u + 16 * g2 + 16),
+                       (u, c2, g2) == (0, 0, 0), (u, c2, g2) == (3, 1, 1))
 
-    def h_data():
-        mm(c("pa", 0, 128), c("sh"), c("o"), False, False)
-        mm(c("pa", 128, 256), c("i37"), c("o"), False, True)
+    A0, R1, R0 = c("pa", 0, 128), c("pa", 129, 257), c("pa", 257, 385)
 
-    def empties():
-        ts(c("emp"), c("o"), 256.0, -8192.0, ge, mul)
-
-    h_consts(0)
-    h_data()
+    def persons(src):
+        act(c("o"), src)
+        act(c("emp"), src, AF.Relu, -255.0)
+        name("emp")
 
     def offsets():
-        tt(c("y1"), c("pa", 0, 128), c("n8"), mul)
-        for i in (0, 1):
-            q, a = 64 * i, 128 * i
-            tt(c("hz", a, a + 64), c("y1", q, q + 64), c("pa", 128 + q, 192 + q), add)
-            tt(c("hz", a + 64, a + 128), c("y1", 64 - q, 128 - q), c("pa", 128 + q, 192 + q), add)
-            ts(c("hm13", a, a + 128), c("hz", a, a + 128), 8191, None, OP.bitwise_and)
-            cp(c("hu", a, a + 128), c("hm13", a, a + 128))
+        tt(c("y1"), A0, c("n8"), mul)
+        for a, y, p in ((0, 0, 0), (64, 64, 0), (128, 64, 64), (192, 0, 64)):
+            tt(c("hz", a, a + 64), c("y1", y, y + 64), c("pa", 129 + p, 193 + p), add)
+            if a & 64:
+                ts(c("hm13", a - 64, a + 64), c("hz", a - 64, a + 64), 8191, None, AND)
+                cp(c("hu", a - 64, a + 64), c("hm13", a - 64, a + 64))
 
-    def setup_b():
-        ts(c("qa"), c("qsi"), 15, None, OP.bitwise_and)
-        ts(c("hm13"), c("qsi"), 4, None, OP.arith_shift_right)
-        ts(c("qi"), c("qsi"), 2048.0, 1920.0, ge, mul)
-        ts(c("qa"), c("qa"), 128.0, None, mul)
-        tt(c("hm13"), c("hm13"), c("qi"), add)
-        tt(c("qi"), c("qa"), c("hm13"), add)
-        cp(c("ql"), c("qi"))
+    cp(c("ob"), c("oci"))
+    relay("ob", "r0")
+    ts(c("ol"), k_("r0", 0), 256.0, None, mi)
+    persons(k_("r0", 0))
+    mm(c("pa", 0, 129), c("ihb"), c("cB"), True, False)
+    mm(R1, c("i37b"), c("o"), False, False)
+    mm(R1, c("ihb"), c("frac"), False, False)
+    for u in range(8):
+        mm(c("pa", 16 * u + 1, 16 * u + 16), c("ihb"), c("o", 16 * u, 16 * u + 15), False, u == 7)
+
+    def setup():
+        ts(c("qa"), c("qsi"), 4, 15, SHR, AND)
+        ts(c("hm13"), c("qsi"), 8, 7, SHR, AND)
+        cp(c("q16"), c("qsi"))
+        ts(c("hfs"), c("qa"), 112.0, None, mul)
+        ts(c("hfd"), c("hm13"), -240.0, None, mul)
+        for i, b in enumerate(("q16", "hfs", "hfd")):
+            mm(c("pq", 0, 256), c("ihb"), c(b), i == 0, i == 2)
+        cp(c("qi"), c("pq", 0, 256))
+        cp(c("ql"), c("pq", 0, 256))
         ts(BC, KC, -256.0, 2048.0, mul, add)
         ts(KX, KC, 16.0, None, mul)
-        cp(TH, c("thi"))
-        cp(c("gc", 0, 8), c("gmb", 0, 128, 16))
-        ts(c("ngc", 0, 8), c("gc", 0, 8), -1.0, None, mul)
-        ts(c("ctb", 0, 128), c("cI"), 32.0, 32.0, ge, mul)
-        ts(c("ctb", 128, 256), c("cI"), 64.0, 32.0, ge, mul)
-        fill(c("on"), 1.0)
-        fill(c("rho"), (7 - rank) / 2048.0)
-        for b in (0, 1):
-            ts(c("rs", 128 * b, 128 * b + 128), c("ck"), 0.0, None, gt)
-            ts(c("rb", 128 * b, 128 * b + 128), c("ck"), 0.0, 1e5, eq, mul)
-        ts(c("rb4"), c("ch"), 0.0, 1e5, eq, mul)
+        ts(TH, c("thi"), 2048.0, None, sub)
+        cp(c("gc"), c("gmb", 0, 128, 16))
+        ts(c("lint"), c("pint"), 1, None, AND)
+        cp(P1, c("lint"))
+        ts(P0, P1, -1.0, 1.0, mul, add)
+        ts(c("lint"), c("pint"), 1, 7, SHR, AND)
+        cp(K2, c("lint"))
+        ts(c("R2"), c("cI", 0, 8), K2, None, eq)
+        for i, par in enumerate((P0, P1)):
+            even(c("t1"), par)
+            diag(k_("pu", 2 * i), c("t1"), 1 - 2 * i)
+            times(c("t1"), k_("pu", 2 * i), -1.0)
+            diag(c("t2"), c("t1"), 0, OP.not_equal, 1.0)
+            times(k_("pu", 2 * i + 1), c("t2"), par)
+        even(c("on"), 1.0)
+        even(c("rho"), RHO / 128.0)
+        even(c("r16"), 16.0)
+        act(c("rs"), c("ck"), AF.Sign)
+        act(c("rb4"), c("ch"), AF.Relu, 1e5, -1e5)
         ts(c("clist"), c("cI", 0, 16), 0.0, None, add)
-        ts(c("sc"), c("cI"), 32.0, -4096.0, ge, mul)
-        ts(c("sc", 64, 128), c("sc", 0, 64), 1.0, None, mul)
+        even(c("hd"), c("R", 0, 1))
         for t in range(3):
-            ts(c("hm", 128 * t, 128 * t + 128), c("c8"), float(t), c("R", 0, 1), eq, mul)
-
-    def setup_s():
-        for k in range(16):
-            act(k_("bkb", k), c("gmb"), AF.Copy, 0.0, c("R", k, k + 1))
-        act(THR, TH, AF.Identity, -2048.5, -1.0)
-        act(c("gth", 0, 8), c("gc", 0, 8), AF.Copy, 0.0, TH)
-        act(c("of32"), c("cI"), AF.Identity, 0.0625, 0.0)
-        act(c("wi", 0, 8), c("gc", 0, 8), AF.Copy, 0.0, KX)
-        mm(c("pq", 0, 8), c("of32"), c("gth", 0, 8), True, True)
-        mm(c("pq", 8, 16), c("of32"), c("gth", 0, 8), True, True)
-        mm(c("pq", 16, 24), c("wn", 0, 128), c("wi", 0, 8), True, True)
-        mm(c("pq", 24, 32), c("wn", 128, 256), c("wi", 0, 8), True, True)
-        act(c("thc"), c("pq", 0, 16), AF.Identity, 0.75 - (7 - rank) / 16.0)
-        act(c("wsc"), c("pq", 16, 32), AF.Identity, -1.21875)
+            select(k_("hm", t), c("hd"), [[0, 16], [1, 8]], eq, 0.0, -t, 0)
+        times(c("wi"), c("gc"), KX)
+        mm(c("pq", 256, 264), k_("wn", 0), c("wi"), True, True)
+        mm(c("pq", 264, 272), k_("wn", 1), c("wi"), True, True)
+        act(c("wsc"), c("pq", 256, 272), AF.Identity, -1.0 - RHO)
         act(c("cht"), c("ch"), AF.Identity, L3)
-        act(c("cno"), c("ch"), AF.Identity, 256.0 - 43.23 - 63 * math.log(2.0), -1.0)
-        act(c("ivb"), c("cI"), AF.Copy)
-        act(c("cneg"), c("cI"), AF.Identity, -10240.0, 0.0)
-        act(c("c16"), c("ck"), AF.Identity, 32768.0, -4096.0)
-        act(c("k2"), c("cI"), AF.Identity, 2048.0, 0.0)
-        act(c("c77", 0, 128), c("cI"), AF.Identity, 77.0, 0.0)
-        act(c("c77", 128, 256), c("cI"), AF.Identity, 154.0, 0.0)
-        act(c("fw", 2048, 2064), c("dw", 2048, 2064), AF.Relu, BC)
-        act(c("qlm"), c("gmb"), AF.Copy, 0.0, 128.0)
-        act(c("lenm"), c("gmb"), AF.Copy, 0.0, -256.0)
-        act(c("in8"), c("ihb"), AF.Copy, 0.0, -8192.0)
-        act(c("i8"), c("ihb"), AF.Copy, 0.0, 8192.0)
-        act(c("trit"), c("tri"), AF.Copy, 0.0, 128.0)
-
-    def setup_c():
-        ts(c("stmp"), c("tri"), 256.0, None, mul)
-        tt(c("trie"), c("stmp"), c("i8"), add)
-        ts(c("cst", 0, 128), c("cI"), 2048.0, None, sub)
-        ts(c("cst", 128, 256), c("cI"), 2048.0, None, sub)
-        ts(c("cst", 256, 384), c("ck"), 256.0, 256.0, mul, add)
-        ts(c("dm", 0, 128), c("ck"), KC, None, eq)
-        ts(c("dm", 128, 256), c("ck"), KC, None, eq)
-        ts(c("wts", 0, 2), c("cI", 0, 2), W64, WX, eq, mul)
-
-    def setup_d():
-        ts(c("stmp"), c("tri"), 2.0, None, mul)
-        tt(c("stmp"), c("stmp"), c("ih"), sub)
-        ts(c("trf"), c("stmp"), 4096.0, None, mul)
-
-    def setup_f():
-        ts(c("csl", 0, 128), c("cI"), 16.0, -2048.0, mul, add)
-        ts(c("csl", 128, 256), c("cI"), 16.0, -2048.0, mul, add)
-        ts(c("csl", 256, 384), c("ck"), 256.0, 256.0, mul, add)
-        ts(c("lv"), c("cI"), 16.0, -2032.0, mul, add)
-        ts(PP, PC, 64.0, 4096.0, ge, mul)
-        ts(c("k2l"), c("cI"), 0.0, PP, mul, add)
-        ts(c("k2l"), c("k2l"), 2048.0, None, sub)
-
-    def spread(src, k0, k1):
-        for k in range(k0, k1):
-            mm(c("r%d" % (k // 4), 128 * (k % 4), 128 * (k % 4) + 128), k_("bkb", k), c(src), True, True)
-
-    def thermo(e, dst, i):
-        if e == "V":
-            ts(c(dst, 512 * i, 512 * i + 512), c("r%d" % i), BC, 0.0, add, mx)
-        else:
-            act(c(dst, 512 * i, 512 * i + 512), c("r%d" % i), AF.Relu, BC)
+        act(c("ivb"), c("cI"))
+        act(BK, KC, AF.Identity, -2048.0, 256.0)
+        even(c("k2"), BK)
+        even(k_("c77", 0), 77.0)
+        even(k_("c77", 1), 154.0)
+        for m, f in (("i8", 8192.0), ("i4k", 4096.0), ("n4k", -4096.0), ("i256", 256.0), ("i16", 16.0), ("nih", -1.0)):
+            times(c(m), c("ihb"), f)
+        times(c("gneg"), c("gmb"), -BIG)
+        for i, f in enumerate((1.0, 37.0, 1.0, 0.0, 37.0, 1.0)):
+            times(c("g3", 8 * i, 8 * i + 8), c("gc"), f)
+        act(BT, KC, AF.Identity, BIG / 2, BIG)
+        diag(c("tri"), c("gmb"), 0, gt)
+        ts(k_("dm", 0), c("ck"), KC, None, eq)
+        act(k_("dm", 1), k_("dm", 0))
+        ts(W0, W64, 0.0, WX, eq, mul)
+        ts(W1, W64, 1.0, WX, eq, mul)
+        ts(THR, PC, float(DV), 4096.0, ge, mul)
+        ts(THR, THR, 4096.5, None, sub)
+        for out, terms in (("m1", (("tri", -256.0), ("ihb", 4096.0))), ("m2", (("gmb", -256.0), ("ihb", -4096.0), ("tri", 4096.0))),
+                           ("wt", (("tri", -1.0), ("ihb", 4096.0))), ("trf", (("tri", -BIG), ("ihb", BIG / 2)))):
+            for i, (m, f) in enumerate(terms):
+                times(c("sc"), c("ihb"), f)
+                mm(k_("r3", 0), c("sc"), c(m), i == 0, i == len(terms) - 1)
+            act(k_(out, 0), k_("r3", 0))
+        act(c("wt", 128, 192), c("wt", 64, 128))
+        act(c("wt", 192, 256), c("wt", 0, 64))
+        times(k_("wt", 2), c("gmb"), -1.0)
+        act(k_("cT", 2), k_("dm", 0), AF.Identity, -16.0, 32.0)
+        act(k_("cT", 5), k_("dm", 0), AF.Identity, -16.0, 32.0)
+        iota(c("t2"), [[0, 8], [-3840, 16]], 28928 + 3840, 0)
+        select(c("cA"), c("t2"), [[0, 8], [1, 16]], gt, 0.0, 0, 0)
+        ts(c("thb"), c("cI"), 0.0, TH, mul, add)
+        mm(k_("r3", 0), c("thb"), c("ihb"), True, True)
+        cp(k_("thx", 0), k_("r3", 0))
+        cp(k_("thx", 1), k_("r3", 0))
 
     def pick(e, z, a, b, win, off):
         if e == "V":
@@ -422,49 +522,59 @@ def rank_program(g, core, T, topo):
         else:
             act(c(z, a, b), ind(win, off), AF.Relu, 256.0, -1.0)
 
-    def slots_gather(e, i):
-        pick(e, "zf", 1024 * i, 1024 * i + 1024, c("fw"), c("ql", 64 * i, 64 * i + 64))
-
-    HB = ("pa", "pq")
-
-    def slots_sum(h, fin):
-        mm(c(HB[h], 0, 128), c("ih"), c("k2l" if fin else "k2"), True, False)
-        for j in range(16):
-            mm(c(HB[h], j, 128, 16), c("zf", 2048 * h + j, 2048 * h + 2048, 16), c("ngc", 0, 8), False, j == 15)
-
-    def slots_turn(h, between=None):
-        q = c("qt", 128 * h, 128 * h + 128)
-        cp(q, c(HB[h], 0, 128))
-        mm(c(HB[h], 128, 256), q, c("ih"), True, True)
-        e = c("em", 128 * h, 128 * h + 128)
-        ts(e, c(HB[h], 128, 256), 0.0, None, eq)
-        if between:
-            between()
-        mm(c(HB[h], 256, 384), c("trf"), e, True, True)
-
-    def slots_put(h, fin):
-        a, b = 128 * h, 128 * h + 128
-        tt(c("fe", a, b), c(HB[h], 256, 384), c("npl", a, b), mx)
-        if fin:
-            tt(c("wmk", a, b), c(HB[h], 128, 256), c("fe", a, b), mi)
-            ts(c("yqs", a, b), c("wmk", a, b), 2048.0, None, add)
+    def masked(e, out, a, col):
+        if e == "V":
+            ts(out, a, col, None, mul)
         else:
-            tt(c("qi", a, b), c(HB[h], 128, 256), c("fe", a, b), mi)
-            ts(c("ql", a, b), c("qi", a, b), 2048.0, None, add)
+            times(out, a, col)
 
-    def list_queues():
-        mm(c("pq", 128, 256), c("apb"), c("ih"), True, True)
-        tt(c("ub"), ind(c("ui"), c("clist")), c("dm"), mul)
-        for b in (0, 1):
-            mm(c("pq", 64 + 8 * b, 72 + 8 * b), c("ub", 128 * b, 128 * b + 128), c("gc", 0, 8), True, True)
+    def by_slots(e, z, win, p0, p1):
+        (cp if e == "V" else act)(c(z, 16 * p0, 16 * p1), ind(c(win), c("ql", p0, p1)))
 
-    def applied():
-        cp(c("qp"), c("pq", 128, 256))
-        cp(c("ul"), c("pq", 64, 80))
+    def slots_sum(h, b, fin):
+        for j in range(16):
+            mm(c(b, 128 + j, 256, 16), c("zf", 2048 * h + j, 2048 * h + 2048, 16), c("gc"), j == 0, j == 15)
+        act(k_("qt", h), k_(b, 1))
+        name("qt")
+        mm(k_(b, 0), c("i256" if fin else "ihb"), k_("qs16" if fin else "qo", h), True, False)
+        if fin:
+            ts(k_("hfs", h), k_("qt", h), 64.0, 960.0, ge, mul)
+            mm(k_(b, 0), c("i16"), k_("hfd", h), False, False)
+            mm(k_(b, 0), k_("hfs", h), c("ihb"), False, False)
+        mm(k_(b, 0), k_("qt", h), c("ihb"), False, True)
 
-    def appended():
-        tt(c("wmk"), ind(c("qp"), c("ul")), c("ipm"), eq)
-        tt(c("npl"), ind(c("qlw"), c("ul")), c("wmk"), mul)
+    def slots_put(h, b):
+        tt(k_("qi", h), k_(b, 0), k_("np2", h), mi)
+        ts(k_("ql", h), k_("qi", h), 2048.0, None, mi)
+
+    def appended(fin):
+        mm(k_("r1", 1), c("apx"), c("i8"), True, False)
+        mm(k_("r1", 1), c("ihb"), k_("ty", fin), False, False)
+        act(c("l1"), k_("r2", 2), AF.Relu)
+        act(c("l2"), k_("r2", 2), AF.Relu, -15.0)
+        mm(k_("r1", 1), c("gmb"), c("l1"), False, False)
+        mm(k_("r1", 1), c("gneg"), c("l2"), False, True)
+        act(c("tab"), k_("r1", 1))
+        name("tab")
+        tt(c("npl"), ind(c("tab"), c("ul")), c("cs"), sub)
+        name("npl")
+        if fin:
+            act(c("cs"), c("npl"), AF.Abs)
+            ts(c("np2"), c("cs"), 2048.0, None, mi)
+        else:
+            act(c("np2"), c("npl"), AF.Abs)
+
+    def gather(i, other, a0, a1):
+        z = 2048 * i + 1024 * other
+        tt(c("mn", z + 16 * a0, z + 16 * a1), ind(c("xs"), c("hu", z // 16 + a0, z // 16 + a1)),
+           c("wg", 1024 * i + 16 * a0, 1024 * i + 16 * a1), mi)
+        (follows if z + a0 else name)("rec")
+
+    def records(i, other, b, at, stop=True):
+        z = 2048 * i + 1024 * other
+        gather(i, other, 0 if i else FIRST, 64)
+        for k in range(16):
+            mm(c(b, at, at + 64), k_("lkb", k), c("mn", z + k, z + 1024, 16), False, stop and k == 15)
 
     off = [d for d in T.cores if d != core and topo.chip(d) != topo.chip(core)]
     near = [d for d in T.cores if d != core and topo.chip(d) == topo.chip(core)]
@@ -475,92 +585,73 @@ def rank_program(g, core, T, topo):
         a = topo.addr(d)
         return DstId(rid=a[0], pnc=a[1])
 
-    def sums(b, a, z0, stop=True):
-        for k in range(16):
-            mm(c(b, a, a + 64), k_("lkb", k), c("mn", z0 + k, z0 + 1024, 16), False, stop and k == 15)
-
     for t in range(3):
         last = t == 2
         land = "land%d" % t
-        for i in (0, 1):
-            act(c("wg", 1024 * i, 1024 * i + 1024), ind(c("wn"), c("ol", 64 * i, 64 * i + 64)), AF.Copy)
+        for a, b in ((0, FIRST), (FIRST, 64), (64, 128)):
+            act(c("wg", 16 * a, 16 * b), ind(c("wn"), c("ol", a, b)))
+            if a == 64:
+                behind("emp")
+            (follows if a else name)("e")
         if t == 0:
             offsets()
-            empties()
-            cp(c("ihb"), c("ih"))
-            ts(c("stmp"), c("cI"), PC, None, gt)
-            tt(c("tri"), c("stmp"), c("gmb"), mul)
-            setup_b()
-            setup_s()
-        else:
-            for i in range(4):
-                thermo("S", "fw", i)
-            for i in range(4):
-                slots_gather("S", i)
-        mm(c("plo", 0, 128), c("ih"), c("pre"), True, False)
-        mm(c("plo", 64, 128), c("ih"), c("emp", 0, 64), False, False)
-        mm(c("phi", 0, 64), c("ih"), c("pre", 0, 64), True, False)
-
-        def records(i, other):
-            a = 2048 * i + 1024 * other
-            tt(c("mn", a, a + 1024), ind(c("xs"), c("hu", 128 * i + 64 * other, 128 * i + 64 * other + 64)),
-               c("wg", 1024 * i, 1024 * i + 1024), mi)
-            return a
-
-        sums("plo", 0, records(0, 0), False)
+            setup()
+        mm(k_("plo", 0), c("ihb"), c("pre"), True, False)
+        mm(c("plo", 64, 128), c("in8"), c("emp", 0, 64), False, False)
+        mm(c("phi", 0, 64), c("ihb"), c("pre", 0, 64), True, False)
+        mm(c("r3", 0, 64), c("in8"), c("emp", 64, 128), True, False)
+        mm(c("r3", 0, 64), c("ihb"), c("pre", 0, 64), False, False)
+        gather(0, 0, 0, FIRST)
+        gather(0, 1, 0, FIRST)
+        records(0, 0, "plo", 0, False)
+        records(0, 1, "plo", 64)
+        records(1, 0, "phi", 0)
+        records(1, 1, "r3", 0)
         if t:
-            list_queues()
-        sums("plo", 64, records(0, 1))
-        mm(c("r3", 0, 64), c("ih"), c("emp", 64, 128), True, False)
-        mm(c("r3", 0, 64), c("ih"), c("pre", 0, 64), False, False)
-        sums("phi", 0, records(1, 0))
-        if t == 1:
-            setup_f()
+            for p in (0, 64, 128):
+                by_slots("S", "zf", "fw", p, p + 64)
+                behind("tab")
+                follows("e")
+            by_slots("V", "zf", "fw", EV, 256)
+            follows("rec")
+            slots_sum(0, "pq", False)
+            links.append((mark["e"], mark["qt"], 0))
+            by_slots("S", "zf", "fw", 192, EV)
+            behind("qt")
         cp(c("ml"), c("plo", 0, 64))
+        cp(c("mh"), c("phi", 0, 64))
         tt(c("dlo"), c("plo", 64, 128), c("ml"), sub)
-        sums("r3", 0, records(1, 1))
-        if t:
-            applied()
-            appended()
-            slots_sum(0, False)
-        cp(c("sd", 64, 128), c("phi", 0, 64))
-        tt(c("dhi"), c("r3", 0, 64), c("sd", 64, 128), sub)
-        tt(c("dd"), c("dhi"), c("dlo"), add)
-        ts(c("s"), c("dd"), 0.0, None, gt)
+        tt(c("dd"), c("phi", 0, 64), c("dlo"), sub)
+        tt(c("s"), c("r3", 0, 64), c("dd"), gt)
+        behind("rec")
+        tt(c("dhi"), c("r3", 0, 64), c("mh"), sub)
         tt(c("dlo"), c("s"), c("dlo"), mul)
         tt(c("dhi"), c("s"), c("dhi"), mul)
-        tt(c("cp", 0, 64), c("ml"), c("dlo"), add)
+        tt(c("cp", 0, 64), c("plo", 0, 64), c("dlo"), add)
         tt(c("cp", 64, 128), c("phi", 0, 64), c("dhi"), add)
-        spread("cp", 0, 4)
+        cp(c("hi"), c("cp"))
+        for i in (0, 1):
+            mm(k_("r%d" % i, 0), k_("pu", 2 * i), c("cp"), True, False)
+            mm(k_("r%d" % i, 0), k_("pu", 2 * i + 1), c("hi"), False, True)
+        cp(k_("uw", 0), k_("r0", 0))
+        act(k_("uw", 1), k_("r1", 0))
+        for b in range(16):
+            masked("S" if b & 1 and b < 2 * US else "V", k_("dw", b), k_("uw", b & 1), c("R2", b // 2, b // 2 + 1))
         if t:
-            slots_turn(0, lambda: spread("cp", 4, 8))
-        else:
-            spread("cp", 4, 8)
-        spread("cp", 8, 16)
-        thermo("V", "dw", 0)
-        if t:
-            slots_put(0, False)
-        thermo("V", "dw", 2)
-        thermo("S", "dw", 1)
-        thermo("S", "dw", 3)
-        if t:
-            slots_sum(1, False)
-        mm(c("plo", 0, 256), c("on"), c("rho"), True, False)
-        for b in (0, 1):
-            mm(c("plo", 128 * b, 128 * b + 128), c("ctb", 128 * b, 128 * b + 128), c("on"), False, False)
-        for b in (0, 1):
-            m = (32, 64)[b]
-            z = 2048 * b
-            pick("V", "zd", z, z + 16 * m, c("dw"), c("ql", 128 * b, 128 * b + m))
-            pick("S", "zd", z + 16 * m, z + 2048, c("dw"), c("ql", 128 * b + m, 128 * b + 128))
-            if b == 0 and t:
-                slots_turn(1)
-                slots_put(1, False)
+            slots_sum(1, "pa", False)
+        for b, sb in enumerate(("plo", "phi")):
+            mm(k_(sb, 0), c("on"), c("rho"), True, False)
+            mm(k_(sb, 0), c("on"), c("r16"), False, False)
+            if t:
+                slots_put(b, ("pq", "pa")[b])
+            by_slots("V", "zd", "dw", 128 * b, 128 * b + CV[b])
+            by_slots("S", "zd", "dw", 128 * b + CV[b], 128 * b + 128)
             for j in range(16):
-                mm(c("plo", 128 * b + j, 128 * b + 128, 16), c("zd", z + j, z + 2048, 16), c("ngc", 0, 8), False, b == 1 and j == 15)
-        own = c(land, 16 * rank, 16 * rank + 16)
-        scan(c("tm"), c("rs"), c("plo", 0, 256), mul, mx)
-        cp(own, c("tm", 15, 256, 16))
+                mm(c(sb, j, 128, 16), c("zd", 2048 * b + j, 2048 * b + 2048, 16), c("gc"), False, j == 15)
+            scan(k_("tm", b), c("rs"), k_(sb, 0), mul, mx)
+            ts(k_("q16", b), k_(sb, 0), 2048.0 + RHO, None, sub)
+        own, best = c(land, 16 * rank, 16 * rank + 16), c("tm", 15, 256, 16)
+        ts(own, best, 0.25, None, mx)
         src = T[land][:, 16 * rank:16 * rank + 16]
         sem = T.sem["arr%d" % t]
         moves = [RemoteDMATransfer(dst_ids=[did(d) for d in off], dma_engine_mask=sum(1 << e for e in off_e), remote_sem=sem,
@@ -571,132 +662,140 @@ def rank_program(g, core, T, topo):
         run("G", lambda moves=moves: g.remote_dma_fused(moves, local_sem=T.sem.loc), [own], [], inc=0, cost=300.0)
         sent = len(ops) - 1
         arrive = len(off_e) * len(off) + len(near_e) * len(near)
-        if t == 0:
-            setup_c()
-        act(c("tsb"), c("plo", 0, 256), AF.Copy)
-        tt(c("x2", 0, 64), c("o", 64, 128), c("o", 0, 64), sub)
-        tt(c("x2", 64, 128), c("cp", 64, 128), c("cp", 0, 64), sub)
-        ts(c("qa"), c("qi"), 3975, None, OP.bitwise_and)
-        tt(c("x2", 128, 192), c("x2", 0, 64), c("s"), mul)
-        tt(c("x2", 192, 256), c("x2", 64, 128), c("s"), mul)
-        ts(c("hfs"), c("qa"), float(t + (2048 if t else 0)), None, eq)
-        tt(c("o2", 0, 64), c("o", 0, 64), c("x2", 128, 192), add)
-        tt(c("o2", 64, 128), c("o", 64, 128), c("x2", 128, 192), sub)
-        tt(c("c2", 0, 64), c("cp", 0, 64), c("x2", 192, 256), add)
-        tt(c("c2", 64, 128), c("cp", 64, 128), c("x2", 192, 256), sub)
-        cp(c("ol2"), c("o2"))
+        act(c("sb", 0, 64), c("s"))
+        for i, b in enumerate(("o", "cp")):
+            mm(k_("r1", i), c("ihb"), c(b), i == 0, False)
+            for q in (0, 1):
+                mm(c("r1", 256 + 128 * i + 64 * q, 320 + 128 * i + 64 * q), c("ihb"), c(b, 64 - 64 * q, 128 - 64 * q), False, False)
+        for q in range(8):
+            mm(c("r1", 64 * q, 64 * q + 64), c("i8" if q > 3 else "in8"), c("sb", 0, 64), False, q == 7)
+        act(c("x2"), c("r1", 256, 512), AF.Identity, -8192.0)
+        tt(c("o2c"), c("r1", 0, 256), c("x2"), mx)
+        ts(c("ol2"), c("o2"), 256.0, None, mi)
+        ts(c("qa"), c("qi"), 0x38F, None, AND)
+        ts(c("hfs"), c("qa"), 128.0 * t, None, eq)
+        ts(c("k16"), best, 2048.0 + RHO, None, sub)
+        mm(c("r3", 0, 256), c("ihb"), c("thx"), True, False)
         for b in (0, 1):
-            mm(c("phi", 128 * b, 128 * b + 128), c("hfs", 128 * b, 128 * b + 128), c("in8"), True, True)
-        mm(c("plo", 0, 128), c("ih"), c("c2"), True, False)
-        mm(c("plo", 0, 128), c("ih"), c("emp"), False, False)
-        mm(c("plo", 0, 128), c("in8"), c("hm", 128 * t, 128 * t + 128), False, False)
-        mm(c("plo", 0, 128), c("ih"), c("sc"), False, False)
-        ts(c("p16", 32, 48), own, 1.0, -100.0, lt, mul)
-        tt(c("ce", 0, 256), c("phi", 0, 256), c("tsb"), add)
-        tt(c("p16", 64, 80), own, c("p16", 32, 48), add)
-        scan(c("ce", 256, 512), c("rb"), c("ce", 0, 256), add, mi)
-        ts(c("p16", 16, 32), c("ce", 271, 512, 16), 1.0, -20000.0, lt, mul)
-        tt(c("p16", 48, 64), c("ce", 271, 512, 16), c("thc"), add)
-        tt(c("p16", 80, 96), c("p16", 48, 64), c("p16", 16, 32), add)
-        tt(c("p16", 112, 128), c("p16", 64, 80), c("p16", 80, 96), gt)
-        tt(c("p16", 128, 144), c("p16", 112, 128), c("p16", 64, 80), mul)
-        mm(c("phi", 0, 384), c("ih"), c("csl" if last else "cst"), True, False)
-        mm(c("r0", 0, 128), c("ih"), c("cneg"), True, False)
-        mm(c("r0", 0, 128), c("ih"), c("o2"), False, False)
-        if t == 0:
-            setup_d()
+            mm(k_("r3", b), k_("hfs", b), c("in8"), False, False)
+        for j in range(16):
+            mm(c("r3", j, 256, 16), c("nih"), c("k16"), False, False)
+        mm(c("r3", 0, 256), c("ihb"), c("q16"), False, True)
+        act(c("sg"), c("r3", 0, 256), AF.Sign, 2048.5)
+        for b in (0, 1):
+            mm(k_("r3", 2 + b), k_("sg", b), c("ihb"), True, True)
+        act(c("sgt"), c("r3", 256, 512))
+        for b in (0, 1):
+            mm(c("plo", 256 + 8 * b, 264 + 8 * b), k_("sgt", b), c("gc"), True, True)
+        ts(c("free"), c("plo", 256, 272), 15.0, None, lt)
+        tt(c("ak"), c("free"), best, mul)
+        mm(c("plo", 0, 256), c("ihb"), c("p8"), True, False)
+        mm(c("plo", 0, 256), c("trf"), c("sgt"), False, True)
+        act(c("cs"), c("plo", 0, 256), AF.Identity, BT)
+        tt(c("zi"), own, c("wsc"), add)
+        ts(c("ui"), c("zi"), 127, None, AND)
+        cp(c("uf"), c("ui"))
+        for i in range(16):
+            ts(k_("oh", i), c("ivb"), c("uf", i, i + 1), None, eq)
+        tt(c("ub"), ind(c("ui"), c("clist")), c("dm"), mul)
+        for b in (0, 1):
+            mm(c("pq", 64 + 8 * b, 72 + 8 * b), k_("ub", b), c("gc"), True, True)
+        cp(c("ul"), c("pq", 64, 80))
+        if last:
+            ts(c("qa"), c("qi"), 4, 3, SHR, AND)
+            cp(c("qs16"), c("qa"))
+            ts(c("qa"), c("qi"), 7, 15, SHR, AND)
+            cp(c("hfd"), c("qa"))
+        else:
+            cp(c("qo"), c("ql"))
+        mm(k_("phi", 0), c("c2"), c("ihb"), True, False)
+        mm(k_("phi", 0), c("emp"), c("in8"), False, False)
+        mm(k_("phi", 0), c("in8"), k_("hm", t), False, False)
+        mm(k_("phi", 0), c("ihb"), k_("thx", 0), False, False)
+        mm(k_("r0", 0), c("ihb"), c("k2"), True, False)
+        mm(k_("r0", 0), c("o2"), c("ihb"), False, False)
+        mm(c("r2", 0, 384), c("ihb"), c("cT", 384 * last, 384 * last + 384), True, False)
+        for q, m in enumerate(("i4k", "i4k", "n4k", "n4k")):
+            mm(c("r2", 64 * q, 64 * q + 64), c(m), c("sb", 0, 64), False, False)
+        if not last:
+            mm(c("pa", 0, 129), c("ihb"), c("cB"), True, False)
+            mm(A0, c("ihb"), c("cA"), False, False)
+            mm(R1, c("i37b"), c("cC"), False, False)
+            mm(R1, c("ihb"), k_("c77", t), False, False)
+        mm(R0, c("ihb"), c("cC"), last, False)
         tt(c("kt", 0, 64), c(land, 0, 64), c(land, 64, 128), mx)
         ops[-1] = ops[-1][:7] + (lambda sem=sem, n=arrive: g.vector.wait_ge(sem, n),)
-        trips.append((sent, len(ops) - 1))
+        links.append((sent, len(ops) - 1, 2))
         tt(c("kt", 64, 96), c("kt", 0, 32), c("kt", 32, 64), mx)
         tt(c("kp"), c("kt", 64, 80), c("kt", 80, 96), mx)
         ts(c("kb"), ind(c("kp"), c("clist")), -2048.21875, None, add)
         for b in (0, 1):
-            mm(c("pa", 128 * b, 128 * b + 128), c("kb", 128 * b, 128 * b + 128), c("ih"), True, True)
-        tt(c("zi"), c("kp"), c("wsc"), add)
-        tt(c("p16", 96, 112), c("kp"), c("p16", 128, 144), eq)
-        ts(c("ui"), c("zi"), 127, None, OP.bitwise_and)
-        ts(c("wm", 0, 256), c("pa", 0, 256), BC, 0.0, add, mx)
-        for i in (0, 1):
-            pick("V", "ze", 1024 * i, 1024 * i + 512, c("wm"), c("ol2", 64 * i, 64 * i + 32))
-            pick("S", "ze", 1024 * i + 512, 1024 * i + 1024, c("wm"), c("ol2", 64 * i + 32, 64 * i + 64))
-            for k in range(16):
-                mm(c("plo", 64 * i, 64 * i + 64), k_("lkb", k), c("ze", 1024 * i + k, 1024 * i + 1024, 16), False, i == 1 and k == 15)
-        cp(c("p16", 144, 160), c("ui"))
-        for i in range(16):
-            ts(k_("oh", i), c("ivb"), c("p16", 144 + i, 145 + i), c("p16", 96 + i, 97 + i), eq, mul)
-        ts(c("st"), c("plo", 0, 128), THR, None, ge)
-        mm(c("r0", 0, 128), c("trie"), c("st"), False, True)
-        mm(c("phi", 0, 128), c("tri" if last else "trit"), c("st"), False, False)
-        mm(c("phi", 128, 256), c("gmb" if last else "qlm"), c("st"), False, False)
-        mm(c("phi", 256, 384), c("st"), c("lenm"), False, True)
-        mm(c("plo", 0, 128), c("ih"), c("c16"), True, False)
+            mm(k_("r3", b), k_("kb", b), c("ihb"), True, True)
+        tt(c("asks"), c("kp"), c("ak"), eq)
+        ts(c("wf", 0, 32, 2), c("asks"), W0, None, mul)
+        ts(c("wf", 1, 32, 2), c("asks"), W1, None, mul)
+        name("wf")
+        act(c("wm", 0, 256), c("r3", 0, 256), AF.Relu, BC)
         for i in range(16):
             b, h = i // 8, i % 8
-            mm(c("pq", 4 * h + 2 * b, 4 * h + 2 * b + 2), k_("oh", i), c("wts", 0, 2), True, True)
+            mm(c("pq", 4 * h + 2 * b, 4 * h + 2 * b + 2), k_("oh", i), c("wf", 2 * i, 2 * i + 2), True, True)
+        pick("V", "ze", 0, 16 * DV, c("wm"), c("ol2", 0, DV))
+        behind("wf")
         act(c("lna", 0, 32), c("pq", 0, 32), AF.Ln, 2.0 ** -63)
-        cp(c("e16"), c("r0", 0, 128))
-
-        def follow():
-            tt(c("tt"), c("phi", 0, 128), c("st"), mul)
-            tt(c("x2", 0, 64), c("tt", 64, 128), c("tt", 0, 64), sub)
-            tt(c("x2", 64, 128), c("x2", 0, 64), c("s"), mul)
-            tt(c("tof", 0, 64), c("tt", 0, 64), c("x2", 64, 128), add)
-            tt(c("tof", 64, 128), c("tt", 64, 128), c("x2", 64, 128), sub)
-
-        if last:
-            follow()
-            spread("tof", 0, 16)
-        for r in range(16):
-            ts(k_("fr", r), c("e16"), 256.0 * r - 2048.0, 256.0 * r - 1792.0, mx, mi)
-            mm(c("plo", r, 128, 16), k_("fr", r), c("gc", 0, 8), False, r == 15)
-        if not last:
-            follow()
-        ts(c("lna", 32, 64), c("pq", 0, 32), 1e-14, None, lt)
-        tt(c("lna", 64, 96), c("lna", 32, 64), c("cno"), mul)
-        ts(c("corr"), c("phi", 256, 384), 256.0, None, mi)
-        tt(c("lna", 32, 64), c("lna", 64, 96), c("cht"), add)
-        tt(c("lna", 96, 128), c("lna", 32, 64), c("lna", 0, 32), sub)
-        ts(c("iseq"), c("phi", 256, 384), 256.0, None, eq)
+        name("ln")
+        pick("S", "ze", 16 * DV, 1536, c("wm"), c("ol2", DV, 96))
+        pick("S", "ze", 1536, 2048, c("wm"), c("ol2", 96, 128))
+        behind("ln")
+        for k in range(16):
+            mm(c("phi", k, 128, 16), c("ze", k, 2048, 16), c("gc"), False, k == 15)
+        ts(c("lna", 32, 64), c("pq", 0, 32), 1e-14, 200.0, lt, mul)
+        tt(c("lna", 64, 96), c("lna", 32, 64), c("cht"), add)
+        tt(c("lna", 96, 128), c("lna", 64, 96), c("lna", 0, 32), sub)
         scan(c("lna", 128, 160), c("rb4"), c("lna", 96, 128), add, mi)
+        ts(c("apf"), c("lna", 131, 160, 4), 12582912.0, 12582912.0, add, sub)
+        tt(c("apm"), ind(c("apf"), c("clist", 0, 8)), k_("dm", 0), mul)
+        act(c("apx"), ind(c("apf"), c("clist", 0, 8)))
+        mm(k_("r1", 0), c("gmb"), c("apm"), True, False)
+        ts(c("st"), k_("phi", 0), THR, None, lt)
+        mm(k_("r1", 0), c("m2"), c("st"), False, True)
+        mm(k_("r0", 0), c("m1"), c("st"), False, True)
+        mm(c("r2", 0, 384), c("st"), c("wt"), False, True)
+        act(c("e2"), k_("r1", 0), AF.Identity, 6144.0)
+        tt(c("e16"), k_("r0", 0), c("e2"), mi)
+        act(c("ym"), k_("r2", 1), AF.Identity, 4096.0)
+        tt(c("tof"), k_("r2", 0), c("ym"), mi)
+        for b in range(16):
+            masked("V" if b < TV[last] else "S", k_("fw", b), c("tof"), c("R", b, b + 1))
         if last:
-            tt(c("l16"), c("phi", 128, 256), c("lv"), lt)
-        else:
-            act(c("qlw"), c("phi", 128, 256), AF.Copy)
-        if last:
-            tt(c("qlw"), c("phi", 128, 256), c("l16"), mul)
-        ts(c("apf"), c("lna", 131, 160, 4), 12582912.0, 12583168.0, add, sub)
-        tt(c("appl"), ind(c("apf"), c("clist", 0, 8)), c("iseq"), mul)
-        tt(c("corr"), c("corr"), c("appl"), add)
-        act(c("apb"), ind(c("apf"), c("clist", 0, 8)), AF.Copy)
-        tt(c("o3t"), c("plo", 0, 128), c("corr"), add)
-        mm(c("plo", 128, 256), c("o3t"), c("ih"), True, True)
+            appended(True)
+        for i, r in enumerate((15, 0, 14, 1, 13, 2, 12, 3, 11, 4, 10, 5, 9, 6, 8, 7)):
+            ts(k_("fr", r), c("e16"), 256.0 * r - 2048.0, 256.0 * r - 1792.0, mx, mi)
+            if last:
+                mm(c("pa", 257 + r, 385, 16), k_("fr", r), c("gc"), False, i == 15)
+                continue
+            if i == 10:
+                mm(R1, c("ihb"), c("frac"), False, False)
+            mm(c("pa", 1 + r, 385, 16), k_("fr", r), c("g3", 24 * (r == 15), 24 * (r == 15) + 24), False, i == 15)
         if not last:
-            h_consts(t + 1)
-            cp(c("o"), c("plo", 128, 256))
-            cp(c("ol"), c("plo", 128, 256))
-            h_data()
-            spread("tof", 0, 16)
+            ts(c("ol"), R0, 256.0, None, mi)
             offsets()
-            empties()
-        else:
-            cp(c("yo"), c("plo", 128, 256))
-            run("Y", lambda: g.sync.dma_start(T.yoc[:, :], T.yo[:, :]), [c("yo")], [], sem="d_yo", inc=16)
-            list_queues()
-            for i in range(4):
-                thermo("VS"[i & 1], "fw", i)
-            applied()
-            appended()
-            for h in (0, 1):
-                slots_gather("V", 2 * h)
-                slots_gather("S", 2 * h + 1)
-                slots_sum(h, True)
-            for h in (0, 1):
-                slots_turn(h)
-                slots_put(h, True)
-            run("Y", lambda: g.sync.dma_start(T.yq[:, :], T.yqs[:, :]), [c("yqs")], [], sem="d_yq", inc=16)
+            persons(R0)
+            appended(False)
+    ts(c("ob"), R0, 256.0, None, mi)
+    relay("ob", "r0")
+    act(c("yo"), k_("r0", 0))
+    run("Y", lambda: g.sync.dma_start(T.yoc[:, :], T.yo[:, :]), [c("yo")], [], sem="d_yo", inc=16, cost=2000.0)
+    for h, b in enumerate(("pq", "phi")):
+        by_slots("V", "zf", "fw", 128 * h, 128 * h + FV[h])
+        behind("npl" if h else "tb")
+        by_slots("S", "zf", "fw", 128 * h + FV[h], 128 * h + 128)
+        behind("tab")
+        slots_sum(h, b, True)
+        tt(k_("yqs", h), k_(b, 0), k_("np2", h), mi)
+    run("Y", lambda: g.sync.dma_start(T.yq[:, :], T.yqs[:, :]), [c("yqs")], [], sem="d_yq", inc=16, cost=2000.0)
+
     if "order" not in PLAN:
-        PLAN["order"] = plan(ops, trips)
+        PLAN["order"] = plan(ops, links)
     for i in PLAN["order"]:
         emit(*ops[i])
     g.sync.wait_ge(T.sem.d_yo, 16)

@@ -10,20 +10,21 @@ def _sb(dtype, **names):
 
 
 SCRATCH = {}
-SCRATCH.update(_sb(BF, xs=8192, wn=272, lkb=2048, mat=3328, pm=512, pu=512, sm=160, c77=256, rho=128, dm=256, hm=384, wt=384,
+SCRATCH.update(_sb(BF, xs=8192, wn=272, lkb=2048, mat=3456, pm=512, pu=512, sm=160, c77=256, rho=128, dm=256, hm=384, wt=384,
                    cT=768, ty=256, p8=256, wg=2048, mn=4096, zd=4096, zf=4096, ze=2048, oh=2048, dw=2064, fw=2064, hfs=256,
                    hfd=256, ub=256, qs16=256, qt=256, uw=256, sg=256, sgt=256, hi=128, o=128, emp=128, st=128, tof=128, ob=128,
                    tb=128, apx=128, apm=128, l1=128, l2=128))
 SCRATCH.update(_sb(I32, oci=128, qsi=256, thi=1, cint=8, qi=256, qa=256, hz=256, hm13=256, zu=32))
-SCRATCH.update(_sb(U16, ol=128, ql=256, hu=256, ol2=128, clist=16, ul=16))
+SCRATCH.update(_sb(U16, ol=128, ql=256, hu=256, ol2=128, clist=16, two=2, ul=16))
 SCRATCH.update(_sb(H, stmp=128, stmp2=128, cB=129, frac=128, pre=128, thb=128, thx=256, q16=256, qo=256, cp=128, o2c=256, k16=16,
-                   kb=256, e16=128, fr=2048))
+                   th2=128, kb=256, e16=128, fr=2048))
 SCRATCH.update(_sb(F32, col=32, cI=128, cg=128, ck=128, n0=128, rs=128, rb4=32, ch=32, cht=32, R=16, R2=8, n8=128, sx=384, wsc=16,
                    y1=128, ym=128, tm=256, land0=128, land1=128, land2=128, x2=256, p16=64, kt=128, kp=16, wm=272, lna=160,
-                   apf=8, e2=128, tab=128, cs=256, npl=256, np2=256, yo=128, yqs=256))
+                   apf=8, akx=32, e2=128, tab=128, cs=256, npl=256, np2=256, yo=128, yqs=256))
 PSUM = ("r0", "r1", "r2", "r3", "pa", "plo", "phi", "pq")
 SCRATCH.update({n: ("psum", [128, 512], F32) for n in PSUM})
-SEMAPHORES = ["cV", "cS", "cP", "cG", "d_oc", "d_qs", "d_wn", "d_th", "d_x", "d_yo", "d_yq", "arr0", "arr1", "arr2", "loc"]
+SEMAPHORES = ["cV", "cS", "cP", "cG", "d_oc", "d_qs", "d_wn", "d_th", "d_x", "d_yo", "d_yq0", "d_yq1", "d_fw0", "d_fw1",
+              "arr0", "arr1", "arr2", "loc"]
 PART = {"pint": ("cint", 0, 1), "kint": ("cint", 1, 1), "gint": ("cint", 2, 1), "lint": ("cint", 3, 1), "hint": ("cint", 4, 1),
         "oint": ("cint", 5, 1), "dlo": ("sx", 0, 64), "dd": ("sx", 64, 64), "s": ("sx", 128, 64), "ml": ("sx", 192, 64),
         "dhi": ("sx", 256, 64), "mh": ("sx", 320, 64), "gc": ("sm", 0, 8), "wi": ("sm", 32, 8), "g3": ("sm", 48, 48),
@@ -31,13 +32,19 @@ PART = {"pint": ("cint", 0, 1), "kint": ("cint", 1, 1), "gint": ("cint", 2, 1), 
         "free": ("p16", 0, 16), "ak": ("p16", 16, 16), "uf": ("p16", 32, 16), "asks": ("p16", 48, 16)}
 PART.update({n: ("mat", 128 * i, 128) for i, n in enumerate(
     ("gmb", "ihb", "tri", "i8", "in8", "i4k", "n4k", "i37b", "i256", "i16", "gneg", "m1", "m2", "trf", "sc", "on", "ivb", "k2",
-     "cA", "cC", "sb", "r16", "nih", "t1", "t2", "hd"))})
+     "cA", "cC", "sb", "r16", "nih", "t1", "t2", "hd", "cD"))})
 FIRST = 20
-CV, DV, TV, EV, FV, US = (64, 64), 64, (8, 10), 208, (40, 56), 5
+CV, DV, TV, EV, FV, US = (64, 64), 8, 10, 232, (40, 56), 5
+DC = (("V", 0, 3), ("S", 8, 11), ("V", 3, 6), ("S", 11, 14), ("V", 6, 8), ("S", 14, 16))
 
 
-CYCLE, WAKE, TRIP, PASSES = 1.04, 70.0, 3000.0, 1500
+CYCLE, WAKE, TRIP, PASSES = 1.04, 150.0, 4700.0, 2500
+PACES = ((1.0, 120.0), (0.88, 240.0))
 PLAN = {}
+
+
+def meet(a, b):
+    return a[0] < b[1] and b[0] < a[1] and (a[2] != b[2] or (a[0] - b[0]) % a[2] == 0)
 
 
 def plan(ops, links):
@@ -46,23 +53,23 @@ def plan(ops, links):
     hist, bank = {}, {}
     for i, op in enumerate(ops):
         e = op[0]
-        regs = [(False, rg[0], rg[1], rg[2]) for rg in op[2]] + [(True, rg[0], rg[1], rg[2]) for rg in op[3]]
-        for wr, b, lo, hi in regs:
+        regs = [(False,) + rg for rg in op[2]] + [(True,) + rg for rg in op[3]]
+        for wr, b, lo, hi, st in regs:
             if b in PSUM:
                 for k, v in bank.get(b, {}).items():
                     pred[i][v] = max(pred[i].get(v, 0), int(k != e))
             else:
                 for a in hist.get(b, []):
-                    if a[1] < hi and lo < a[2] and (wr or a[0]):
+                    if (wr or a[0]) and meet((a[1], a[2], a[4]), (lo, hi, st)):
                         pred[i][a[3]] = 1
-        for wr, b, lo, hi in regs:
+        for wr, b, lo, hi, st in regs:
             if b in PSUM:
                 bank.setdefault(b, {})[e] = i
             else:
                 h = hist.setdefault(b, [])
-                if wr:
+                if wr and st == 1:
                     h[:] = [a for a in h if not (lo <= a[1] and a[2] <= hi)]
-                h.append((wr, lo, hi, i))
+                h.append((wr, lo, hi, i, st))
     dmas = [i for i in range(n) if ops[i][0] == "Y"]
     for a, b in zip(dmas, dmas[1:]):
         pred[b].setdefault(a, 0)
@@ -112,23 +119,30 @@ def plan(ops, links):
     def tried(key):
         at = lay(key, False)
         order = sorted(range(n), key=lambda q: (at[q], q))
-        free, newest, end, why = dict.fromkeys("VSPGY", 0.0), dict.fromkeys("VSPGY", -1), [0.0] * n, [-1] * n
-        for i in order:
-            e = queue[i]
-            t, why[i] = free[e], newest[e]
-            for p, k in pred[i].items():
-                if k and (k == 2 or end[p] > free[e] or newest[e] == p) and end[p] + gap[k] > t:
-                    t, why[i] = end[p] + gap[k], p
-            end[i], free[e], newest[e] = t + cost[i], t + held[i], i
-        i = max(range(n), key=lambda q: end[q])
-        total, pairs = end[i], []
-        while why[i] >= 0:
-            if why[i] not in pred[i] or pred[i][why[i]] == 1 and queue[why[i]] == queue[i]:
-                pairs.append((why[i], i))
-            i = why[i]
+        total, pairs = 0.0, []
+        for f, wake in PACES:
+            free, newest, end, why = dict.fromkeys("VSPGY", 0.0), dict.fromkeys("VSPGY", -1), [0.0] * n, [-1] * n
+            late, ready = (0.0, wake, TRIP), [0.0] * n
+            for i in order:
+                e = queue[i]
+                t, why[i] = free[e], newest[e]
+                for p, k in pred[i].items():
+                    if end[p] > ready[i]:
+                        ready[i] = end[p]
+                    if k and (k > 1 or end[p] > free[e] or newest[e] == p) and end[p] + late[k] > t:
+                        t, why[i] = end[p] + late[k], p
+                end[i], free[e], newest[e] = t + f * cost[i], t + f * held[i], i
+            i = max(range(n), key=lambda q: end[q])
+            total += end[i] / len(PACES)
+            while why[i] >= 0:
+                if why[i] not in pred[i]:
+                    pairs += [(why[i], i)] * (1 + int(min(end[why[i]] - ready[i], 1200.0) / 150.0))
+                elif pred[i][why[i]] == 1 and queue[why[i]] == queue[i]:
+                    pairs += [(why[i], i)] * 2
+                i = why[i]
         return total, order, at, pairs
 
-    seed = [1]
+    seed = [2]
 
     def draw(k):
         seed[0] = (seed[0] * 1103515245 + 12345) % 2147483648
@@ -164,7 +178,7 @@ def plan(ops, links):
             else:
                 key[u] = key[v] + 1.0 + draw(2) * draw(1500)
         new = tried(key)
-        if new[0] <= now[0] + 30.0:
+        if new[0] <= now[0] + 100.0 * (1.0 - k / PASSES):
             now = new
             if new[0] < best[0]:
                 best = new
@@ -182,7 +196,7 @@ def rank_program(g, core, T, topo):
     snap = {}
     ops = []
     links = []
-    mark = {}
+    mark, glued = {}, set()
     hist = {}
     bank = {}
 
@@ -207,6 +221,9 @@ def rank_program(g, core, T, topo):
         behind(n)
         name(n)
 
+    def block(k):
+        glued.update(range(len(ops) - k + 1, len(ops)))
+
     def emit(e, fn, reads, writes, sem, inc, cost, pre):
         evs = []
         for wr, regs in ((False, reads), (True, writes)):
@@ -215,7 +232,7 @@ def rank_program(g, core, T, topo):
                 if b in PSUM:
                     evs += [v for k, v in bank.get(b, {}).items() if k != e]
                 else:
-                    evs += [a[3] for a in hist.get(b, []) if a[1] < hi and lo < a[2] and (wr or a[0])]
+                    evs += [a[3] for a in hist.get(b, []) if (wr or a[0]) and meet((a[1], a[2], a[4]), rg[1:])]
         need = {}
         for k, v in evs:
             need[k] = max(need.get(k, 0), v)
@@ -231,7 +248,8 @@ def rank_program(g, core, T, topo):
             count[e] += 1
             ev = (sem, count[e])
         else:
-            ev = (sem, inc)
+            sem, whole = sem if isinstance(sem, tuple) else (sem, inc)
+            ev = (sem, whole)
         fn().then_inc(T.sem[sem], inc)
         snap[ev] = dict(known[e])
         for wr, regs in ((False, reads), (True, writes)):
@@ -241,11 +259,11 @@ def rank_program(g, core, T, topo):
                     bank.setdefault(b, {})[e] = ev
                 else:
                     h = hist.setdefault(b, [])
-                    if wr:
+                    if wr and rg[3] == 1:
                         h[:] = [a for a in h if not (lo <= a[1] and a[2] <= hi)]
-                    else:
-                        h[:] = [a for a in h if not (not a[0] and a[3][0] == ev[0] and a[1] == lo and a[2] == hi)]
-                    h.append((wr, lo, hi, ev))
+                    elif not wr:
+                        h[:] = [a for a in h if not (not a[0] and a[3][0] == ev[0] and (a[1], a[2], a[4]) == rg[1:])]
+                    h.append((wr, lo, hi, ev, rg[3]))
 
     def c(b, lo=None, hi=None, step=1):
         n, at, w = PART.get(b) or (b, 0, SCRATCH[b][1][1])
@@ -279,7 +297,7 @@ def rank_program(g, core, T, topo):
 
     def took(out, *ins):
         if any(x[0] == "ind" for x in ins):
-            return 50 + 1.56 * CYCLE * wide(out)
+            return 50 + 1.3 * wide(out)
         small = all(SCRATCH[x[0]][2] in (BF, H, U16) for x in (out,) + ins)
         both = len(ins) == 2 and not any(x[0] in PSUM for x in ins)
         return CYCLE * max(64, wide(out) * (2 if both else 0.5 if small and len(ins) == 1 else 1))
@@ -306,7 +324,7 @@ def rank_program(g, core, T, topo):
         run("V", lambda: g.vector.transpose(ap(out), ap(a)), [a], [out], cost=took(out, a))
 
     def act(out, a, func=AF.Copy, bias=0.0, scale=1.0):
-        cost = 65 + 1.56 * CYCLE * wide(out) if a[0] == "ind" else CYCLE * max(64, wide(out))
+        cost = 65 + 1.3 * wide(out) if a[0] == "ind" else CYCLE * max(64, wide(out))
         run("S", lambda: g.scalar.activation(ap(out), ap(a), func, bias=val(bias), scale=val(scale)), rd(a, bias, scale), [out],
             cost=cost + (1300 if func == AF.Exp else 1500 if func == AF.Ln and wide(out) == 1 else 0))
 
@@ -334,7 +352,8 @@ def rank_program(g, core, T, topo):
         select(out, a, [[1, 128]], op, other, -d, -1)
 
     def load(e, sem, b, hi, src):
-        run(e, lambda: eng[e].dma_start(T[b][:, 0:hi], src), [], [c(b, 0, hi)], sem=sem, inc=16, cost=7000.0 if b == "xs" else 1200.0)
+        run(e, lambda: eng[e].dma_start(T[b][:, 0:hi], src), [], [c(b, 0, hi)], sem=sem, inc=16,
+            cost=1200.0 if b in ("oci", "wn") else 7000.0)
 
     PC, KC, GC, BC, TH, THR, P64, W64, WX, W0, W1, L3, LN, KX, K2, EVN, ODD, BK, BT, P0, P1 = [c("col", i, i + 1) for i in range(21)]
     add, sub, mul, mx, mi, eq, ge, gt, lt = (OP.add, OP.subtract, OP.mult, OP.max, OP.min, OP.is_equal, OP.is_ge, OP.is_gt, OP.is_lt)
@@ -343,9 +362,9 @@ def rank_program(g, core, T, topo):
 
     load("Y", "d_oc", "oci", 128, T.oc[:, :])
     load("Y", "d_wn", "wn", 256, T.want[:, :])
+    load("Y", "d_x", "xs", 8192, T.x[:, :])
     load("Y", "d_qs", "qsi", 256, T.qs[:, :])
     load("Y", "d_th", "thi", 1, T.th[:, :])
-    load("Y", "d_x", "xs", 8192, T.x[:, :])
 
     iota(c("pint"), [[0, 1]], 0, 1)
     iota(c("cI"), [[1, 128]], 0, 0)
@@ -366,9 +385,10 @@ def rank_program(g, core, T, topo):
 
     fill(c("lkb", 0, 512), 0.0)
     fill(c("wn", 256, 272), 0.0)
-    fill(LN, math.exp(43.23))
+    fill(LN, math.exp(-23.67))
     fill(c("dw", 2048, 2064), -1024.0)
     fill(c("fw", 2048, 2064), 128.0)
+    iota(c("fw", 0, 2048), [[0, 2048]], 0, 0)
     fill(c("wm", 256, 272), 0.0)
     fill(c("frac"), -0.46875)
     fill(c("pre"), -2047.0)
@@ -388,7 +408,8 @@ def rank_program(g, core, T, topo):
     ts(c("R"), c("cI", 0, 16), KC, None, eq)
     ts(K2, KC, 2.0, None, mul)
     act(WX, P64, AF.Exp, 43.0, -1.0)
-    act(L3, LN, AF.Ln)
+    act(W1, LN, AF.Ln)
+    times(L3, W1, 10.0)
     times(k_("pm", 0), c("ihb"), EVN)
     times(k_("pm", 3), c("ihb"), ODD)
     even(c("t1"), EVN)
@@ -406,14 +427,16 @@ def rank_program(g, core, T, topo):
     for k in range(16):
         act(c("lkb", 128 * k + k, 128 * k + 128, 16), c("gmb", k, 128, 16))
 
-    def relay(src, b):
-        turn(c("tb"), c(src))
+    def relay(src, tb, b, s=(16, 1)):
+        turn(c(tb), c(src))
         name("tb")
         for u in range(4):
             for c2 in (0, 1):
                 for g2 in (0, 1):
-                    mm(c(b, 32 * u + 16 * c2, 32 * u + 16 * c2 + 16), k_("pm", 2 * c2 + g2), c("tb", 32 * u + 16 * g2, 32 * u + 16 * g2 + 16),
+                    a = s[0] * (2 * u + c2)
+                    mm(c(b, a, a + 15 * s[1] + 1, s[1]), k_("pm", 2 * c2 + g2), c(tb, 32 * u + 16 * g2, 32 * u + 16 * g2 + 16),
                        (u, c2, g2) == (0, 0, 0), (u, c2, g2) == (3, 1, 1))
+        block(16)
 
     A0, R1, R0 = c("pa", 0, 128), c("pa", 129, 257), c("pa", 257, 385)
 
@@ -431,7 +454,7 @@ def rank_program(g, core, T, topo):
                 cp(c("hu", a - 64, a + 64), c("hm13", a - 64, a + 64))
 
     cp(c("ob"), c("oci"))
-    relay("ob", "r0")
+    relay("ob", "tb", "r0")
     ts(c("ol"), k_("r0", 0), 256.0, None, mi)
     persons(k_("r0", 0))
     mm(c("pa", 0, 129), c("ihb"), c("cB"), True, False)
@@ -439,6 +462,7 @@ def rank_program(g, core, T, topo):
     mm(R1, c("ihb"), c("frac"), False, False)
     for u in range(8):
         mm(c("pa", 16 * u + 1, 16 * u + 16), c("ihb"), c("o", 16 * u, 16 * u + 15), False, u == 7)
+    block(8)
 
     def setup():
         ts(c("qa"), c("qsi"), 4, 15, SHR, AND)
@@ -470,7 +494,8 @@ def rank_program(g, core, T, topo):
         even(c("rho"), RHO / 128.0)
         even(c("r16"), 16.0)
         act(c("rs"), c("ck"), AF.Sign)
-        act(c("rb4"), c("ch"), AF.Relu, 1e5, -1e5)
+        act(c("cht"), c("ch"), AF.Relu, 1e5, -1e5)
+        act(c("rb4"), c("cht"), AF.Identity, -64.0)
         ts(c("clist"), c("cI", 0, 16), 0.0, None, add)
         even(c("hd"), c("R", 0, 1))
         for t in range(3):
@@ -479,7 +504,6 @@ def rank_program(g, core, T, topo):
         mm(c("pq", 256, 264), k_("wn", 0), c("wi"), True, True)
         mm(c("pq", 264, 272), k_("wn", 1), c("wi"), True, True)
         act(c("wsc"), c("pq", 256, 272), AF.Identity, -1.0 - RHO)
-        act(c("cht"), c("ch"), AF.Identity, L3)
         act(c("ivb"), c("cI"))
         act(BK, KC, AF.Identity, -2048.0, 256.0)
         even(c("k2"), BK)
@@ -494,10 +518,9 @@ def rank_program(g, core, T, topo):
         diag(c("tri"), c("gmb"), 0, gt)
         ts(k_("dm", 0), c("ck"), KC, None, eq)
         act(k_("dm", 1), k_("dm", 0))
-        ts(W0, W64, 0.0, WX, eq, mul)
-        ts(W1, W64, 1.0, WX, eq, mul)
-        ts(THR, PC, float(DV), 4096.0, ge, mul)
-        ts(THR, THR, 4096.5, None, sub)
+        ts(W0, W64, -1.0, 1.0, mul, add)
+        ts(c("two"), c("cI", 0, 16, 8), K2, None, add)
+        ts(c("cD"), c("ck"), float(DV), -4096.0, ge, mul)
         for out, terms in (("m1", (("tri", -256.0), ("ihb", 4096.0))), ("m2", (("gmb", -256.0), ("ihb", -4096.0), ("tri", 4096.0))),
                            ("wt", (("tri", -1.0), ("ihb", 4096.0))), ("trf", (("tri", -BIG), ("ihb", BIG / 2)))):
             for i, (m, f) in enumerate(terms):
@@ -528,24 +551,31 @@ def rank_program(g, core, T, topo):
         else:
             times(out, a, col)
 
+    def blocks(sem):
+        moves = [g.sync.dma_start(T.fw[b::16, 128 * b:128 * b + 128], T.tof[b::16, :]) for b in range(16)]
+        for x in moves[:15]:
+            x.then_inc(T.sem[sem], 16)
+        return moves[15]
+
     def by_slots(e, z, win, p0, p1):
         (cp if e == "V" else act)(c(z, 16 * p0, 16 * p1), ind(c(win), c("ql", p0, p1)))
 
     def slots_sum(h, b, fin):
         for j in range(16):
             mm(c(b, 128 + j, 256, 16), c("zf", 2048 * h + j, 2048 * h + 2048, 16), c("gc"), j == 0, j == 15)
-        act(k_("qt", h), k_(b, 1))
-        name("qt")
+            if j % 4 == 3:
+                block(4)
+                if h and not fin:
+                    behind("uw", "turn")
+        (cp if fin else act)(k_("qt", h), k_(b, 1))
+        if fin:
+            ts(k_("hfs", h), k_(b, 1), 64.0, 960.0, ge, mul)
         mm(k_(b, 0), c("i256" if fin else "ihb"), k_("qs16" if fin else "qo", h), True, False)
         if fin:
-            ts(k_("hfs", h), k_("qt", h), 64.0, 960.0, ge, mul)
             mm(k_(b, 0), c("i16"), k_("hfd", h), False, False)
             mm(k_(b, 0), k_("hfs", h), c("ihb"), False, False)
         mm(k_(b, 0), k_("qt", h), c("ihb"), False, True)
-
-    def slots_put(h, b):
-        tt(k_("qi", h), k_(b, 0), k_("np2", h), mi)
-        ts(k_("ql", h), k_("qi", h), 2048.0, None, mi)
+        name("turn")
 
     def appended(fin):
         mm(k_("r1", 1), c("apx"), c("i8"), True, False)
@@ -570,20 +600,33 @@ def rank_program(g, core, T, topo):
            c("wg", 1024 * i + 16 * a0, 1024 * i + 16 * a1), mi)
         (follows if z + a0 else name)("rec")
 
-    def records(i, other, b, at, stop=True):
+    def records(i, other, b, at, stop=True, fetched=False):
         z = 2048 * i + 1024 * other
-        gather(i, other, 0 if i else FIRST, 64)
+        if fetched:
+            for q in (0, 1):
+                tt(c("mn", z + 512 * q, z + 512 * q + 512), c("r%d" % q), c("zf", z + 512 * q, z + 512 * q + 512), mi)
+                follows("rec")
+        else:
+            gather(i, other, 0 if i else FIRST, 64)
         for k in range(16):
             mm(c(b, at, at + 64), k_("lkb", k), c("mn", z + k, z + 1024, 16), False, stop and k == 15)
+        block(16)
 
-    off = [d for d in T.cores if d != core and topo.chip(d) != topo.chip(core)]
+    far = [d for d in T.cores if topo.chip(d) != topo.chip(core)]
     near = [d for d in T.cores if d != core and topo.chip(d) == topo.chip(core)]
-    off_e = sorted(set(e for d in off for e in topo.engines(core, d)))
-    near_e = [e for d in near for e in topo.engines(core, d) if e not in off_e]
+    far_e = topo.engines(core, far[0])
+    near_e = [e for e in topo.engines(core, near[0]) if e not in far_e]
 
-    def did(d):
-        a = topo.addr(d)
-        return DstId(rid=a[0], pnc=a[1])
+    def send(keys, sem):
+        moves = [RemoteDMATransfer(dst_ids=[DstId(rid=topo.addr(d)[0], pnc=topo.addr(d)[1]) for d in to],
+                                   dma_engine_mask=sum(1 << e for e in engines), remote_sem=T.sem[sem],
+                                   srcs=[ap(keys)], dsts=[ap(keys) for d in to]) for to, engines in ((far, far_e), (near, near_e))]
+        run("G", lambda: g.remote_dma_fused(moves, local_sem=T.sem.loc), [keys], [], inc=0, cost=300.0)
+        return len(ops) - 1
+
+    def arrived(sent, sem):
+        ops[-1] = ops[-1][:7] + (lambda: g.vector.wait_ge(T.sem[sem], len(far_e) * len(far) + len(near_e) * len(near)),)
+        links.append((sent, len(ops) - 1, 2))
 
     for t in range(3):
         last = t == 2
@@ -605,19 +648,22 @@ def rank_program(g, core, T, topo):
         gather(0, 1, 0, FIRST)
         records(0, 0, "plo", 0, False)
         records(0, 1, "plo", 64)
-        records(1, 0, "phi", 0)
-        records(1, 1, "r3", 0)
+        if not t:
+            for q in (0, 1):
+                mm(c("r%d" % q), c("ihb"), c("wg", 1024 + 512 * q, 1536 + 512 * q), True, True)
+            for a in range(2048, 4096, 512):
+                act(c("zf", a, a + 512), ind(c("xs"), c("hu", a // 16, a // 16 + 32)))
+        records(1, 0, "phi", 0, True, not t)
+        records(1, 1, "r3", 0, True, not t)
         if t:
-            for p in (0, 64, 128):
-                by_slots("S", "zf", "fw", p, p + 64)
+            for p in (0, 64, 128, 192):
+                by_slots("S", "zf", "fw", p, min(p + 64, EV))
                 behind("tab")
                 follows("e")
             by_slots("V", "zf", "fw", EV, 256)
+            behind("npl")
             follows("rec")
             slots_sum(0, "pq", False)
-            links.append((mark["e"], mark["qt"], 0))
-            by_slots("S", "zf", "fw", 192, EV)
-            behind("qt")
         cp(c("ml"), c("plo", 0, 64))
         cp(c("mh"), c("phi", 0, 64))
         tt(c("dlo"), c("plo", 64, 128), c("ml"), sub)
@@ -627,12 +673,13 @@ def rank_program(g, core, T, topo):
         tt(c("dhi"), c("r3", 0, 64), c("mh"), sub)
         tt(c("dlo"), c("s"), c("dlo"), mul)
         tt(c("dhi"), c("s"), c("dhi"), mul)
-        tt(c("cp", 0, 64), c("plo", 0, 64), c("dlo"), add)
-        tt(c("cp", 64, 128), c("phi", 0, 64), c("dhi"), add)
-        cp(c("hi"), c("cp"))
+        for b in ("hi", "cp"):
+            tt(c(b, 0, 64), c("plo", 0, 64), c("dlo"), add)
+            tt(c(b, 64, 128), c("phi", 0, 64), c("dhi"), add)
         for i in (0, 1):
-            mm(k_("r%d" % i, 0), k_("pu", 2 * i), c("cp"), True, False)
-            mm(k_("r%d" % i, 0), k_("pu", 2 * i + 1), c("hi"), False, True)
+            mm(k_("r%d" % i, 0), k_("pu", 2 * i + 1), c("hi"), True, False)
+            mm(k_("r%d" % i, 0), k_("pu", 2 * i), c("cp"), False, True)
+            name("uw")
         cp(k_("uw", 0), k_("r0", 0))
         act(k_("uw", 1), k_("r1", 0))
         for b in range(16):
@@ -642,26 +689,32 @@ def rank_program(g, core, T, topo):
         for b, sb in enumerate(("plo", "phi")):
             mm(k_(sb, 0), c("on"), c("rho"), True, False)
             mm(k_(sb, 0), c("on"), c("r16"), False, False)
-            if t:
-                slots_put(b, ("pq", "pa")[b])
-            by_slots("V", "zd", "dw", 128 * b, 128 * b + CV[b])
+            if t and not b:
+                tt(k_("qi", 0), k_("pq", 0), k_("np2", 0), mi)
+                ts(k_("ql", 0), k_("qi", 0), 2048.0, None, mi)
+                by_slots("V", "zd", "dw", 0, CV[0] // 2)
+                name("c")
+                tt(k_("qi", 1), k_("pa", 0), k_("np2", 1), mi)
+                follows("c")
+                by_slots("V", "zd", "dw", CV[0] // 2, CV[0])
+                follows("c")
+                ts(k_("ql", 1), k_("qi", 1), 2048.0, None, mi)
+                follows("c")
+            else:
+                by_slots("V", "zd", "dw", 128 * b, 128 * b + CV[b])
             by_slots("S", "zd", "dw", 128 * b + CV[b], 128 * b + 128)
             for j in range(16):
                 mm(c(sb, j, 128, 16), c("zd", 2048 * b + j, 2048 * b + 2048, 16), c("gc"), False, j == 15)
+            block(16)
             scan(k_("tm", b), c("rs"), k_(sb, 0), mul, mx)
-            ts(k_("q16", b), k_(sb, 0), 2048.0 + RHO, None, sub)
+            if not b:
+                ts(k_("q16", 0), k_(sb, 0), 2048.0 + RHO, None, sub)
         own, best = c(land, 16 * rank, 16 * rank + 16), c("tm", 15, 256, 16)
         ts(own, best, 0.25, None, mx)
-        src = T[land][:, 16 * rank:16 * rank + 16]
-        sem = T.sem["arr%d" % t]
-        moves = [RemoteDMATransfer(dst_ids=[did(d) for d in off], dma_engine_mask=sum(1 << e for e in off_e), remote_sem=sem,
-                                   srcs=[src], dsts=[src for d in off])]
-        if near:
-            moves.append(RemoteDMATransfer(dst_ids=[did(d) for d in near], dma_engine_mask=sum(1 << e for e in near_e),
-                                           remote_sem=sem, srcs=[src], dsts=[src for d in near]))
-        run("G", lambda moves=moves: g.remote_dma_fused(moves, local_sem=T.sem.loc), [own], [], inc=0, cost=300.0)
-        sent = len(ops) - 1
-        arrive = len(off_e) * len(off) + len(near_e) * len(near)
+        name("own")
+        sent = send(own, "arr%d" % t)
+        ts(k_("q16", 1), k_("phi", 0), 2048.0 + RHO, None, sub)
+        behind("own")
         act(c("sb", 0, 64), c("s"))
         for i, b in enumerate(("o", "cp")):
             mm(k_("r1", i), c("ihb"), c(b), i == 0, False)
@@ -669,9 +722,10 @@ def rank_program(g, core, T, topo):
                 mm(c("r1", 256 + 128 * i + 64 * q, 320 + 128 * i + 64 * q), c("ihb"), c(b, 64 - 64 * q, 128 - 64 * q), False, False)
         for q in range(8):
             mm(c("r1", 64 * q, 64 * q + 64), c("i8" if q > 3 else "in8"), c("sb", 0, 64), False, q == 7)
+        block(8)
         act(c("x2"), c("r1", 256, 512), AF.Identity, -8192.0)
         tt(c("o2c"), c("r1", 0, 256), c("x2"), mx)
-        ts(c("ol2"), c("o2"), 256.0, None, mi)
+        relay("o2", "th2", "r1", (1, 8))
         ts(c("qa"), c("qi"), 0x38F, None, AND)
         ts(c("hfs"), c("qa"), 128.0 * t, None, eq)
         ts(c("k16"), best, 2048.0 + RHO, None, sub)
@@ -680,6 +734,7 @@ def rank_program(g, core, T, topo):
             mm(k_("r3", b), k_("hfs", b), c("in8"), False, False)
         for j in range(16):
             mm(c("r3", j, 256, 16), c("nih"), c("k16"), False, False)
+        block(16)
         mm(c("r3", 0, 256), c("ihb"), c("q16"), False, True)
         act(c("sg"), c("r3", 0, 256), AF.Sign, 2048.5)
         for b in (0, 1):
@@ -696,27 +751,26 @@ def rank_program(g, core, T, topo):
         ts(c("ui"), c("zi"), 127, None, AND)
         cp(c("uf"), c("ui"))
         for i in range(16):
-            ts(k_("oh", i), c("ivb"), c("uf", i, i + 1), None, eq)
+            ts(k_("oh", i), c("ivb"), c("uf", i, i + 1), WX, eq, mul)
         tt(c("ub"), ind(c("ui"), c("clist")), c("dm"), mul)
         for b in (0, 1):
             mm(c("pq", 64 + 8 * b, 72 + 8 * b), k_("ub", b), c("gc"), True, True)
-        cp(c("ul"), c("pq", 64, 80))
         if last:
             ts(c("qa"), c("qi"), 4, 3, SHR, AND)
             cp(c("qs16"), c("qa"))
             ts(c("qa"), c("qi"), 7, 15, SHR, AND)
             cp(c("hfd"), c("qa"))
-        else:
-            cp(c("qo"), c("ql"))
         mm(k_("phi", 0), c("c2"), c("ihb"), True, False)
         mm(k_("phi", 0), c("emp"), c("in8"), False, False)
         mm(k_("phi", 0), c("in8"), k_("hm", t), False, False)
         mm(k_("phi", 0), c("ihb"), k_("thx", 0), False, False)
+        mm(k_("phi", 0), c("ihb"), c("cD"), False, False)
         mm(k_("r0", 0), c("ihb"), c("k2"), True, False)
         mm(k_("r0", 0), c("o2"), c("ihb"), False, False)
         mm(c("r2", 0, 384), c("ihb"), c("cT", 384 * last, 384 * last + 384), True, False)
         for q, m in enumerate(("i4k", "i4k", "n4k", "n4k")):
             mm(c("r2", 64 * q, 64 * q + 64), c(m), c("sb", 0, 64), False, False)
+        block(4)
         if not last:
             mm(c("pa", 0, 129), c("ihb"), c("cB"), True, False)
             mm(A0, c("ihb"), c("cA"), False, False)
@@ -724,39 +778,52 @@ def rank_program(g, core, T, topo):
             mm(R1, c("ihb"), k_("c77", t), False, False)
         mm(R0, c("ihb"), c("cC"), last, False)
         tt(c("kt", 0, 64), c(land, 0, 64), c(land, 64, 128), mx)
-        ops[-1] = ops[-1][:7] + (lambda sem=sem, n=arrive: g.vector.wait_ge(sem, n),)
-        links.append((sent, len(ops) - 1, 2))
+        arrived(sent, "arr%d" % t)
+        name("max")
+        ts(c("ol2"), k_("r1", 0), 256.0, None, mi)
+        follows("max")
         tt(c("kt", 64, 96), c("kt", 0, 32), c("kt", 32, 64), mx)
+        follows("max")
+        ts(c("akx", 0, 32, 2), c("ak"), W0, None, mul)
+        follows("max")
+        ts(c("akx", 1, 32, 2), c("ak"), W64, None, mul)
+        follows("max")
         tt(c("kp"), c("kt", 64, 80), c("kt", 80, 96), mx)
-        ts(c("kb"), ind(c("kp"), c("clist")), -2048.21875, None, add)
-        for b in (0, 1):
-            mm(k_("r3", b), k_("kb", b), c("ihb"), True, True)
-        tt(c("asks"), c("kp"), c("ak"), eq)
-        ts(c("wf", 0, 32, 2), c("asks"), W0, None, mul)
-        ts(c("wf", 1, 32, 2), c("asks"), W1, None, mul)
+        follows("max")
+        cp(c("ul"), c("pq", 64, 80))
+        follows("max")
+        if not last:
+            cp(c("qo"), c("ql"))
+            follows("max")
+        tt(c("wf"), ind(c("kp"), c("two")), c("akx"), eq)
         name("wf")
-        act(c("wm", 0, 256), c("r3", 0, 256), AF.Relu, BC)
+        for b in (0, 1):
+            ts(k_("kb", b), ind(c("kp"), c("clist", 8 * b, 8 * b + 8)), -2048.21875, None, add)
+            behind("max")
+            mm(k_(("r3", "r1")[b], 0), k_("kb", b), c("ihb"), True, True)
+        act(k_("wm", 0), k_("r3", 0), AF.Relu, BC)
+        ts(k_("wm", 1), k_("r1", 0), BC, 0.0, add, mx)
         for i in range(16):
             b, h = i // 8, i % 8
             mm(c("pq", 4 * h + 2 * b, 4 * h + 2 * b + 2), k_("oh", i), c("wf", 2 * i, 2 * i + 2), True, True)
-        pick("V", "ze", 0, 16 * DV, c("wm"), c("ol2", 0, DV))
-        behind("wf")
-        act(c("lna", 0, 32), c("pq", 0, 32), AF.Ln, 2.0 ** -63)
+            if h == 7:
+                block(8)
+        act(c("lna", 0, 32), c("pq", 0, 32), AF.Ln, 2.0 ** -63, math.exp(-0.23))
+        act(c("lna", 32, 64), c("lna", 0, 32), AF.Relu, L3, -10.0)
         name("ln")
-        pick("S", "ze", 16 * DV, 1536, c("wm"), c("ol2", DV, 96))
-        pick("S", "ze", 1536, 2048, c("wm"), c("ol2", 96, 128))
-        behind("ln")
-        for k in range(16):
-            mm(c("phi", k, 128, 16), c("ze", k, 2048, 16), c("gc"), False, k == 15)
-        ts(c("lna", 32, 64), c("pq", 0, 32), 1e-14, 200.0, lt, mul)
-        tt(c("lna", 64, 96), c("lna", 32, 64), c("cht"), add)
-        tt(c("lna", 96, 128), c("lna", 64, 96), c("lna", 0, 32), sub)
+        for e, a, b in DC:
+            pick(e, "ze", 128 * a, 128 * b, c("wm"), c("ol2", 8 * a, 8 * b))
+            behind(*(["wf"] if e == "V" else ["ln"] if b == 16 else []))
+            for k in range(a, b):
+                mm(c("phi", k, 128, 16), k_("ze", k), c("gc"), False, k == 15)
+            block(b - a)
+        tt(c("lna", 96, 128), c("lna", 32, 64), c("lna", 0, 32), sub)
         scan(c("lna", 128, 160), c("rb4"), c("lna", 96, 128), add, mi)
-        ts(c("apf"), c("lna", 131, 160, 4), 12582912.0, 12582912.0, add, sub)
+        ts(c("apf"), c("lna", 131, 160, 4), 12582912.0 + 235.0, 12582912.0, add, sub)
         tt(c("apm"), ind(c("apf"), c("clist", 0, 8)), k_("dm", 0), mul)
         act(c("apx"), ind(c("apf"), c("clist", 0, 8)))
         mm(k_("r1", 0), c("gmb"), c("apm"), True, False)
-        ts(c("st"), k_("phi", 0), THR, None, lt)
+        ts(c("st"), k_("phi", 0), -4096.5, None, lt)
         mm(k_("r1", 0), c("m2"), c("st"), False, True)
         mm(k_("r0", 0), c("m1"), c("st"), False, True)
         mm(c("r2", 0, 384), c("st"), c("wt"), False, True)
@@ -764,10 +831,12 @@ def rank_program(g, core, T, topo):
         tt(c("e16"), k_("r0", 0), c("e2"), mi)
         act(c("ym"), k_("r2", 1), AF.Identity, 4096.0)
         tt(c("tof"), k_("r2", 0), c("ym"), mi)
-        for b in range(16):
-            masked("V" if b < TV[last] else "S", k_("fw", b), c("tof"), c("R", b, b + 1))
         if last:
+            for b in range(16):
+                masked("V" if b < TV else "S", k_("fw", b), c("tof"), c("R", b, b + 1))
             appended(True)
+        else:
+            run("Y", lambda t=t: blocks("d_fw%d" % t), [c("tof")], [c("fw", 0, 2048)], sem=("d_fw%d" % t, 256), inc=16, cost=3200.0)
         for i, r in enumerate((15, 0, 14, 1, 13, 2, 12, 3, 11, 4, 10, 5, 9, 6, 8, 7)):
             ts(k_("fr", r), c("e16"), 256.0 * r - 2048.0, 256.0 * r - 1792.0, mx, mi)
             if last:
@@ -782,7 +851,7 @@ def rank_program(g, core, T, topo):
             persons(R0)
             appended(False)
     ts(c("ob"), R0, 256.0, None, mi)
-    relay("ob", "r0")
+    relay("ob", "tb", "r0")
     act(c("yo"), k_("r0", 0))
     run("Y", lambda: g.sync.dma_start(T.yoc[:, :], T.yo[:, :]), [c("yo")], [], sem="d_yo", inc=16, cost=2000.0)
     for h, b in enumerate(("pq", "phi")):
@@ -792,14 +861,21 @@ def rank_program(g, core, T, topo):
         behind("tab")
         slots_sum(h, b, True)
         tt(k_("yqs", h), k_(b, 0), k_("np2", h), mi)
-    run("Y", lambda: g.sync.dma_start(T.yq[:, :], T.yqs[:, :]), [c("yqs")], [], sem="d_yq", inc=16, cost=2000.0)
+        run("Y", lambda h=h: g.sync.dma_start(T.yq[:, 128 * h:128 * h + 128], ap(k_("yqs", h))), [k_("yqs", h)], [],
+            sem="d_yq%d" % h, inc=16, cost=2000.0)
 
     if "order" not in PLAN:
-        PLAN["order"] = plan(ops, links)
+        first = [i for i in range(len(ops)) if i not in glued] + [len(ops)]
+        piece = [k for k in range(len(first) - 1) for _ in range(first[k], first[k + 1])]
+        whole = [(ops[a][0], None, sum((op[2] for op in ops[a:b]), []), sum((op[3] for op in ops[a:b]), []), None, 1,
+                  sum(op[6] for op in ops[a:b])) for a, b in zip(first, first[1:])]
+        order = plan(whole, [(piece[a], piece[b], k) for a, b, k in links])
+        PLAN["order"] = [i for k in order for i in range(first[k], first[k + 1])]
     for i in PLAN["order"]:
         emit(*ops[i])
     g.sync.wait_ge(T.sem.d_yo, 16)
-    g.sync.wait_ge(T.sem.d_yq, 16)
+    g.sync.wait_ge(T.sem.d_yq0, 16)
+    g.sync.wait_ge(T.sem.d_yq1, 16)
     for e in ("V", "S", "P", "G"):
         g.wait_ge(T.sem["c" + e], count[e])
-    g.wait_ge(T.sem.loc, 3 * (len(off_e) + (len(near_e) if near else 0)))
+    g.wait_ge(T.sem.loc, 3 * (len(far_e) + len(near_e)))

@@ -13,12 +13,12 @@ SCRATCH = {}
 SCRATCH.update(_sb(BF, xs=8192, wn=272, lkb=2048, mat=3456, pm=512, pu=512, sm=160, c77=256, rho=128, dm=256, hm=384, wt=384,
                    cT=768, ty=256, p8=256, wg=2048, mn=4096, zd=4096, zf=4096, ze=2048, oh=2048, dw=2064, fw=2064, hfs=256,
                    hfd=256, ub=256, qs16=256, qt=256, uw=256, sg=256, sgt=256, hi=128, o=128, emp=128, st=128, tof=128, ob=128,
-                   tb=128, apx=128, apm=128, l1=128, l2=128))
+                   tb=128, apx=128, apm=128, l1=128, l2=128, Rb=24, uf=17))
 SCRATCH.update(_sb(I32, oci=128, qsi=256, thi=1, cint=8, qi=256, qa=256, hz=256, hm13=256, zu=32))
 SCRATCH.update(_sb(U16, ol=128, ql=256, hu=256, ol2=128, clist=16, two=2, ul=16))
 SCRATCH.update(_sb(H, stmp=128, stmp2=128, cB=129, frac=128, pre=128, thb=128, thx=256, q16=256, qo=256, cp=128, o2c=256, k16=16,
                    th2=128, kb=256, e16=128, fr=2048))
-SCRATCH.update(_sb(F32, col=32, cI=128, cg=128, ck=128, n0=128, rs=128, rb4=32, ch=32, cht=32, R=16, R2=8, n8=128, sx=384, wsc=16,
+SCRATCH.update(_sb(F32, col=32, cI=128, cg=128, ck=128, n0=128, rs=128, rb4=32, ch=32, cht=32, R=24, n8=128, sx=384, wsc=16,
                    y1=128, ym=128, tm=256, land0=128, land1=128, land2=128, x2=256, p16=64, kt=128, kp=16, wm=272, lna=160,
                    apf=8, akx=32, e2=128, tab=128, cs=256, npl=256, np2=256, yo=128, yqs=256))
 PSUM = ("r0", "r1", "r2", "r3", "pa", "plo", "phi", "pq")
@@ -29,7 +29,7 @@ PART = {"pint": ("cint", 0, 1), "kint": ("cint", 1, 1), "gint": ("cint", 2, 1), 
         "oint": ("cint", 5, 1), "dlo": ("sx", 0, 64), "dd": ("sx", 64, 64), "s": ("sx", 128, 64), "ml": ("sx", 192, 64),
         "dhi": ("sx", 256, 64), "mh": ("sx", 320, 64), "gc": ("sm", 0, 8), "wi": ("sm", 32, 8), "g3": ("sm", 48, 48),
         "wf": ("sm", 96, 32), "o2": ("o2c", 0, 128), "c2": ("o2c", 128, 128), "zi": ("zu", 0, 16), "ui": ("zu", 16, 16),
-        "free": ("p16", 0, 16), "ak": ("p16", 16, 16), "uf": ("p16", 32, 16), "asks": ("p16", 48, 16)}
+        "free": ("p16", 0, 16), "ak": ("p16", 16, 16), "R2": ("R", 16, 8)}
 PART.update({n: ("mat", 128 * i, 128) for i, n in enumerate(
     ("gmb", "ihb", "tri", "i8", "in8", "i4k", "n4k", "i37b", "i256", "i16", "gneg", "m1", "m2", "trf", "sc", "on", "ivb", "k2",
      "cA", "cC", "sb", "r16", "nih", "t1", "t2", "hd", "cD"))})
@@ -38,8 +38,8 @@ CV, DV, TV, EV, FV, US = (64, 64), 8, 10, 232, (40, 56), 5
 DC = (("V", 0, 3), ("S", 8, 11), ("V", 3, 6), ("S", 11, 14), ("V", 6, 8), ("S", 14, 16))
 
 
-CYCLE, WAKE, TRIP, PASSES = 1.04, 150.0, 4700.0, 2500
-PACES = ((1.0, 120.0), (0.88, 240.0))
+CYCLE, WAKE, TRIP, PASSES = 1.04, 150.0, 4700.0, 3600
+PACES = ((1.0, 100.0), (0.88, 210.0))
 PLAN = {}
 
 
@@ -65,6 +65,8 @@ def plan(ops, links):
         for wr, b, lo, hi, st in regs:
             if b in PSUM:
                 bank.setdefault(b, {})[e] = i
+                if wr and e != "P":
+                    bank[b]["wrote"] = i
             else:
                 h = hist.setdefault(b, [])
                 if wr and st == 1:
@@ -257,6 +259,8 @@ def rank_program(g, core, T, topo):
                 b, lo, hi = rg[0], rg[1], rg[2]
                 if b in PSUM:
                     bank.setdefault(b, {})[e] = ev
+                    if wr and e != "P":
+                        bank[b]["wrote"] = ev
                 else:
                     h = hist.setdefault(b, [])
                     if wr and rg[3] == 1:
@@ -295,18 +299,20 @@ def rank_program(g, core, T, topo):
     def wide(x):
         return 16 * (x[2][2] - x[2][1]) if x[0] == "ind" else -(-(x[2] - x[1]) // x[3])
 
-    def took(out, *ins):
+    def took(out, *ins, cols=()):
         if any(x[0] == "ind" for x in ins):
             return 50 + 1.3 * wide(out)
-        small = all(SCRATCH[x[0]][2] in (BF, H, U16) for x in (out,) + ins)
+        small = all(SCRATCH[x[0]][2] in (BF, H, U16) for x in [out, *ins, *cols])
         both = len(ins) == 2 and not any(x[0] in PSUM for x in ins)
         return CYCLE * max(64, wide(out) * (2 if both else 0.5 if small and len(ins) == 1 else 1))
 
     def ts(out, a, s1, s2, o0, o1=None):
         if o1 is None:
-            run("V", lambda: g.vector.tensor_scalar(ap(out), ap(a), val(s1), None, o0), rd(a, s1), [out], cost=took(out, a))
+            run("V", lambda: g.vector.tensor_scalar(ap(out), ap(a), val(s1), None, o0), rd(a, s1), [out],
+                cost=took(out, a, cols=rd(s1)))
         else:
-            run("V", lambda: g.vector.tensor_scalar(ap(out), ap(a), val(s1), val(s2), o0, o1), rd(a, s1, s2), [out], cost=took(out, a))
+            run("V", lambda: g.vector.tensor_scalar(ap(out), ap(a), val(s1), val(s2), o0, o1), rd(a, s1, s2), [out],
+                cost=took(out, a, cols=rd(s1, s2)))
 
     def tt(out, a, b, op):
         run("V", lambda: g.vector.tensor_tensor(ap(out), ap(a), ap(b), op), rd(a, b), [out], cost=took(out, a, b))
@@ -405,7 +411,7 @@ def rank_program(g, core, T, topo):
     ts(EVN, ODD, -1.0, 1.0, mul, add)
     ts(c("gmb"), c("cg"), GC, None, eq)
     ts(c("ihb"), c("cI"), PC, None, eq)
-    ts(c("R"), c("cI", 0, 16), KC, None, eq)
+    ts(c("R", 0, 16), c("cI", 0, 16), KC, None, eq)
     ts(K2, KC, 2.0, None, mul)
     act(WX, P64, AF.Exp, 43.0, -1.0)
     act(W1, LN, AF.Ln)
@@ -438,6 +444,7 @@ def rank_program(g, core, T, topo):
                        (u, c2, g2) == (0, 0, 0), (u, c2, g2) == (3, 1, 1))
         block(16)
 
+    swap = c("r2", 448, 512)
     A0, R1, R0 = c("pa", 0, 128), c("pa", 129, 257), c("pa", 257, 385)
 
     def persons(src):
@@ -447,11 +454,12 @@ def rank_program(g, core, T, topo):
 
     def offsets():
         tt(c("y1"), A0, c("n8"), mul)
-        for a, y, p in ((0, 0, 0), (64, 64, 0), (128, 64, 64), (192, 0, 64)):
-            tt(c("hz", a, a + 64), c("y1", y, y + 64), c("pa", 129 + p, 193 + p), add)
-            if a & 64:
-                ts(c("hm13", a - 64, a + 64), c("hz", a - 64, a + 64), 8191, None, AND)
-                cp(c("hu", a - 64, a + 64), c("hm13", a - 64, a + 64))
+        tt(k_("hz", 0), c("y1"), R1, add)
+        for p in (0, 64):
+            tt(c("hz", 128 + p, 192 + p), c("y1", 64 - p, 128 - p), c("pa", 129 + p, 193 + p), add)
+        for b in (0, 1):
+            ts(k_("hm13", b), k_("hz", b), 8191, None, AND)
+            cp(k_("hu", b), k_("hm13", b))
 
     cp(c("ob"), c("oci"))
     relay("ob", "tb", "r0")
@@ -484,6 +492,8 @@ def rank_program(g, core, T, topo):
         ts(c("lint"), c("pint"), 1, 7, SHR, AND)
         cp(K2, c("lint"))
         ts(c("R2"), c("cI", 0, 8), K2, None, eq)
+        act(c("Rb"), c("R"))
+        act(c("uf", 16, 17), WX)
         for i, par in enumerate((P0, P1)):
             even(c("t1"), par)
             diag(k_("pu", 2 * i), c("t1"), 1 - 2 * i)
@@ -547,7 +557,7 @@ def rank_program(g, core, T, topo):
 
     def masked(e, out, a, col):
         if e == "V":
-            ts(out, a, col, None, mul)
+            ts(out, a, ("Rb",) + col[1:], None, mul)
         else:
             times(out, a, col)
 
@@ -596,7 +606,8 @@ def rank_program(g, core, T, topo):
 
     def gather(i, other, a0, a1):
         z = 2048 * i + 1024 * other
-        tt(c("mn", z + 16 * a0, z + 16 * a1), ind(c("xs"), c("hu", z // 16 + a0, z // 16 + a1)),
+        u = 128 * other + 64 * i
+        tt(c("mn", z + 16 * a0, z + 16 * a1), ind(c("xs"), c("hu", u + a0, u + a1)),
            c("wg", 1024 * i + 16 * a0, 1024 * i + 16 * a1), mi)
         (follows if z + a0 else name)("rec")
 
@@ -651,8 +662,8 @@ def rank_program(g, core, T, topo):
         if not t:
             for q in (0, 1):
                 mm(c("r%d" % q), c("ihb"), c("wg", 1024 + 512 * q, 1536 + 512 * q), True, True)
-            for a in range(2048, 4096, 512):
-                act(c("zf", a, a + 512), ind(c("xs"), c("hu", a // 16, a // 16 + 32)))
+            for q, a in enumerate((64, 96, 192, 224)):
+                act(c("zf", 2048 + 512 * q, 2560 + 512 * q), ind(c("xs"), c("hu", a, a + 32)))
         records(1, 0, "phi", 0, True, not t)
         records(1, 1, "r3", 0, True, not t)
         if t:
@@ -668,11 +679,11 @@ def rank_program(g, core, T, topo):
         cp(c("mh"), c("phi", 0, 64))
         tt(c("dlo"), c("plo", 64, 128), c("ml"), sub)
         tt(c("dd"), c("phi", 0, 64), c("dlo"), sub)
-        tt(c("s"), c("r3", 0, 64), c("dd"), gt)
+        tt(swap, c("r3", 0, 64), c("dd"), gt)
         behind("rec")
         tt(c("dhi"), c("r3", 0, 64), c("mh"), sub)
-        tt(c("dlo"), c("s"), c("dlo"), mul)
-        tt(c("dhi"), c("s"), c("dhi"), mul)
+        tt(c("dlo"), swap, c("dlo"), mul)
+        tt(c("dhi"), swap, c("dhi"), mul)
         for b in ("hi", "cp"):
             tt(c(b, 0, 64), c("plo", 0, 64), c("dlo"), add)
             tt(c(b, 64, 128), c("phi", 0, 64), c("dhi"), add)
@@ -715,7 +726,7 @@ def rank_program(g, core, T, topo):
         sent = send(own, "arr%d" % t)
         ts(k_("q16", 1), k_("phi", 0), 2048.0 + RHO, None, sub)
         behind("own")
-        act(c("sb", 0, 64), c("s"))
+        act(c("sb", 0, 64), swap)
         for i, b in enumerate(("o", "cp")):
             mm(k_("r1", i), c("ihb"), c(b), i == 0, False)
             for q in (0, 1):
@@ -749,9 +760,9 @@ def rank_program(g, core, T, topo):
         act(c("cs"), c("plo", 0, 256), AF.Identity, BT)
         tt(c("zi"), own, c("wsc"), add)
         ts(c("ui"), c("zi"), 127, None, AND)
-        cp(c("uf"), c("ui"))
+        cp(c("uf", 0, 16), c("ui"))
         for i in range(16):
-            ts(k_("oh", i), c("ivb"), c("uf", i, i + 1), WX, eq, mul)
+            ts(k_("oh", i), c("ivb"), c("uf", i, i + 1), c("uf", 16, 17), eq, mul)
         tt(c("ub"), ind(c("ui"), c("clist")), c("dm"), mul)
         for b in (0, 1):
             mm(c("pq", 64 + 8 * b, 72 + 8 * b), k_("ub", b), c("gc"), True, True)
@@ -794,7 +805,6 @@ def rank_program(g, core, T, topo):
         follows("max")
         if not last:
             cp(c("qo"), c("ql"))
-            follows("max")
         tt(c("wf"), ind(c("kp"), c("two")), c("akx"), eq)
         name("wf")
         for b in (0, 1):

import math
from concourse.bass import DstId, RemoteDMATransfer
from concourse.mybir import AluOpType as OP, ActivationFunctionType as AF

F32, BF, H, I32, U16 = "float32", "bfloat16", "float16", "int32", "uint16"


def _sb(dtype, **names):
    return {n: ("sbuf", [128, w], dtype) for n, w in names.items()}


SCRATCH = {}
SCRATCH.update(_sb(BF, xs=8192, wn=272, lkb=2048, mat=3456, pm=512, pu=512, sm=160, c77=256, rho=128, dm=256, hm=384, wt=384,
                   cT=768, ty=256, p8=256, wg=2048, mn=4096, zd=4096, zf=4096, ze=2048, oh=2048, dw=2064, fw=2064, hfs=256,
                   hfd=256, ub=256, qs16=256, qt=256, uw=256, sg=256, sgt=256, hi=128, o=128, emp=128, st=128, tof=128, ob=128,
                   tb=128, apx=128, apm=128, l1=128, l2=128, Rb=24, uf=17))
SCRATCH.update(_sb(I32, oci=128, qsi=256, thi=1, cint=8, qi=256, qa=256, hz=256, hm13=256, zu=32))
SCRATCH.update(_sb(U16, ol=128, ql=256, hu=256, ol2=128, clist=16, two=2, ul=16))
SCRATCH.update(_sb(H, stmp=128, stmp2=128, cB=129, frac=128, pre=128, thb=128, thx=256, q16=256, qo=256, cp=128, o2c=256, k16=16,
                   th2=128, kb=256, e16=128, fr=2048))
SCRATCH.update(_sb(F32, col=32, cI=128, cg=128, ck=128, n0=128, rs=128, rb4=32, ch=32, cht=32, R=24, n8=128, sx=384, wsc=16,
                   y1=128, ym=128, tm=256, land0=128, land1=128, land2=128, x2=256, p16=64, kt=128, kp=16, wm=272, lna=160,
                   apf=8, akx=32, e2=128, tab=128, cs=256, npl=256, np2=256, yo=128, yqs=256))
PSUM = ("r0", "r1", "r2", "r3", "pa", "plo", "phi", "pq")
SCRATCH.update({n: ("psum", [128, 512], F32) for n in PSUM})
SEMAPHORES = ["cV", "cS", "cP", "cG", "d_oc", "d_qs", "d_wn", "d_th", "d_x", "d_yo", "d_yq0", "d_yq1", "d_fw0", "d_fw1",
              "arr0", "arr1", "arr2", "loc"]
PART = {"pint": ("cint", 0, 1), "kint": ("cint", 1, 1), "gint": ("cint", 2, 1), "lint": ("cint", 3, 1), "hint": ("cint", 4, 1),
        "oint": ("cint", 5, 1), "dlo": ("sx", 0, 64), "dd": ("sx", 64, 64), "s": ("sx", 128, 64), "ml": ("sx", 192, 64),
        "dhi": ("sx", 256, 64), "mh": ("sx", 320, 64), "gc": ("sm", 0, 8), "wi": ("sm", 32, 8), "g3": ("sm", 48, 48),
        "wf": ("sm", 96, 32), "o2": ("o2c", 0, 128), "c2": ("o2c", 128, 128), "zi": ("zu", 0, 16), "ui": ("zu", 16, 16),
        "free": ("p16", 0, 16), "ak": ("p16", 16, 16), "R2": ("R", 16, 8)}
PART.update({n: ("mat", 128 * i, 128) for i, n in enumerate(
    ("gmb", "ihb", "tri", "i8", "in8", "i4k", "n4k", "i37b", "i256", "i16", "gneg", "m1", "m2", "trf", "sc", "on", "ivb", "k2",
     "cA", "cC", "sb", "r16", "nih", "t1", "t2", "hd", "cD"))})
FIRST = 20
CV, DV, TV, EV, FV, US = (64, 64), 8, 10, 232, (40, 56), 5
DC = (("V", 0, 3), ("S", 8, 11), ("V", 3, 6), ("S", 11, 14), ("V", 6, 8), ("S", 14, 16))


CYCLE, WAKE, TRIP, PASSES = 1.04, 150.0, 4700.0, 3600
PACES = ((1.0, 100.0), (0.88, 210.0))
PLAN = {}


def meet(a, b):
    return a[0] < b[1] and b[0] < a[1] and (a[2] != b[2] or (a[0] - b[0]) % a[2] == 0)


def plan(ops, links):
    n = len(ops)
    pred = [dict() for _ in range(n)]
    hist, bank = {}, {}
    for i, op in enumerate(ops):
        e = op[0]
        regs = [(False,) + rg for rg in op[2]] + [(True,) + rg for rg in op[3]]
        for wr, b, lo, hi, st in regs:
            if b in PSUM:
                for k, v in bank.get(b, {}).items():
                    pred[i][v] = max(pred[i].get(v, 0), int(k != e))
            else:
                for a in hist.get(b, []):
                    if (wr or a[0]) and meet((a[1], a[2], a[4]), (lo, hi, st)):
                        pred[i][a[3]] = 1
        for wr, b, lo, hi, st in regs:
            if b in PSUM:
                bank.setdefault(b, {})[e] = i
                if wr and e != "P":
                    bank[b]["wrote"] = i
            else:
                h = hist.setdefault(b, [])
                if wr and st == 1:
                    h[:] = [a for a in h if not (lo <= a[1] and a[2] <= hi)]
                h.append((wr, lo, hi, i, st))
    dmas = [i for i in range(n) if ops[i][0] == "Y"]
    for a, b in zip(dmas, dmas[1:]):
        pred[b].setdefault(a, 0)
    for a, b, k in links:
        pred[b][a] = max(k, pred[b].get(a, 0))
    queue = [op[0] for op in ops]
    cost = [op[6] for op in ops]
    held = [70.0 if op[0] == "Y" else op[6] for op in ops]
    gap = (0.0, WAKE, TRIP)
    before = [[(p, (held if k == 0 else cost)[p] + gap[k]) for p, k in pred[i].items()] for i in range(n)]
    after = [[] for _ in range(n)]
    for i in range(n):
        for p, d in before[i]:
            after[p].append((i, d))

    def lay(key, back):
        near = after if back else before
        key, at = list(key), [0.0] * n
        for i in (range(n - 1, -1, -1) if back else range(n)):
            for p, d in near[i]:
                if key[p] >= key[i]:
                    key[i] = key[p] + 1e-3
        busy = {e: ([], []) for e in "VSPGY"}
        for i in sorted(range(n), key=lambda q: key[q]):
            h = held[i]
            t = cost[i] - h if back else 0.0
            for p, d in near[i]:
                x = at[p] + d - h if back else at[p] + d
                if x > t:
                    t = x
            starts, ends = busy[queue[i]]
            lo, hi = 0, len(ends)
            while lo < hi:
                mid = (lo + hi) // 2
                if ends[mid] <= t:
                    lo = mid + 1
                else:
                    hi = mid
            while lo < len(ends) and starts[lo] < t + h - 1e-6:
                t = ends[lo]
                lo += 1
            starts.insert(lo, t)
            ends.insert(lo, t + h)
            at[i] = t + h if back else t
        return at

    def tried(key):
        at = lay(key, False)
        order = sorted(range(n), key=lambda q: (at[q], q))
        total, pairs = 0.0, []
        for f, wake in PACES:
            free, newest, end, why = dict.fromkeys("VSPGY", 0.0), dict.fromkeys("VSPGY", -1), [0.0] * n, [-1] * n
            late, ready = (0.0, wake, TRIP), [0.0] * n
            for i in order:
                e = queue[i]
                t, why[i] = free[e], newest[e]
                for p, k in pred[i].items():
                    if end[p] > ready[i]:
                        ready[i] = end[p]
                    if k and (k > 1 or end[p] > free[e] or newest[e] == p) and end[p] + late[k] > t:
                        t, why[i] = end[p] + late[k], p
                end[i], free[e], newest[e] = t + f * cost[i], t + f * held[i], i
            i = max(range(n), key=lambda q: end[q])
            total += end[i] / len(PACES)
            while why[i] >= 0:
                if why[i] not in pred[i]:
                    pairs += [(why[i], i)] * (1 + int(min(end[why[i]] - ready[i], 1200.0) / 150.0))
                elif pred[i][why[i]] == 1 and queue[why[i]] == queue[i]:
                    pairs += [(why[i], i)] * 2
                i = why[i]
        return total, order, at, pairs

    seed = [2]

    def draw(k):
        seed[0] = (seed[0] * 1103515245 + 12345) % 2147483648
        return seed[0] * k // 2147483648

    def sooner(key, i, k):
        todo = {i}
        key[i] = k
        while todo:
            j = max(todo)
            todo.remove(j)
            for p in pred[j]:
                if key[p] >= key[j]:
                    key[p] = key[j] - 1e-3
                    todo.add(p)

    way = [0.0] * n
    for i in range(n - 1, -1, -1):
        way[i] = max([way[j] + d for j, d in after[i]] + [cost[i]])
    best = now = tried([-w for w in way])
    for k in range(PASSES):
        key = list(now[2])
        if k % 16 == 0:
            key = [-a for a in lay([-(key[i] + cost[i]) for i in range(n)], True)]
        for _ in range(1 + draw(2)):
            u, v = now[3][draw(len(now[3]))]
            if u in pred[v]:
                later = [j for j in range(n) if queue[j] == queue[v] and key[v] < key[j] < key[v] + 1500.0]
                if later:
                    sooner(key, later[draw(len(later))], key[v] - 0.5)
            elif draw(2):
                sooner(key, v, key[u] - 1.0 - draw(2) * draw(1500))
            else:
                key[u] = key[v] + 1.0 + draw(2) * draw(1500)
        new = tried(key)
        if new[0] <= now[0] + 100.0 * (1.0 - k / PASSES):
            now = new
            if new[0] < best[0]:
                best = new
    PLAN["length"] = best[0]
    return best[1]


def rank_program(g, core, T, topo):
    rank = T.rank_of(core)
    if rank is None:
        return
    eng = {"V": g.vector, "S": g.scalar, "P": g.tensor, "G": g, "Y": g.sync}
    count = {"V": 0, "S": 0, "P": 0, "G": 0}
    known = {e: {} for e in eng}
    snap = {}
    ops = []
    links = []
    mark, glued = {}, set()
    hist = {}
    bank = {}

    def wait(e, ev):
        if known[e].get(ev[0], 0) >= ev[1]:
            return
        eng[e].wait_ge(T.sem[ev[0]], ev[1])
        for k, v in list(snap[ev].items()) + [ev]:
            if known[e].get(k, 0) < v:
                known[e][k] = v

    def run(e, fn, reads, writes, sem=None, inc=1, cost=100.0, pre=None):
        ops.append((e, fn, reads, writes, sem, inc, cost, pre))

    def name(n):
        mark[n] = len(ops) - 1

    def behind(*names):
        links.extend((mark[n], len(ops) - 1, 0) for n in names)

    def follows(n):
        behind(n)
        name(n)

    def block(k):
        glued.update(range(len(ops) - k + 1, len(ops)))

    def emit(e, fn, reads, writes, sem, inc, cost, pre):
        evs = []
        for wr, regs in ((False, reads), (True, writes)):
            for rg in regs:
                b, lo, hi = rg[0], rg[1], rg[2]
                if b in PSUM:
                    evs += [v for k, v in bank.get(b, {}).items() if k != e]
                else:
                    evs += [a[3] for a in hist.get(b, []) if (wr or a[0]) and meet((a[1], a[2], a[4]), rg[1:])]
        need = {}
        for k, v in evs:
            need[k] = max(need.get(k, 0), v)
        for ev in sorted(need.items(), key=lambda q: -q[1]):
            wait(e, ev)
        if pre:
            pre()
        if not inc:
            fn()
            return
        if sem is None:
            sem = "c" + e
            count[e] += 1
            ev = (sem, count[e])
        else:
            sem, whole = sem if isinstance(sem, tuple) else (sem, inc)
            ev = (sem, whole)
        fn().then_inc(T.sem[sem], inc)
        snap[ev] = dict(known[e])
        for wr, regs in ((False, reads), (True, writes)):
            for rg in regs:
                b, lo, hi = rg[0], rg[1], rg[2]
                if b in PSUM:
                    bank.setdefault(b, {})[e] = ev
                    if wr and e != "P":
                        bank[b]["wrote"] = ev
                else:
                    h = hist.setdefault(b, [])
                    if wr and rg[3] == 1:
                        h[:] = [a for a in h if not (lo <= a[1] and a[2] <= hi)]
                    elif not wr:
                        h[:] = [a for a in h if not (not a[0] and a[3][0] == ev[0] and (a[1], a[2], a[4]) == rg[1:])]
                    h.append((wr, lo, hi, ev, rg[3]))

    def c(b, lo=None, hi=None, step=1):
        n, at, w = PART.get(b) or (b, 0, SCRATCH[b][1][1])
        if lo is None:
            lo, hi = 0, w
        return (n, at + lo, at + hi, step)

    def k_(b, k):
        return c(b, 128 * k, 128 * k + 128)

    def ap(x):
        if x[0] == "ind":
            return ap(x[1]).indirect(ap(x[2]))
        return T[x[0]][:, x[1]:x[2]:x[3]] if x[3] != 1 else T[x[0]][:, x[1]:x[2]]

    def ind(w, o):
        return ("ind", w, o)

    def rd(*xs):
        out = []
        for x in xs:
            if isinstance(x, tuple):
                out += [x[1], x[2]] if x[0] == "ind" else [x]
        return out

    def val(x):
        return ap(x) if isinstance(x, tuple) else x

    def wide(x):
        return 16 * (x[2][2] - x[2][1]) if x[0] == "ind" else -(-(x[2] - x[1]) // x[3])

    def took(out, *ins, cols=()):
        if any(x[0] == "ind" for x in ins):
            return 50 + 1.3 * wide(out)
        small = all(SCRATCH[x[0]][2] in (BF, H, U16) for x in [out, *ins, *cols])
        both = len(ins) == 2 and not any(x[0] in PSUM for x in ins)
        return CYCLE * max(64, wide(out) * (2 if both else 0.5 if small and len(ins) == 1 else 1))

    def ts(out, a, s1, s2, o0, o1=None):
        if o1 is None:
            run("V", lambda: g.vector.tensor_scalar(ap(out), ap(a), val(s1), None, o0), rd(a, s1), [out],
                cost=took(out, a, cols=rd(s1)))
        else:
            run("V", lambda: g.vector.tensor_scalar(ap(out), ap(a), val(s1), val(s2), o0, o1), rd(a, s1, s2), [out],
                cost=took(out, a, cols=rd(s1, s2)))

    def tt(out, a, b, op):
        run("V", lambda: g.vector.tensor_tensor(ap(out), ap(a), ap(b), op), rd(a, b), [out], cost=took(out, a, b))

    def cp(out, a):
        run("V", lambda: g.vector.tensor_copy(ap(out), ap(a)), rd(a), [out], cost=took(out, a))

    def scan(out, d0, d1, o0, o1):
        run("V", lambda: g.vector.tensor_tensor_scan(ap(out), ap(d0), ap(d1), 0.0, o0, o1), rd(d0, d1), [out], cost=CYCLE * max(64, wide(out)))

    def fill(out, v):
        run("V", lambda: g.vector.memset(ap(out), v), [], [out], cost=took(out))

    def turn(out, a):
        run("V", lambda: g.vector.transpose(ap(out), ap(a)), [a], [out], cost=took(out, a))

    def act(out, a, func=AF.Copy, bias=0.0, scale=1.0):
        cost = 65 + 1.3 * wide(out) if a[0] == "ind" else CYCLE * max(64, wide(out))
        run("S", lambda: g.scalar.activation(ap(out), ap(a), func, bias=val(bias), scale=val(scale)), rd(a, bias, scale), [out],
            cost=cost + (1300 if func == AF.Exp else 1500 if func == AF.Ln and wide(out) == 1 else 0))

    def times(out, a, f):
        act(out, a, AF.Copy, 0.0, f)

    def even(out, v):
        act(out, c("cI"), AF.Identity, v, 0.0)

    def mm(out, l, r, start, stop):
        run("P", lambda: g.tensor.matmul(ap(out), ap(l), ap(r), start, stop), rd(l, r), [out],
            cost=CYCLE * max(min(64, wide(l)), wide(r)) * (4 if SCRATCH[l[0]][2] == F32 else 1))

    def iota(out, pattern, base, cm):
        cost = 130 + 2 * CYCLE * wide(out)
        if SCRATCH[out[0]][2] != I32:
            run("G", lambda: g.iota(ap(out), pattern, base, cm, allow_small_or_imprecise_dtypes=True), [], [out], cost=cost)
        else:
            run("G", lambda: g.iota(ap(out), pattern, base, cm), [], [out], cost=cost)

    def select(out, a, pattern, op, other, base, cm):
        run("G", lambda: g.affine_select(ap(out), ap(a), pattern, op, other, base, cm), [a], [out], cost=170 + 2 * CYCLE * wide(out))

    def diag(out, a, d, op=OP.is_equal, other=0.0):
        select(out, a, [[1, 128]], op, other, -d, -1)

    def load(e, sem, b, hi, src):
        run(e, lambda: eng[e].dma_start(T[b][:, 0:hi], src), [], [c(b, 0, hi)], sem=sem, inc=16,
            cost=1200.0 if b in ("oci", "wn") else 7000.0)

    PC, KC, GC, BC, TH, THR, P64, W64, WX, W0, W1, L3, LN, KX, K2, EVN, ODD, BK, BT, P0, P1 = [c("col", i, i + 1) for i in range(21)]
    add, sub, mul, mx, mi, eq, ge, gt, lt = (OP.add, OP.subtract, OP.mult, OP.max, OP.min, OP.is_equal, OP.is_ge, OP.is_gt, OP.is_lt)
    AND, SHR = OP.bitwise_and, OP.arith_shift_right
    BIG, RHO = float(1 << 22), (7 - rank) / 16.0

    load("Y", "d_oc", "oci", 128, T.oc[:, :])
    load("Y", "d_wn", "wn", 256, T.want[:, :])
    load("Y", "d_x", "xs", 8192, T.x[:, :])
    load("Y", "d_qs", "qsi", 256, T.qs[:, :])
    load("Y", "d_th", "thi", 1, T.th[:, :])

    iota(c("pint"), [[0, 1]], 0, 1)
    iota(c("cI"), [[1, 128]], 0, 0)
    iota(PC, [[0, 1]], 0, 1)
    iota(c("cg"), [[1, 8], [0, 16]], 0, 0)
    iota(c("ck"), [[0, 8], [1, 16]], 0, 0)
    iota(c("ch"), [[0, 8], [64, 4]], 0, 0)
    iota(c("n0"), [[256, 8], [1, 16]], 0, 0)
    iota(c("p8"), [[8192, 256]], 0, 0)
    iota(c("cC"), [[0, 8], [-3840, 16]], 28928, 0)
    iota(k_("ty", 0), [[16, 8], [128, 16]], 0, 0)
    iota(k_("ty", 1), [[16, 128]], 0, 0)
    iota(k_("cT", 0), [[0, 128]], 0, 0)
    iota(k_("cT", 1), [[-128, 2], [0, 64]], 64, 0)
    iota(k_("cT", 3), [[64, 2], [0, 4], [1, 16]], 0, 0)
    iota(k_("cT", 4), [[-64, 2], [0, 4], [1, 16]], 64, 0)
    iota(c("lkb", 512, 2048), [[0, 1536]], 0, 0)

    fill(c("lkb", 0, 512), 0.0)
    fill(c("wn", 256, 272), 0.0)
    fill(LN, math.exp(-23.67))
    fill(c("dw", 2048, 2064), -1024.0)
    fill(c("fw", 2048, 2064), 128.0)
    iota(c("fw", 0, 2048), [[0, 2048]], 0, 0)
    fill(c("wm", 256, 272), 0.0)
    fill(c("frac"), -0.46875)
    fill(c("pre"), -2047.0)
    ts(c("kint"), c("pint"), 15, None, AND)
    ts(c("gint"), c("pint"), 4, None, SHR)
    ts(c("lint"), c("pint"), 63, None, AND)
    ts(c("hint"), c("pint"), 6, None, SHR)
    ts(c("oint"), c("pint"), 4, 1, SHR, AND)
    cp(KC, c("kint"))
    cp(GC, c("gint"))
    cp(P64, c("lint"))
    cp(W64, c("hint"))
    cp(ODD, c("oint"))
    ts(EVN, ODD, -1.0, 1.0, mul, add)
    ts(c("gmb"), c("cg"), GC, None, eq)
    ts(c("ihb"), c("cI"), PC, None, eq)
    ts(c("R", 0, 16), c("cI", 0, 16), KC, None, eq)
    ts(K2, KC, 2.0, None, mul)
    act(WX, P64, AF.Exp, 43.0, -1.0)
    act(W1, LN, AF.Ln)
    times(L3, W1, 10.0)
    times(k_("pm", 0), c("ihb"), EVN)
    times(k_("pm", 3), c("ihb"), ODD)
    even(c("t1"), EVN)
    even(c("t2"), ODD)
    diag(k_("pm", 1), c("t1"), 16)
    diag(k_("pm", 2), c("t2"), -16)
    times(c("i37b"), c("ihb"), 37.0)
    times(c("in8"), c("ihb"), -8192.0)
    ts(c("n8"), c("n0"), 0.125, K2, mul, add)
    ts(c("stmp"), c("cg"), 16.0, KC, mul, add)
    ts(c("stmp2"), c("ck"), 0.0, None, eq)
    tt(c("stmp"), c("stmp"), c("stmp2"), mul)
    ts(c("cB", 0, 128), c("stmp"), 8.5, None, add)
    fill(c("cB", 128, 129), 0.0)
    for k in range(16):
        act(c("lkb", 128 * k + k, 128 * k + 128, 16), c("gmb", k, 128, 16))

    def relay(src, tb, b, s=(16, 1)):
        turn(c(tb), c(src))
        name("tb")
        for u in range(4):
            for c2 in (0, 1):
                for g2 in (0, 1):
                    a = s[0] * (2 * u + c2)
                    mm(c(b, a, a + 15 * s[1] + 1, s[1]), k_("pm", 2 * c2 + g2), c(tb, 32 * u + 16 * g2, 32 * u + 16 * g2 + 16),
                       (u, c2, g2) == (0, 0, 0), (u, c2, g2) == (3, 1, 1))
        block(16)

    swap = c("r2", 448, 512)
    A0, R1, R0 = c("pa", 0, 128), c("pa", 129, 257), c("pa", 257, 385)

    def persons(src):
        act(c("o"), src)
        act(c("emp"), src, AF.Relu, -255.0)
        name("emp")

    def offsets():
        tt(c("y1"), A0, c("n8"), mul)
        tt(k_("hz", 0), c("y1"), R1, add)
        for p in (0, 64):
            tt(c("hz", 128 + p, 192 + p), c("y1", 64 - p, 128 - p), c("pa", 129 + p, 193 + p), add)
        for b in (0, 1):
            ts(k_("hm13", b), k_("hz", b), 8191, None, AND)
            cp(k_("hu", b), k_("hm13", b))

    cp(c("ob"), c("oci"))
    relay("ob", "tb", "r0")
    ts(c("ol"), k_("r0", 0), 256.0, None, mi)
    persons(k_("r0", 0))
    mm(c("pa", 0, 129), c("ihb"), c("cB"), True, False)
    mm(R1, c("i37b"), c("o"), False, False)
    mm(R1, c("ihb"), c("frac"), False, False)
    for u in range(8):
        mm(c("pa", 16 * u + 1, 16 * u + 16), c("ihb"), c("o", 16 * u, 16 * u + 15), False, u == 7)
    block(8)

    def setup():
        ts(c("qa"), c("qsi"), 4, 15, SHR, AND)
        ts(c("hm13"), c("qsi"), 8, 7, SHR, AND)
        cp(c("q16"), c("qsi"))
        ts(c("hfs"), c("qa"), 112.0, None, mul)
        ts(c("hfd"), c("hm13"), -240.0, None, mul)
        for i, b in enumerate(("q16", "hfs", "hfd")):
            mm(c("pq", 0, 256), c("ihb"), c(b), i == 0, i == 2)
        cp(c("qi"), c("pq", 0, 256))
        cp(c("ql"), c("pq", 0, 256))
        ts(BC, KC, -256.0, 2048.0, mul, add)
        ts(KX, KC, 16.0, None, mul)
        ts(TH, c("thi"), 2048.0, None, sub)
        cp(c("gc"), c("gmb", 0, 128, 16))
        ts(c("lint"), c("pint"), 1, None, AND)
        cp(P1, c("lint"))
        ts(P0, P1, -1.0, 1.0, mul, add)
        ts(c("lint"), c("pint"), 1, 7, SHR, AND)
        cp(K2, c("lint"))
        ts(c("R2"), c("cI", 0, 8), K2, None, eq)
        act(c("Rb"), c("R"))
        act(c("uf", 16, 17), WX)
        for i, par in enumerate((P0, P1)):
            even(c("t1"), par)
            diag(k_("pu", 2 * i), c("t1"), 1 - 2 * i)
            times(c("t1"), k_("pu", 2 * i), -1.0)
            diag(c("t2"), c("t1"), 0, OP.not_equal, 1.0)
            times(k_("pu", 2 * i + 1), c("t2"), par)
        even(c("on"), 1.0)
        even(c("rho"), RHO / 128.0)
        even(c("r16"), 16.0)
        act(c("rs"), c("ck"), AF.Sign)
        act(c("cht"), c("ch"), AF.Relu, 1e5, -1e5)
        act(c("rb4"), c("cht"), AF.Identity, -64.0)
        ts(c("clist"), c("cI", 0, 16), 0.0, None, add)
        even(c("hd"), c("R", 0, 1))
        for t in range(3):
            select(k_("hm", t), c("hd"), [[0, 16], [1, 8]], eq, 0.0, -t, 0)
        times(c("wi"), c("gc"), KX)
        mm(c("pq", 256, 264), k_("wn", 0), c("wi"), True, True)
        mm(c("pq", 264, 272), k_("wn", 1), c("wi"), True, True)
        act(c("wsc"), c("pq", 256, 272), AF.Identity, -1.0 - RHO)
        act(c("ivb"), c("cI"))
        act(BK, KC, AF.Identity, -2048.0, 256.0)
        even(c("k2"), BK)
        even(k_("c77", 0), 77.0)
        even(k_("c77", 1), 154.0)
        for m, f in (("i8", 8192.0), ("i4k", 4096.0), ("n4k", -4096.0), ("i256", 256.0), ("i16", 16.0), ("nih", -1.0)):
            times(c(m), c("ihb"), f)
        times(c("gneg"), c("gmb"), -BIG)
        for i, f in enumerate((1.0, 37.0, 1.0, 0.0, 37.0, 1.0)):
            times(c("g3", 8 * i, 8 * i + 8), c("gc"), f)
        act(BT, KC, AF.Identity, BIG / 2, BIG)
        diag(c("tri"), c("gmb"), 0, gt)
        ts(k_("dm", 0), c("ck"), KC, None, eq)
        act(k_("dm", 1), k_("dm", 0))
        ts(W0, W64, -1.0, 1.0, mul, add)
        ts(c("two"), c("cI", 0, 16, 8), K2, None, add)
        ts(c("cD"), c("ck"), float(DV), -4096.0, ge, mul)
        for out, terms in (("m1", (("tri", -256.0), ("ihb", 4096.0))), ("m2", (("gmb", -256.0), ("ihb", -4096.0), ("tri", 4096.0))),
                           ("wt", (("tri", -1.0), ("ihb", 4096.0))), ("trf", (("tri", -BIG), ("ihb", BIG / 2)))):
            for i, (m, f) in enumerate(terms):
                times(c("sc"), c("ihb"), f)
                mm(k_("r3", 0), c("sc"), c(m), i == 0, i == len(terms) - 1)
            act(k_(out, 0), k_("r3", 0))
        act(c("wt", 128, 192), c("wt", 64, 128))
        act(c("wt", 192, 256), c("wt", 0, 64))
        times(k_("wt", 2), c("gmb"), -1.0)
        act(k_("cT", 2), k_("dm", 0), AF.Identity, -16.0, 32.0)
        act(k_("cT", 5), k_("dm", 0), AF.Identity, -16.0, 32.0)
        iota(c("t2"), [[0, 8], [-3840, 16]], 28928 + 3840, 0)
        select(c("cA"), c("t2"), [[0, 8], [1, 16]], gt, 0.0, 0, 0)
        ts(c("thb"), c("cI"), 0.0, TH, mul, add)
        mm(k_("r3", 0), c("thb"), c("ihb"), True, True)
        cp(k_("thx", 0), k_("r3", 0))
        cp(k_("thx", 1), k_("r3", 0))

    def pick(e, z, a, b, win, off):
        if e == "V":
            ts(c(z, a, b), ind(win, off), -1.0, -256.0, mul, mx)
        else:
            act(c(z, a, b), ind(win, off), AF.Relu, 256.0, -1.0)

    def masked(e, out, a, col):
        if e == "V":
            ts(out, a, ("Rb",) + col[1:], None, mul)
        else:
            times(out, a, col)

    def blocks(sem):
        moves = [g.sync.dma_start(T.fw[b::16, 128 * b:128 * b + 128], T.tof[b::16, :]) for b in range(16)]
        for x in moves[:15]:
            x.then_inc(T.sem[sem], 16)
        return moves[15]

    def by_slots(e, z, win, p0, p1):
        (cp if e == "V" else act)(c(z, 16 * p0, 16 * p1), ind(c(win), c("ql", p0, p1)))

    def slots_sum(h, b, fin):
        for j in range(16):
            mm(c(b, 128 + j, 256, 16), c("zf", 2048 * h + j, 2048 * h + 2048, 16), c("gc"), j == 0, j == 15)
            if j % 4 == 3:
                block(4)
                if h and not fin:
                    behind("uw", "turn")
        (cp if fin else act)(k_("qt", h), k_(b, 1))
        if fin:
            ts(k_("hfs", h), k_(b, 1), 64.0, 960.0, ge, mul)
        mm(k_(b, 0), c("i256" if fin else "ihb"), k_("qs16" if fin else "qo", h), True, False)
        if fin:
            mm(k_(b, 0), c("i16"), k_("hfd", h), False, False)
            mm(k_(b, 0), k_("hfs", h), c("ihb"), False, False)
        mm(k_(b, 0), k_("qt", h), c("ihb"), False, True)
        name("turn")

    def appended(fin):
        mm(k_("r1", 1), c("apx"), c("i8"), True, False)
        mm(k_("r1", 1), c("ihb"), k_("ty", fin), False, False)
        act(c("l1"), k_("r2", 2), AF.Relu)
        act(c("l2"), k_("r2", 2), AF.Relu, -15.0)
        mm(k_("r1", 1), c("gmb"), c("l1"), False, False)
        mm(k_("r1", 1), c("gneg"), c("l2"), False, True)
        act(c("tab"), k_("r1", 1))
        name("tab")
        tt(c("npl"), ind(c("tab"), c("ul")), c("cs"), sub)
        name("npl")
        if fin:
            act(c("cs"), c("npl"), AF.Abs)
            ts(c("np2"), c("cs"), 2048.0, None, mi)
        else:
            act(c("np2"), c("npl"), AF.Abs)

    def gather(i, other, a0, a1):
        z = 2048 * i + 1024 * other
        u = 128 * other + 64 * i
        tt(c("mn", z + 16 * a0, z + 16 * a1), ind(c("xs"), c("hu", u + a0, u + a1)),
           c("wg", 1024 * i + 16 * a0, 1024 * i + 16 * a1), mi)
        (follows if z + a0 else name)("rec")

    def records(i, other, b, at, stop=True, fetched=False):
        z = 2048 * i + 1024 * other
        if fetched:
            for q in (0, 1):
                tt(c("mn", z + 512 * q, z + 512 * q + 512), c("r%d" % q), c("zf", z + 512 * q, z + 512 * q + 512), mi)
                follows("rec")
        else:
            gather(i, other, 0 if i else FIRST, 64)
        for k in range(16):
            mm(c(b, at, at + 64), k_("lkb", k), c("mn", z + k, z + 1024, 16), False, stop and k == 15)
        block(16)

    far = [d for d in T.cores if topo.chip(d) != topo.chip(core)]
    near = [d for d in T.cores if d != core and topo.chip(d) == topo.chip(core)]
    far_e = topo.engines(core, far[0])
    near_e = [e for e in topo.engines(core, near[0]) if e not in far_e]

    def send(keys, sem):
        moves = [RemoteDMATransfer(dst_ids=[DstId(rid=topo.addr(d)[0], pnc=topo.addr(d)[1]) for d in to],
                                   dma_engine_mask=sum(1 << e for e in engines), remote_sem=T.sem[sem],
                                   srcs=[ap(keys)], dsts=[ap(keys) for d in to]) for to, engines in ((far, far_e), (near, near_e))]
        run("G", lambda: g.remote_dma_fused(moves, local_sem=T.sem.loc), [keys], [], inc=0, cost=300.0)
        return len(ops) - 1

    def arrived(sent, sem):
        ops[-1] = ops[-1][:7] + (lambda: g.vector.wait_ge(T.sem[sem], len(far_e) * len(far) + len(near_e) * len(near)),)
        links.append((sent, len(ops) - 1, 2))

    for t in range(3):
        last = t == 2
        land = "land%d" % t
        for a, b in ((0, FIRST), (FIRST, 64), (64, 128)):
            act(c("wg", 16 * a, 16 * b), ind(c("wn"), c("ol", a, b)))
            if a == 64:
                behind("emp")
            (follows if a else name)("e")
        if t == 0:
            offsets()
            setup()
        mm(k_("plo", 0), c("ihb"), c("pre"), True, False)
        mm(c("plo", 64, 128), c("in8"), c("emp", 0, 64), False, False)
        mm(c("phi", 0, 64), c("ihb"), c("pre", 0, 64), True, False)
        mm(c("r3", 0, 64), c("in8"), c("emp", 64, 128), True, False)
        mm(c("r3", 0, 64), c("ihb"), c("pre", 0, 64), False, False)
        gather(0, 0, 0, FIRST)
        gather(0, 1, 0, FIRST)
        records(0, 0, "plo", 0, False)
        records(0, 1, "plo", 64)
        if not t:
            for q in (0, 1):
                mm(c("r%d" % q), c("ihb"), c("wg", 1024 + 512 * q, 1536 + 512 * q), True, True)
            for q, a in enumerate((64, 96, 192, 224)):
                act(c("zf", 2048 + 512 * q, 2560 + 512 * q), ind(c("xs"), c("hu", a, a + 32)))
        records(1, 0, "phi", 0, True, not t)
        records(1, 1, "r3", 0, True, not t)
        if t:
            for p in (0, 64, 128, 192):
                by_slots("S", "zf", "fw", p, min(p + 64, EV))
                behind("tab")
                follows("e")
            by_slots("V", "zf", "fw", EV, 256)
            behind("npl")
            follows("rec")
            slots_sum(0, "pq", False)
        cp(c("ml"), c("plo", 0, 64))
        cp(c("mh"), c("phi", 0, 64))
        tt(c("dlo"), c("plo", 64, 128), c("ml"), sub)
        tt(c("dd"), c("phi", 0, 64), c("dlo"), sub)
        tt(swap, c("r3", 0, 64), c("dd"), gt)
        behind("rec")
        tt(c("dhi"), c("r3", 0, 64), c("mh"), sub)
        tt(c("dlo"), swap, c("dlo"), mul)
        tt(c("dhi"), swap, c("dhi"), mul)
        for b in ("hi", "cp"):
            tt(c(b, 0, 64), c("plo", 0, 64), c("dlo"), add)
            tt(c(b, 64, 128), c("phi", 0, 64), c("dhi"), add)
        for i in (0, 1):
            mm(k_("r%d" % i, 0), k_("pu", 2 * i + 1), c("hi"), True, False)
            mm(k_("r%d" % i, 0), k_("pu", 2 * i), c("cp"), False, True)
            name("uw")
        cp(k_("uw", 0), k_("r0", 0))
        act(k_("uw", 1), k_("r1", 0))
        for b in range(16):
            masked("S" if b & 1 and b < 2 * US else "V", k_("dw", b), k_("uw", b & 1), c("R2", b // 2, b // 2 + 1))
        if t:
            slots_sum(1, "pa", False)
        for b, sb in enumerate(("plo", "phi")):
            mm(k_(sb, 0), c("on"), c("rho"), True, False)
            mm(k_(sb, 0), c("on"), c("r16"), False, False)
            if t and not b:
                tt(k_("qi", 0), k_("pq", 0), k_("np2", 0), mi)
                ts(k_("ql", 0), k_("qi", 0), 2048.0, None, mi)
                by_slots("V", "zd", "dw", 0, CV[0] // 2)
                name("c")
                tt(k_("qi", 1), k_("pa", 0), k_("np2", 1), mi)
                follows("c")
                by_slots("V", "zd", "dw", CV[0] // 2, CV[0])
                follows("c")
                ts(k_("ql", 1), k_("qi", 1), 2048.0, None, mi)
                follows("c")
            else:
                by_slots("V", "zd", "dw", 128 * b, 128 * b + CV[b])
            by_slots("S", "zd", "dw", 128 * b + CV[b], 128 * b + 128)
            for j in range(16):
                mm(c(sb, j, 128, 16), c("zd", 2048 * b + j, 2048 * b + 2048, 16), c("gc"), False, j == 15)
            block(16)
            scan(k_("tm", b), c("rs"), k_(sb, 0), mul, mx)
            if not b:
                ts(k_("q16", 0), k_(sb, 0), 2048.0 + RHO, None, sub)
        own, best = c(land, 16 * rank, 16 * rank + 16), c("tm", 15, 256, 16)
        ts(own, best, 0.25, None, mx)
        name("own")
        sent = send(own, "arr%d" % t)
        ts(k_("q16", 1), k_("phi", 0), 2048.0 + RHO, None, sub)
        behind("own")
        act(c("sb", 0, 64), swap)
        for i, b in enumerate(("o", "cp")):
            mm(k_("r1", i), c("ihb"), c(b), i == 0, False)
            for q in (0, 1):
                mm(c("r1", 256 + 128 * i + 64 * q, 320 + 128 * i + 64 * q), c("ihb"), c(b, 64 - 64 * q, 128 - 64 * q), False, False)
        for q in range(8):
            mm(c("r1", 64 * q, 64 * q + 64), c("i8" if q > 3 else "in8"), c("sb", 0, 64), False, q == 7)
        block(8)
        act(c("x2"), c("r1", 256, 512), AF.Identity, -8192.0)
        tt(c("o2c"), c("r1", 0, 256), c("x2"), mx)
        relay("o2", "th2", "r1", (1, 8))
        ts(c("qa"), c("qi"), 0x38F, None, AND)
        ts(c("hfs"), c("qa"), 128.0 * t, None, eq)
        ts(c("k16"), best, 2048.0 + RHO, None, sub)
        mm(c("r3", 0, 256), c("ihb"), c("thx"), True, False)
        for b in (0, 1):
            mm(k_("r3", b), k_("hfs", b), c("in8"), False, False)
        for j in range(16):
            mm(c("r3", j, 256, 16), c("nih"), c("k16"), False, False)
        block(16)
        mm(c("r3", 0, 256), c("ihb"), c("q16"), False, True)
        act(c("sg"), c("r3", 0, 256), AF.Sign, 2048.5)
        for b in (0, 1):
            mm(k_("r3", 2 + b), k_("sg", b), c("ihb"), True, True)
        act(c("sgt"), c("r3", 256, 512))
        for b in (0, 1):
            mm(c("plo", 256 + 8 * b, 264 + 8 * b), k_("sgt", b), c("gc"), True, True)
        ts(c("free"), c("plo", 256, 272), 15.0, None, lt)
        tt(c("ak"), c("free"), best, mul)
        mm(c("plo", 0, 256), c("ihb"), c("p8"), True, False)
        mm(c("plo", 0, 256), c("trf"), c("sgt"), False, True)
        act(c("cs"), c("plo", 0, 256), AF.Identity, BT)
        tt(c("zi"), own, c("wsc"), add)
        ts(c("ui"), c("zi"), 127, None, AND)
        cp(c("uf", 0, 16), c("ui"))
        for i in range(16):
            ts(k_("oh", i), c("ivb"), c("uf", i, i + 1), c("uf", 16, 17), eq, mul)
        tt(c("ub"), ind(c("ui"), c("clist")), c("dm"), mul)
        for b in (0, 1):
            mm(c("pq", 64 + 8 * b, 72 + 8 * b), k_("ub", b), c("gc"), True, True)
        if last:
            ts(c("qa"), c("qi"), 4, 3, SHR, AND)
            cp(c("qs16"), c("qa"))
            ts(c("qa"), c("qi"), 7, 15, SHR, AND)
            cp(c("hfd"), c("qa"))
        mm(k_("phi", 0), c("c2"), c("ihb"), True, False)
        mm(k_("phi", 0), c("emp"), c("in8"), False, False)
        mm(k_("phi", 0), c("in8"), k_("hm", t), False, False)
        mm(k_("phi", 0), c("ihb"), k_("thx", 0), False, False)
        mm(k_("phi", 0), c("ihb"), c("cD"), False, False)
        mm(k_("r0", 0), c("ihb"), c("k2"), True, False)
        mm(k_("r0", 0), c("o2"), c("ihb"), False, False)
        mm(c("r2", 0, 384), c("ihb"), c("cT", 384 * last, 384 * last + 384), True, False)
        for q, m in enumerate(("i4k", "i4k", "n4k", "n4k")):
            mm(c("r2", 64 * q, 64 * q + 64), c(m), c("sb", 0, 64), False, False)
        block(4)
        if not last:
            mm(c("pa", 0, 129), c("ihb"), c("cB"), True, False)
            mm(A0, c("ihb"), c("cA"), False, False)
            mm(R1, c("i37b"), c("cC"), False, False)
            mm(R1, c("ihb"), k_("c77", t), False, False)
        mm(R0, c("ihb"), c("cC"), last, False)
        tt(c("kt", 0, 64), c(land, 0, 64), c(land, 64, 128), mx)
        arrived(sent, "arr%d" % t)
        name("max")
        ts(c("ol2"), k_("r1", 0), 256.0, None, mi)
        follows("max")
        tt(c("kt", 64, 96), c("kt", 0, 32), c("kt", 32, 64), mx)
        follows("max")
        ts(c("akx", 0, 32, 2), c("ak"), W0, None, mul)
        follows("max")
        ts(c("akx", 1, 32, 2), c("ak"), W64, None, mul)
        follows("max")
        tt(c("kp"), c("kt", 64, 80), c("kt", 80, 96), mx)
        follows("max")
        cp(c("ul"), c("pq", 64, 80))
        follows("max")
        if not last:
            cp(c("qo"), c("ql"))
        tt(c("wf"), ind(c("kp"), c("two")), c("akx"), eq)
        name("wf")
        for b in (0, 1):
            ts(k_("kb", b), ind(c("kp"), c("clist", 8 * b, 8 * b + 8)), -2048.21875, None, add)
            behind("max")
            mm(k_(("r3", "r1")[b], 0), k_("kb", b), c("ihb"), True, True)
        act(k_("wm", 0), k_("r3", 0), AF.Relu, BC)
        ts(k_("wm", 1), k_("r1", 0), BC, 0.0, add, mx)
        for i in range(16):
            b, h = i // 8, i % 8
            mm(c("pq", 4 * h + 2 * b, 4 * h + 2 * b + 2), k_("oh", i), c("wf", 2 * i, 2 * i + 2), True, True)
            if h == 7:
                block(8)
        act(c("lna", 0, 32), c("pq", 0, 32), AF.Ln, 2.0 ** -63, math.exp(-0.23))
        act(c("lna", 32, 64), c("lna", 0, 32), AF.Relu, L3, -10.0)
        name("ln")
        for e, a, b in DC:
            pick(e, "ze", 128 * a, 128 * b, c("wm"), c("ol2", 8 * a, 8 * b))
            behind(*(["wf"] if e == "V" else ["ln"] if b == 16 else []))
            for k in range(a, b):
                mm(c("phi", k, 128, 16), k_("ze", k), c("gc"), False, k == 15)
            block(b - a)
        tt(c("lna", 96, 128), c("lna", 32, 64), c("lna", 0, 32), sub)
        scan(c("lna", 128, 160), c("rb4"), c("lna", 96, 128), add, mi)
        ts(c("apf"), c("lna", 131, 160, 4), 12582912.0 + 235.0, 12582912.0, add, sub)
        tt(c("apm"), ind(c("apf"), c("clist", 0, 8)), k_("dm", 0), mul)
        act(c("apx"), ind(c("apf"), c("clist", 0, 8)))
        mm(k_("r1", 0), c("gmb"), c("apm"), True, False)
        ts(c("st"), k_("phi", 0), -4096.5, None, lt)
        mm(k_("r1", 0), c("m2"), c("st"), False, True)
        mm(k_("r0", 0), c("m1"), c("st"), False, True)
        mm(c("r2", 0, 384), c("st"), c("wt"), False, True)
        act(c("e2"), k_("r1", 0), AF.Identity, 6144.0)
        tt(c("e16"), k_("r0", 0), c("e2"), mi)
        act(c("ym"), k_("r2", 1), AF.Identity, 4096.0)
        tt(c("tof"), k_("r2", 0), c("ym"), mi)
        if last:
            for b in range(16):
                masked("V" if b < TV else "S", k_("fw", b), c("tof"), c("R", b, b + 1))
            appended(True)
        else:
            run("Y", lambda t=t: blocks("d_fw%d" % t), [c("tof")], [c("fw", 0, 2048)], sem=("d_fw%d" % t, 256), inc=16, cost=3200.0)
        for i, r in enumerate((15, 0, 14, 1, 13, 2, 12, 3, 11, 4, 10, 5, 9, 6, 8, 7)):
            ts(k_("fr", r), c("e16"), 256.0 * r - 2048.0, 256.0 * r - 1792.0, mx, mi)
            if last:
                mm(c("pa", 257 + r, 385, 16), k_("fr", r), c("gc"), False, i == 15)
                continue
            if i == 10:
                mm(R1, c("ihb"), c("frac"), False, False)
            mm(c("pa", 1 + r, 385, 16), k_("fr", r), c("g3", 24 * (r == 15), 24 * (r == 15) + 24), False, i == 15)
        if not last:
            ts(c("ol"), R0, 256.0, None, mi)
            offsets()
            persons(R0)
            appended(False)
    ts(c("ob"), R0, 256.0, None, mi)
    relay("ob", "tb", "r0")
    act(c("yo"), k_("r0", 0))
    run("Y", lambda: g.sync.dma_start(T.yoc[:, :], T.yo[:, :]), [c("yo")], [], sem="d_yo", inc=16, cost=2000.0)
    for h, b in enumerate(("pq", "phi")):
        by_slots("V", "zf", "fw", 128 * h, 128 * h + FV[h])
        behind("npl" if h else "tb")
        by_slots("S", "zf", "fw", 128 * h + FV[h], 128 * h + 128)
        behind("tab")
        slots_sum(h, b, True)
        tt(k_("yqs", h), k_(b, 0), k_("np2", h), mi)
        run("Y", lambda h=h: g.sync.dma_start(T.yq[:, 128 * h:128 * h + 128], ap(k_("yqs", h))), [k_("yqs", h)], [],
            sem="d_yq%d" % h, inc=16, cost=2000.0)

    if "order" not in PLAN:
        first = [i for i in range(len(ops)) if i not in glued] + [len(ops)]
        piece = [k for k in range(len(first) - 1) for _ in range(first[k], first[k + 1])]
        whole = [(ops[a][0], None, sum((op[2] for op in ops[a:b]), []), sum((op[3] for op in ops[a:b]), []), None, 1,
                  sum(op[6] for op in ops[a:b])) for a, b in zip(first, first[1:])]
        order = plan(whole, [(piece[a], piece[b], k) for a, b, k in links])
        PLAN["order"] = [i for k in order for i in range(first[k], first[k + 1])]
    for i in PLAN["order"]:
        emit(*ops[i])
    g.sync.wait_ge(T.sem.d_yo, 16)
    g.sync.wait_ge(T.sem.d_yq0, 16)
    g.sync.wait_ge(T.sem.d_yq1, 16)
    for e in ("V", "S", "P", "G"):
        g.wait_ge(T.sem["c" + e], count[e])
    g.wait_ge(T.sem.loc, 3 * (len(far_e) + len(near_e)))
